import numpy as np
import ml_dtypes


def mxq(x, axis, fmt="e4m3"):
    dtype, down = {"e4m3": (ml_dtypes.float8_e4m3fn, 7), "e5m2": (ml_dtypes.float8_e5m2, 14)}[fmt]
    v = np.moveaxis(np.asarray(x, np.float32).astype(ml_dtypes.bfloat16).astype(np.float64), axis, -1)
    blocks = v.reshape(v.shape[:-1] + (-1, 32))
    amax = np.abs(blocks).max(-1, keepdims=True)
    byte = np.maximum(np.where(amax > 0, np.frexp(amax)[1] - 1 + 127, 0) - down, 1)
    scale = np.exp2(byte - 127.0)
    codes = (blocks / scale).astype(np.float32).astype(dtype).astype(np.float64)
    return np.moveaxis((codes * scale).reshape(v.shape), -1, axis)


WIDE = False


def mx_kscale(k):
    if not WIDE:
        return np.ones(k)
    levels = np.array([10, -10, 5, -5, 0])
    if k % 512:
        return np.exp2(np.random.permutation(np.resize(levels, k // 32))).repeat(32)
    a = np.empty((k // 512, 16))
    for p in range(k // 512):
        a[p, :8] = np.random.permutation(np.resize(levels, 8))
        for g in range(8):
            far = levels[np.abs(levels - a[p, g]) >= 10]
            a[p, g + 8] = far[np.random.randint(len(far))]
    return np.exp2(a.ravel()).repeat(32)


def f64(x):
    return np.asarray(x).astype(np.float64)


def striped(idx):
    return np.tile(idx.reshape(-1, 16).T, (8, 1)).astype(np.uint16)


def unstriped(offs):
    return offs[:16].T.reshape(-1).astype(np.int64)


E2M1 = np.array([0.0, 0.5, 1.0, 1.5, 2.0, 3.0, 4.0, 6.0, -0.0, -0.5, -1.0, -1.5, -2.0, -3.0, -4.0, -6.0])


def pack_weight(w, fmt):
    k, n = w.shape
    w = f64(np.asarray(w, np.float32).astype(ml_dtypes.bfloat16)).reshape(k // 32, 32, n)
    amax = np.abs(w).max(1)
    if fmt == "e4m3":
        byte = np.frexp(amax)[1] - 1 + 127 - 7
    else:
        mant, ex = np.frexp(amax / 6.0)
        byte = np.where(mant > 0.5, ex, ex - 1) + 127
    byte = np.clip(np.where(amax > 0, byte, 1), 1, 254)
    scaled = (w * np.exp2(127.0 - byte)[:, None, :]).reshape(k, n).astype(np.float32)
    by_word = np.ascontiguousarray(scaled.reshape(k // 512, 128, 4, n).transpose(0, 1, 3, 2))
    if fmt == "e4m3":
        words = by_word.astype(ml_dtypes.float8_e4m3fn).view(np.uint8)
    else:
        c = by_word.astype(ml_dtypes.float4_e2m1fn).view(np.uint8) & 0xF
        words = (c[..., 0::2] | (c[..., 1::2] << 4)).reshape(k // 512, 128, 2 * n)
    return np.ascontiguousarray(words), np.ascontiguousarray(byte.astype(np.uint8).reshape(k // 512, 16, n))


def unpack_weight(words, scales, fmt):
    g, _, n = scales.shape
    words = np.ascontiguousarray(words).reshape(g, 128, n, -1)
    if fmt == "e4m3":
        vals = words.view(ml_dtypes.float8_e4m3fn).astype(np.float64)
    else:
        nib = np.empty((g, 128, n, 4), np.uint8)
        nib[..., 0::2] = words & 0xF
        nib[..., 1::2] = words >> 4
        vals = E2M1[nib]
    vals = vals * np.repeat(np.exp2(scales.astype(np.float64) - 127.0), 8, axis=1)[..., None]
    return vals.transpose(0, 1, 3, 2).reshape(g * 512, n)


def gelu(v):
    return 0.5 * v * (1.0 + np.tanh(np.sqrt(2.0 / np.pi) * (v + 0.044715 * v**3)))


def striped8(idx):
    return np.concatenate([v.reshape(-1, 16).T for v in idx]).astype(np.uint16)


def unstriped8(offs):
    return np.stack([offs[16 * g:16 * g + 16].T.reshape(-1) for g in range(8)]).astype(np.int64)


def runs(v, idx8):
    k = np.arange(v.shape[0])
    return v[k[:, None], idx8[k % 512 // 64]]


K, T, S, N = 1024, 2048, 1024, 512

def setup_inputs():
    n = np.random.standard_normal
    s = mx_kscale(K)[:, None]
    w = mx_kscale(S)
    tab_words, tab_scales = pack_weight(n((K, T)) * s, "e4m3")
    tab2_words, tab2_scales = pack_weight(n((K, T)) / np.sqrt(K) / s, "e4m3")
    w4_words, w4_scales = pack_weight(n((K, N)) / np.sqrt(K) / s, "e2m1")
    return {
        "tab_words": tab_words, "tab_scales": tab_scales,
        "tab2_words": tab2_words, "tab2_scales": tab2_scales,
        "offs": striped8(np.stack([np.random.permutation(T)[:S] for _ in range(8)])),
        "offs2": striped(np.random.permutation(T)[:S]),
        "w4_words": w4_words, "w4_scales": w4_scales,
        "wv": (n((K, N)) * s).astype(np.float32),
        "gm": (np.exp(0.3 * n(S)) * S ** -0.25 * w).astype(np.float32),
        "gv": (np.exp(0.3 * n(S)) * S ** -0.25 / w).astype(np.float32),
        "prior": (0.7 * n((S, S)) * S ** -0.25 * w[:, None]).astype(np.float32),
    }

def reference(tab_words, tab_scales, tab2_words, tab2_scales, offs, offs2,
              w4_words, w4_scales, wv, gm, gv, prior):
    v = runs(unpack_weight(tab_words, tab_scales, "e4m3"), unstriped8(offs))
    v2 = unpack_weight(tab2_words, tab2_scales, "e4m3")[:, unstriped(offs2)]
    w4 = unpack_weight(w4_words, w4_scales, "e2m1")
    e = f64(gm)[:, None] * (v2.T @ v) + f64(prior)
    val = f64(gv)[:, None] * (v2.T @ mxq(f64(wv), 0, "e4m3"))
    y = mxq(val, 0, "e4m3").T @ mxq(e, 0, "e4m3") + w4.T @ v
    return y / (1.0 + np.exp(-y))

@@ -1,0 +1,294 @@
+from contextlib import ExitStack
+
+import concourse.mybir as mybir
+
+K, T, S, N = 1024, 2048, 1024, 512
+FLOPS = 2 * K * S * S + 2 * K * S * N + 2 * S * N * S + 2 * K * N * S
+
+F32 = mybir.dt.float32
+BF16 = mybir.dt.bfloat16
+I32 = mybir.dt.int32
+U32 = mybir.dt.uint32
+U16 = mybir.dt.uint16
+U8 = mybir.dt.uint8
+FP8X4 = mybir.dt.float8_e4m3fn_x4
+FP4X4 = mybir.dt.float4_e2m1fn_x4
+ACT = mybir.ActivationFunctionType
+ALU = mybir.AluOpType
+
+P = 128
+PACK = 4
+PASS = P * PACK
+PASSES = 2
+HALF = 512
+LIST_ROWS = 16
+CHUNKS = ((0, 512), (512, 256), (768, 256))
+
+
+def weave(copy, woven, planes):
+    copy(
+        out=woven.rearrange("p (c i) t -> p c t i", i=PACK),
+        in_=planes[:].rearrange("p t (c i) -> p c t i", i=PACK),
+    )
+
+
+def quantize(nc, pool, woven, name, codes):
+    width = woven.shape[1]
+    scales = pool.tile([P, width], U8, name=f"{name}_scales", align_bytes=64)
+    nc.vector.quantize_mx(out=codes[:].bitcast(FP8X4), scales=scales[:], in_=woven[:].rearrange("p c t -> p (c t)"))
+    return codes, scales
+
+
+def tile_list_splice_map_reading_kernel(
+    tc, tab_words, tab_scales, tab2_words, tab2_scales, offs, offs2, w4_words, w4_scales, wv, gm, gv, prior, out
+):
+    nc = tc.nc
+    with ExitStack() as ctx:
+        keep = ctx.enter_context(tc.tile_pool(name="keep", bufs=1))
+        ring = ctx.enter_context(tc.tile_pool(name="ring", bufs=3))
+        reuse = ctx.enter_context(tc.tile_pool(name="reuse", bufs=1))
+        early = ctx.enter_context(tc.tile_pool(name="early", bufs=1))
+        psum = ctx.enter_context(tc.psum_pool(name="psum", bufs=1))
+
+        def bank(index, shape):
+            return psum.tile(shape, F32, name=f"bank{index}", tag=f"bank{index}")
+
+        def scalar_cast(out, in_):
+            nc.scalar.activation(out=out, in_=in_, func=ACT.Copy)
+
+        def load_words(words, a, name):
+            window = keep.tile([P, T], I32, name=name, tag=name, align_bytes=64)
+            nc.sync.dma_start(out=window[:], in_=words[a].rearrange("p t i -> p (t i)").bitcast(I32))
+            return window
+
+        v2_scale_window = keep.tile([P, T], U8, align_bytes=64)
+        v_scale_window = keep.tile([P, T], U8, align_bytes=64)
+        w4_scale_tile = keep.tile([P, PASSES, N], U8, align_bytes=64)
+        nc.gpsimd.memset(v_scale_window[:].bitcast(I32), 0)
+        nc.vector.memset(v2_scale_window[:].bitcast(I32), 0)
+        nc.gpsimd.memset(w4_scale_tile[:].bitcast(I32), 0)
+
+        lists = keep.tile([P, S // LIST_ROWS], U16)
+        nc.sync.dma_start(lists[:], offs)
+        list2 = keep.tile([P, S // LIST_ROWS], U16)
+        nc.sync.dma_start(list2[:], offs2)
+        nc.scalar.dma_start(
+            out=v_scale_window[0:P:4, :].bitcast(I32), in_=tab_scales.bitcast(I32).rearrange("a q t -> q a t")
+        )
+        for d in range(4):
+            nc.scalar.dma_start(
+                out=v2_scale_window[32 * d : 32 * d + 8, :].bitcast(I32),
+                in_=tab2_scales.bitcast(I32)[:, 4 * d : 4 * d + 4, :],
+            )
+        warm = keep.tile([P, 2], F32)
+        nc.gpsimd.memset(warm[:], 0.0)
+        nc.scalar.activation(out=warm[:, 1:2], in_=warm[:, 0:1], func=ACT.Silu)
+
+        wv_raw = []
+        for a in range(PASSES):
+            raw = early.tile([P, PACK, N], F32, name=f"wv_raw{a}", offset=a * N * PACK * 4, align_bytes=64)
+            nc.sync.dma_start(out=raw[:], in_=wv[a * PASS : (a + 1) * PASS, :].rearrange("(p t) n -> p t n", t=PACK))
+            wv_raw.append(raw)
+        v2_windows = [load_words(tab2_words, a, f"v2_window{a}") for a in range(PASSES)]
+        gm_cols = keep.tile([P, PASSES, PACK], F32)
+        gv_cols = keep.tile([P, PASSES, PACK], F32)
+        nc.sync.dma_start(out=gv_cols[:], in_=gv.rearrange("(b p t) -> p b t", p=P, t=PACK))
+        nc.sync.dma_start(out=gm_cols[:], in_=gm.rearrange("(b p t) -> p b t", p=P, t=PACK))
+
+        v_scales_listed = keep.tile([P, S], U8, align_bytes=64)
+        nc.vector.tensor_copy(out=v_scales_listed[:], in_=v_scale_window[:].indirect(lists[:]))
+        v2_scales_listed = keep.tile([P, S], U8, align_bytes=64)
+        nc.vector.tensor_copy(out=v2_scales_listed[:], in_=v2_scale_window[:].indirect(list2[:]))
+        v2_scales = keep.tile([P, S], U8, align_bytes=64)
+        nc.vector.tensor_copy(
+            out=v2_scales[:].rearrange("p (b t c) -> p b t c", b=PASSES, t=PACK),
+            in_=v2_scales_listed[:].rearrange("p (b c t) -> p b t c", b=PASSES, t=PACK),
+        )
+
+        wv_woven = early.tile([P, PASSES * N, PACK], BF16, offset=PASSES * N * PACK * 4, align_bytes=64)
+        for a in range(PASSES):
+            weave(scalar_cast, wv_woven[:, a * N : (a + 1) * N, :], wv_raw[a])
+        wv_codes, wv_scales = quantize(nc, keep, wv_woven, "wv", keep.tile([P, PASSES * N], U32, name="wv_codes", align_bytes=64))
+
+        v_scales = early.tile([P, PASSES, S], U8, offset=N * PACK * 4, align_bytes=64)
+        nc.gpsimd.memset(v_scales[:].bitcast(I32), 0)
+        for d in range(4):
+            nc.sync.dma_start(
+                out=v_scales[32 * d : 32 * d + 4, :, :].bitcast(I32),
+                in_=v_scales_listed[32 * d : 32 * d + 32 : 4, :].bitcast(I32),
+            )
+
+        v_windows = [load_words(tab_words, a, f"v_window{a}") for a in range(PASSES)]
+        prior_rows = {}
+
+        def prior_offset(chunk, b):
+            j0, width = CHUNKS[chunk]
+            return (PASSES * j0 + b * width) * PACK * 4
+
+        def words_after(chunk, b, place, width, name):
+            return reuse.tile([P, width], U32, name=name, offset=prior_offset(chunk, b) + place * HALF * 4, align_bytes=64)
+
+        def load_prior(chunk, b):
+            j0, width = CHUNKS[chunk]
+            rows = reuse.tile([P, PACK, width], F32, name=f"prior{chunk}_{b}", offset=prior_offset(chunk, b), align_bytes=64)
+            nc.sync.dma_start(
+                out=rows[:],
+                in_=prior[b * PASS : (b + 1) * PASS, j0 : j0 + width].rearrange("(p t) j -> p t j", t=PACK),
+            )
+            prior_rows[chunk, b] = rows
+
+        load_prior(0, 0)
+        w4_codes = keep.tile([P, PASSES, 2 * N], U8, align_bytes=64)
+        nc.sync.dma_start(out=w4_codes[:].bitcast(I32), in_=w4_words.bitcast(I32).rearrange("a p c -> p a c"))
+        for d in range(4):
+            nc.sync.dma_start(
+                out=w4_scale_tile[32 * d : 32 * d + 4, :, :].bitcast(I32),
+                in_=w4_scales.bitcast(I32)[:, 4 * d : 4 * d + 4, :].rearrange("a r c -> r a c"),
+            )
+        load_prior(0, 1)
+        for chunk in (1, 2):
+            for b in range(PASSES):
+                load_prior(chunk, b)
+
+        cols = HALF // LIST_ROWS
+        v2_codes = {}
+        for a in range(PASSES):
+            for b in range(PASSES):
+                codes = early.tile(
+                    [P, PACK, P], U32, name=f"v2_codes{a}_{b}", offset=(PASSES * PACK + 2 * a + b) * N * 4, align_bytes=64
+                )
+                nc.vector.tensor_copy(
+                    out=codes[:].rearrange("p t c -> p c t"),
+                    in_=v2_windows[a][:].bitcast(U32).indirect(list2[:, b * cols : (b + 1) * cols]),
+                )
+                v2_codes[a, b] = codes
+
+        def times_v2(acc, b, t, moving):
+            for a in range(PASSES):
+                codes, scales = moving(a)
+                first = b * PASS + t * P
+                nc.tensor.matmul_mx(
+                    out=acc,
+                    lhsT=v2_codes[a, b][:, t, :].bitcast(FP8X4),
+                    lhsT_scale=v2_scales[4 * a : P, first : first + P],
+                    rhs=codes.bitcast(FP8X4),
+                    rhs_scale=scales,
+                    start=(a == 0),
+                    stop=(a == PASSES - 1),
+                )
+
+        val_woven = []
+        for b in range(PASSES):
+            planes = ring.tile([P, PACK, N], BF16, name="val_planes", align_bytes=64, bufs=2)
+            for t in range(PACK):
+                acc = bank(4 + t, [P, N])
+                times_v2(acc[:], b, t, lambda a: (wv_codes[:, a * N : (a + 1) * N], wv_scales[:, a * N : (a + 1) * N]))
+                nc.scalar.activation(out=planes[:, t, :], in_=acc[:], func=ACT.Copy, scale=gv_cols[:, b, t : t + 1])
+            woven = ring.tile([P, N, PACK], BF16, name="woven", align_bytes=64, bufs=4)
+            weave(nc.scalar.copy, woven[:], planes)
+            val_woven.append(woven)
+
+        v_codes = {}
+
+        def gather_v(a, h, codes):
+            nc.vector.tensor_copy(
+                out=codes[:], in_=v_windows[a][:].bitcast(U32).indirect(lists[:, h * cols : (h + 1) * cols])
+            )
+            v_codes[a, h] = codes
+
+        for a in range(PASSES):
+            for h in range(S // HALF):
+                gather_v(a, h, keep.tile([P, HALF], U32, name=f"v_codes{a}_{h}", align_bytes=64))
+        val_mx = []
+
+        def v_operand(a, j0, width):
+            h, first = divmod(j0, HALF)
+            return v_codes[a, h][:, first : first + width], v_scales[:, a, j0 : j0 + width]
+
+        out_rows = out.rearrange("(n p) j -> p n j", p=P)
+
+        def score(chunk, b):
+            j0, width = CHUNKS[chunk]
+            share = HALF // width
+            planes = ring.tile([P, PACK, width], BF16, name="e_planes", align_bytes=64)
+            for t0 in range(0, PACK, share):
+                acc = bank((b * PACK + t0) // share % 4, [P, share, width])
+                for i in range(share):
+                    times_v2(acc[:, i, :], b, t0 + i, lambda a: v_operand(a, j0, width))
+                for i in range(share):
+                    nc.vector.scalar_tensor_tensor(
+                        out=planes[:, t0 + i, :],
+                        in0=acc[:, i, :],
+                        scalar=gm_cols[:, b, t0 + i : t0 + i + 1],
+                        in1=prior_rows[chunk, b][:, t0 + i, :],
+                        op0=ALU.mult,
+                        op1=ALU.add,
+                    )
+            woven = ring.tile([P, width, PACK], BF16, name="woven", align_bytes=64, bufs=4)
+            last = chunk == len(CHUNKS) - 1 and b == PASSES - 1
+            weave(nc.vector.tensor_copy if last else nc.scalar.copy, woven[:], planes)
+            return woven
+
+        def read_map(chunk, e_mx):
+            j0, width = CHUNKS[chunk]
+            share = HALF // width
+            step = width if width == HALF else P
+            first_bank = 0 if chunk == len(CHUNKS) - 1 else 4
+            results = [keep.tile([P, 2 * width], F32, name=f"result{chunk}_{pair}") for pair in range(2)]
+            for tile0 in range(0, N // P, share):
+                y = bank(first_bank + tile0 // share, [P, HALF])
+                for i in range(share):
+                    n0 = (tile0 + i) * P
+                    for a in range(PASSES):
+                        for c0 in range(0, width, step):
+                            codes, scales = v_operand(a, j0 + c0, step)
+                            nc.tensor.matmul_mx(
+                                out=y[:, i * width + c0 : i * width + c0 + step],
+                                lhsT=w4_codes[:, a, 2 * n0 : 2 * (n0 + P)].bitcast(FP4X4),
+                                lhsT_scale=w4_scale_tile[:, a, n0 : n0 + P],
+                                rhs=codes.bitcast(FP8X4),
+                                rhs_scale=scales,
+                                start=(i == 0 and a == 0 and c0 == 0),
+                                stop=False,
+                            )
+                for b in range(PASSES):
+                    for i in range(share):
+                        n0 = (tile0 + i) * P
+                        nc.tensor.matmul_mx(
+                            out=y[:, i * width : (i + 1) * width],
+                            lhsT=val_mx[b][0][:, n0 : n0 + P].bitcast(FP8X4),
+                            lhsT_scale=val_mx[b][1][:, n0 : n0 + P],
+                            rhs=e_mx[b][0][:].bitcast(FP8X4),
+                            rhs_scale=e_mx[b][1][:],
+                            start=False,
+                            stop=(b == PASSES - 1 and i == share - 1),
+                        )
+                pair, within = divmod(tile0, 2)
+                nc.scalar.activation(
+                    out=results[pair][:, within * HALF : (within + 1) * HALF], in_=y[:], func=ACT.Silu
+                )
+                if within + share == 2:
+                    nc.sync.dma_start(
+                        out=out_rows[:, 2 * pair : 2 * pair + 2, j0 : j0 + width],
+                        in_=results[pair][:].rearrange("p (n j) -> p n j", n=2),
+                    )
+
+        units = [(chunk, b) for chunk in range(len(CHUNKS)) for b in range(PASSES)]
+        e_woven, e_mx = {}, {}
+        for i in range(len(units) + 1):
+            if i < len(units):
+                e_woven[units[i]] = score(*units[i])
+            if i == 0:
+                val_mx.append(quantize(nc, keep, val_woven[0], "val0", words_after(0, 0, 0, N, "val0_codes")))
+            if i == 1:
+                val_mx.append(quantize(nc, keep, val_woven[1], "val1", words_after(0, 1, 1, N, "val1_codes")))
+            if i > 0:
+                chunk, b = units[i - 1]
+                width = CHUNKS[chunk][1]
+                if i < len(units):
+                    codes = words_after(*units[i], 0, width, f"e{chunk}_{b}_codes")
+                else:
+                    codes = keep.tile([P, width], U32, name="last_codes", align_bytes=64)
+                e_mx[chunk, b] = quantize(nc, keep, e_woven[chunk, b], f"e{chunk}_{b}", codes)
+                if b == PASSES - 1:
+                    read_map(chunk, [e_mx[chunk, 0], e_mx[chunk, 1]])

@@ -111,7 +111,7 @@ def tile_list_splice_map_reading_kernel(
         wv_codes, wv_scales = quantize(nc, keep, wv_woven, "wv", keep.tile([P, PASSES * N], U32, name="wv_codes", align_bytes=64))
 
         v_scales = early.tile([P, PASSES, S], U8, offset=N * PACK * 4, align_bytes=64)
-        nc.gpsimd.memset(v_scales[:].bitcast(I32), 0)
+        nc.vector.memset(v_scales[:].bitcast(I32), 0)
         for d in range(4):
             nc.sync.dma_start(
                 out=v_scales[32 * d : 32 * d + 4, :, :].bitcast(I32),
@@ -152,8 +152,8 @@ def tile_list_splice_map_reading_kernel(
 
         cols = HALF // LIST_ROWS
         v2_codes = {}
-        for a in range(PASSES):
-            for b in range(PASSES):
+        for b in range(PASSES):
+            for a in range(PASSES):
                 codes = early.tile(
                     [P, PACK, P], U32, name=f"v2_codes{a}_{b}", offset=(PASSES * PACK + 2 * a + b) * N * 4, align_bytes=64
                 )

@@ -22,8 +22,9 @@ PASS = P * PACK
 PASSES = 2
 HALF = 512
 LIST_ROWS = 16
+WINDOW = 4 * T
+KIB = 1024
 CHUNKS = ((0, 512), (512, 256), (768, 256))
-
 
 def weave(copy, woven, planes):
     copy(
@@ -31,13 +32,11 @@ def weave(copy, woven, planes):
         in_=planes[:].rearrange("p t (c i) -> p c t i", i=PACK),
     )
 
-
 def quantize(nc, pool, woven, name, codes):
     width = woven.shape[1]
     scales = pool.tile([P, width], U8, name=f"{name}_scales", align_bytes=64)
     nc.vector.quantize_mx(out=codes[:].bitcast(FP8X4), scales=scales[:], in_=woven[:].rearrange("p c t -> p (c t)"))
     return codes, scales
-
 
 def tile_list_splice_map_reading_kernel(
     tc, tab_words, tab_scales, tab2_words, tab2_scales, offs, offs2, w4_words, w4_scales, wv, gm, gv, prior, out
@@ -45,8 +44,6 @@ def tile_list_splice_map_reading_kernel(
     nc = tc.nc
     with ExitStack() as ctx:
         keep = ctx.enter_context(tc.tile_pool(name="keep", bufs=1))
-        ring = ctx.enter_context(tc.tile_pool(name="ring", bufs=3))
-        reuse = ctx.enter_context(tc.tile_pool(name="reuse", bufs=1))
         early = ctx.enter_context(tc.tile_pool(name="early", bufs=1))
         psum = ctx.enter_context(tc.psum_pool(name="psum", bufs=1))
 
@@ -56,47 +53,69 @@ def tile_list_splice_map_reading_kernel(
         def scalar_cast(out, in_):
             nc.scalar.activation(out=out, in_=in_, func=ACT.Copy)
 
-        def load_words(words, a, name):
-            window = keep.tile([P, T], I32, name=name, tag=name, align_bytes=64)
+        def load_words(words, a, name, pool, **place):
+            window = pool.tile([P, T], I32, name=name, align_bytes=64, **place)
             nc.sync.dma_start(out=window[:], in_=words[a].rearrange("p t i -> p (t i)").bitcast(I32))
             return window
 
-        v2_scale_window = keep.tile([P, T], U8, align_bytes=64)
+        def load_wv(a, pieces):
+            width = N // pieces
+            rows = wv[a * PASS : (a + 1) * PASS, :].rearrange("(p t) n -> p t n", t=PACK)
+            raw = []
+            for i in range(pieces):
+                piece = early.tile(
+                    [P, PACK, width], F32, name=f"wv_raw{a}_{i}", offset=a * WINDOW + i * WINDOW // pieces, align_bytes=64
+                )
+                nc.sync.dma_start(out=piece[:], in_=rows[:, :, i * width : (i + 1) * width])
+                raw.append(piece)
+            return raw
+
+        v2_scale_window = early.tile([P, T], U8, offset=4 * WINDOW, align_bytes=64)
         v_scale_window = keep.tile([P, T], U8, align_bytes=64)
-        w4_scale_tile = keep.tile([P, PASSES, N], U8, align_bytes=64)
+        moved_scales = keep.tile([P, PASSES, S + N], U8, align_bytes=64)
         nc.gpsimd.memset(v_scale_window[:].bitcast(I32), 0)
         nc.vector.memset(v2_scale_window[:].bitcast(I32), 0)
-        nc.gpsimd.memset(w4_scale_tile[:].bitcast(I32), 0)
+        warm = keep.tile([P, 2], F32)
+        nc.gpsimd.memset(warm[:], 0.0)
+        nc.vector.memset(moved_scales[:].bitcast(I32), 0)
 
         lists = keep.tile([P, S // LIST_ROWS], U16)
         nc.sync.dma_start(lists[:], offs)
         list2 = keep.tile([P, S // LIST_ROWS], U16)
         nc.sync.dma_start(list2[:], offs2)
-        nc.scalar.dma_start(
-            out=v_scale_window[0:P:4, :].bitcast(I32), in_=tab_scales.bitcast(I32).rearrange("a q t -> q a t")
-        )
-        for d in range(4):
-            nc.scalar.dma_start(
-                out=v2_scale_window[32 * d : 32 * d + 8, :].bitcast(I32),
-                in_=tab2_scales.bitcast(I32)[:, 4 * d : 4 * d + 4, :],
-            )
-        warm = keep.tile([P, 2], F32)
-        nc.gpsimd.memset(warm[:], 0.0)
-        nc.scalar.activation(out=warm[:, 1:2], in_=warm[:, 0:1], func=ACT.Silu)
-
-        wv_raw = []
-        for a in range(PASSES):
-            raw = early.tile([P, PACK, N], F32, name=f"wv_raw{a}", offset=a * N * PACK * 4, align_bytes=64)
-            nc.sync.dma_start(out=raw[:], in_=wv[a * PASS : (a + 1) * PASS, :].rearrange("(p t) n -> p t n", t=PACK))
-            wv_raw.append(raw)
-        v2_windows = [load_words(tab2_words, a, f"v2_window{a}") for a in range(PASSES)]
         gm_cols = keep.tile([P, PASSES, PACK], F32)
         gv_cols = keep.tile([P, PASSES, PACK], F32)
         nc.sync.dma_start(out=gv_cols[:], in_=gv.rearrange("(b p t) -> p b t", p=P, t=PACK))
         nc.sync.dma_start(out=gm_cols[:], in_=gm.rearrange("(b p t) -> p b t", p=P, t=PACK))
+        nc.sync.dma_start(
+            out=v_scale_window[0:P:4, :].bitcast(I32), in_=tab_scales.bitcast(I32).rearrange("a q t -> q a t")
+        )
+        for d in range(4):
+            nc.sync.dma_start(
+                out=v2_scale_window[32 * d : 32 * d + 8, :].bitcast(I32),
+                in_=tab2_scales.bitcast(I32)[:, 4 * d : 4 * d + 4, :],
+            )
+        nc.scalar.activation(out=warm[:, 1:2], in_=warm[:, 0:1], func=ACT.Silu)
+
+        wv_raw, v2_windows = [], []
+        wv_raw.append(load_wv(0, 2))
+        v2_windows.append(load_words(tab2_words, 0, "v2_window0", early, offset=2 * WINDOW))
+        staged_scales = keep.tile([P, S + N], U8, align_bytes=64)
+        nc.sync.dma_start(
+            out=staged_scales[0:P:4, S:].bitcast(I32), in_=w4_scales.bitcast(I32).rearrange("a q c -> q a c")
+        )
+        v2_windows.append(load_words(tab2_words, 1, "v2_window1", early, offset=3 * WINDOW))
+        wv_raw.append(load_wv(1, 2))
 
         v_scales_listed = keep.tile([P, S], U8, align_bytes=64)
         nc.vector.tensor_copy(out=v_scales_listed[:], in_=v_scale_window[:].indirect(lists[:]))
+
+        nc.vector.tensor_copy(out=staged_scales[:, :S].bitcast(I32), in_=v_scales_listed[:].bitcast(I32))
+        for d in range(4):
+            nc.scalar.dma_start(
+                out=moved_scales[32 * d : 32 * d + 4, :, :].bitcast(I32),
+                in_=staged_scales[32 * d : 32 * d + 32 : 4, :].bitcast(I32),
+            )
         v2_scales_listed = keep.tile([P, S], U8, align_bytes=64)
         nc.vector.tensor_copy(out=v2_scales_listed[:], in_=v2_scale_window[:].indirect(list2[:]))
         v2_scales = keep.tile([P, S], U8, align_bytes=64)
@@ -105,190 +124,219 @@ def tile_list_splice_map_reading_kernel(
             in_=v2_scales_listed[:].rearrange("p (b c t) -> p b t c", b=PASSES, t=PACK),
         )
 
-        wv_woven = early.tile([P, PASSES * N, PACK], BF16, offset=PASSES * N * PACK * 4, align_bytes=64)
-        for a in range(PASSES):
-            weave(scalar_cast, wv_woven[:, a * N : (a + 1) * N, :], wv_raw[a])
-        wv_codes, wv_scales = quantize(nc, keep, wv_woven, "wv", keep.tile([P, PASSES * N], U32, name="wv_codes", align_bytes=64))
+        cols = HALF // LIST_ROWS
+        v2_codes = {}
 
-        v_scales = early.tile([P, PASSES, S], U8, offset=N * PACK * 4, align_bytes=64)
-        nc.vector.memset(v_scales[:].bitcast(I32), 0)
-        for d in range(4):
-            nc.sync.dma_start(
-                out=v_scales[32 * d : 32 * d + 4, :, :].bitcast(I32),
-                in_=v_scales_listed[32 * d : 32 * d + 32 : 4, :].bitcast(I32),
+        def gather_v2(a, b):
+            codes = keep.tile([P, PACK, P], U32, name=f"v2_codes{a}_{b}", align_bytes=64)
+            nc.vector.tensor_copy(
+                out=codes[:].rearrange("p t c -> p c t"),
+                in_=v2_windows[a][:].bitcast(U32).indirect(list2[:, b * cols : (b + 1) * cols]),
+            )
+            v2_codes[a, b] = codes
+
+        def pass_v2(acc, a, b, t, codes, scales):
+            first = b * PASS + t * P
+            nc.tensor.matmul_mx(
+                out=acc,
+                lhsT=v2_codes[a, b][:, t, :].bitcast(FP8X4),
+                lhsT_scale=v2_scales[4 * a : P, first : first + P],
+                rhs=codes.bitcast(FP8X4),
+                rhs_scale=scales,
+                start=(a == 0),
+                stop=(a == PASSES - 1),
             )
 
-        v_windows = [load_words(tab_words, a, f"v_window{a}") for a in range(PASSES)]
+        val_acc = {(b, t): bank(PACK * b + t, [P, N]) for b in range(PASSES) for t in range(PACK)}
+        val_planes = keep.tile([P, PASSES, PACK, N], BF16, align_bytes=64)
+        for a in range(PASSES):
+            woven = keep.tile([P, N, PACK], BF16, name=f"wv_woven{a}", align_bytes=64)
+            width = N // len(wv_raw[a])
+            for i, piece in enumerate(wv_raw[a]):
+                weave(scalar_cast, woven[:, i * width : (i + 1) * width, :], piece)
+            gather_v2(a, 0)
+            if a == 1:
+                gather_v2(a, 1)
+            codes, scales = quantize(nc, keep, woven, f"wv{a}", keep.tile([P, N], U32, name=f"wv_codes{a}", align_bytes=64))
+            if a == 0:
+                gather_v2(a, 1)
+            for b in range(PASSES):
+                for t in range(PACK):
+                    pass_v2(val_acc[b, t][:], a, b, t, codes[:], scales[:])
+
+        for b in range(PASSES):
+            for t in range(PACK):
+                nc.scalar.activation(
+                    out=val_planes[:, b, t, :], in_=val_acc[b, t][:], func=ACT.Copy, scale=gv_cols[:, b, t : t + 1]
+                )
+
+        v_windows = [load_words(tab_words, a, f"v_window{a}", early, offset=(4 - 4 * a) * WINDOW) for a in range(PASSES)]
         prior_rows = {}
 
-        def prior_offset(chunk, b):
+        def load_prior(chunk, b, offset):
             j0, width = CHUNKS[chunk]
-            return (PASSES * j0 + b * width) * PACK * 4
-
-        def words_after(chunk, b, place, width, name):
-            return reuse.tile([P, width], U32, name=name, offset=prior_offset(chunk, b) + place * HALF * 4, align_bytes=64)
-
-        def load_prior(chunk, b):
-            j0, width = CHUNKS[chunk]
-            rows = reuse.tile([P, PACK, width], F32, name=f"prior{chunk}_{b}", offset=prior_offset(chunk, b), align_bytes=64)
+            rows = early.tile([P, PACK, width], F32, name=f"prior{chunk}_{b}", offset=offset, align_bytes=64)
             nc.sync.dma_start(
                 out=rows[:],
                 in_=prior[b * PASS : (b + 1) * PASS, j0 : j0 + width].rearrange("(p t) j -> p t j", t=PACK),
             )
             prior_rows[chunk, b] = rows
 
-        load_prior(0, 0)
-        w4_codes = keep.tile([P, PASSES, 2 * N], U8, align_bytes=64)
+        load_prior(0, 0, 2 * WINDOW)
+        w4_codes = early.tile([P, PASSES, 2 * N], U8, offset=WINDOW, align_bytes=64)
         nc.sync.dma_start(out=w4_codes[:].bitcast(I32), in_=w4_words.bitcast(I32).rearrange("a p c -> p a c"))
-        for d in range(4):
-            nc.sync.dma_start(
-                out=w4_scale_tile[32 * d : 32 * d + 4, :, :].bitcast(I32),
-                in_=w4_scales.bitcast(I32)[:, 4 * d : 4 * d + 4, :].rearrange("a r c -> r a c"),
-            )
-        load_prior(0, 1)
-        for chunk in (1, 2):
-            for b in range(PASSES):
-                load_prior(chunk, b)
-
-        cols = HALF // LIST_ROWS
-        v2_codes = {}
-        for b in range(PASSES):
-            for a in range(PASSES):
-                codes = early.tile(
-                    [P, PACK, P], U32, name=f"v2_codes{a}_{b}", offset=(PASSES * PACK + 2 * a + b) * N * 4, align_bytes=64
-                )
-                nc.vector.tensor_copy(
-                    out=codes[:].rearrange("p t c -> p c t"),
-                    in_=v2_windows[a][:].bitcast(U32).indirect(list2[:, b * cols : (b + 1) * cols]),
-                )
-                v2_codes[a, b] = codes
-
-        def times_v2(acc, b, t, moving):
-            for a in range(PASSES):
-                codes, scales = moving(a)
-                first = b * PASS + t * P
-                nc.tensor.matmul_mx(
-                    out=acc,
-                    lhsT=v2_codes[a, b][:, t, :].bitcast(FP8X4),
-                    lhsT_scale=v2_scales[4 * a : P, first : first + P],
-                    rhs=codes.bitcast(FP8X4),
-                    rhs_scale=scales,
-                    start=(a == 0),
-                    stop=(a == PASSES - 1),
-                )
-
-        val_woven = []
-        for b in range(PASSES):
-            planes = ring.tile([P, PACK, N], BF16, name="val_planes", align_bytes=64, bufs=2)
-            for t in range(PACK):
-                acc = bank(4 + t, [P, N])
-                times_v2(acc[:], b, t, lambda a: (wv_codes[:, a * N : (a + 1) * N], wv_scales[:, a * N : (a + 1) * N]))
-                nc.scalar.activation(out=planes[:, t, :], in_=acc[:], func=ACT.Copy, scale=gv_cols[:, b, t : t + 1])
-            woven = ring.tile([P, N, PACK], BF16, name="woven", align_bytes=64, bufs=4)
-            weave(nc.scalar.copy, woven[:], planes)
-            val_woven.append(woven)
+        load_prior(0, 1, 3 * WINDOW)
+        val_woven = keep.tile([P, PASSES * N, PACK], BF16, align_bytes=64)
+        nc.scalar.copy(
+            out=val_woven[:].rearrange("p (b c i) t -> p b c t i", b=PASSES, i=PACK),
+            in_=val_planes[:].rearrange("p b t (c i) -> p b c t i", i=PACK),
+        )
 
         v_codes = {}
+        for h in range(S // HALF):
+            for a in range(PASSES):
+                codes = keep.tile([P, HALF], U32, name=f"v_codes{a}_{h}", align_bytes=64)
+                nc.vector.tensor_copy(
+                    out=codes[:], in_=v_windows[a][:].bitcast(U32).indirect(lists[:, h * cols : (h + 1) * cols])
+                )
+                v_codes[a, h] = codes
 
-        def gather_v(a, h, codes):
-            nc.vector.tensor_copy(
-                out=codes[:], in_=v_windows[a][:].bitcast(U32).indirect(lists[:, h * cols : (h + 1) * cols])
-            )
-            v_codes[a, h] = codes
-
-        for a in range(PASSES):
-            for h in range(S // HALF):
-                gather_v(a, h, keep.tile([P, HALF], U32, name=f"v_codes{a}_{h}", align_bytes=64))
-        val_mx = []
+        for chunk in (1, 2):
+            for b in range(PASSES):
+                load_prior(chunk, b, (8 - 4 * chunk) * WINDOW + b * WINDOW // 2)
 
         def v_operand(a, j0, width):
             h, first = divmod(j0, HALF)
-            return v_codes[a, h][:, first : first + width], v_scales[:, a, j0 : j0 + width]
+            return v_codes[a, h][:, first : first + width], moved_scales[:, a, j0 : j0 + width]
 
         out_rows = out.rearrange("(n p) j -> p n j", p=P)
+        e_acc, e_planes, e_woven, e_mx, val_mx, y_acc = {}, {}, {}, {}, {}, {}
 
-        def score(chunk, b):
+        def score(chunk, b, first_bank):
             j0, width = CHUNKS[chunk]
             share = HALF // width
-            planes = ring.tile([P, PACK, width], BF16, name="e_planes", align_bytes=64)
-            for t0 in range(0, PACK, share):
-                acc = bank((b * PACK + t0) // share % 4, [P, share, width])
-                for i in range(share):
-                    times_v2(acc[:, i, :], b, t0 + i, lambda a: v_operand(a, j0, width))
-                for i in range(share):
-                    nc.vector.scalar_tensor_tensor(
-                        out=planes[:, t0 + i, :],
-                        in0=acc[:, i, :],
-                        scalar=gm_cols[:, b, t0 + i : t0 + i + 1],
-                        in1=prior_rows[chunk, b][:, t0 + i, :],
-                        op0=ALU.mult,
-                        op1=ALU.add,
-                    )
-            woven = ring.tile([P, width, PACK], BF16, name="woven", align_bytes=64, bufs=4)
-            last = chunk == len(CHUNKS) - 1 and b == PASSES - 1
-            weave(nc.vector.tensor_copy if last else nc.scalar.copy, woven[:], planes)
-            return woven
+            tiles = [bank(first_bank + i, [P, share, width]) for i in range(PACK // share)]
+            e_acc[chunk, b] = [tiles[t // share][:, t % share, :] for t in range(PACK)]
+            if share == 1:
+                order = [(a, t) for a in range(PASSES) for t in range(PACK)]
+            else:
+                order = [(a, t) for t in range(PACK) for a in range(PASSES)]
+            for a, t in order:
+                pass_v2(e_acc[chunk, b][t], a, b, t, *v_operand(a, j0, width))
 
-        def read_map(chunk, e_mx):
+        def offset(chunk, b):
+            width = CHUNKS[chunk][1]
+            planes = keep.tile([P, PACK, width], BF16, name=f"e_planes{chunk}_{b}", align_bytes=64)
+            for t in range(PACK):
+                nc.vector.scalar_tensor_tensor(
+                    out=planes[:, t, :],
+                    in0=e_acc[chunk, b][t],
+                    scalar=gm_cols[:, b, t : t + 1],
+                    in1=prior_rows[chunk, b][:, t, :],
+                    op0=ALU.mult,
+                    op1=ALU.add,
+                )
+            e_planes[chunk, b] = planes
+
+        def weave_e(chunk, b, copy):
+            width = CHUNKS[chunk][1]
+            woven = keep.tile([P, width, PACK], BF16, name=f"e_woven{chunk}_{b}", align_bytes=64)
+            weave(copy, woven[:], e_planes[chunk, b])
+            e_woven[chunk, b] = woven
+
+        def quantize_e(chunk, b):
+            width = CHUNKS[chunk][1]
+            codes = keep.tile([P, width], U32, name=f"e_codes{chunk}_{b}", align_bytes=64)
+            e_mx[chunk, b] = quantize(nc, keep, e_woven[chunk, b], f"e{chunk}_{b}", codes)
+
+        def quantize_val():
+            codes = keep.tile([P, PASSES * N], U32, name="val_codes", align_bytes=64)
+            codes, scales = quantize(nc, keep, val_woven, "val", codes)
+            for b in range(PASSES):
+                val_mx[b] = (codes[:, b * N : (b + 1) * N], scales[:, b * N : (b + 1) * N])
+
+        def own_codes(chunk, first_bank):
             j0, width = CHUNKS[chunk]
             share = HALF // width
             step = width if width == HALF else P
-            first_bank = 0 if chunk == len(CHUNKS) - 1 else 4
-            results = [keep.tile([P, 2 * width], F32, name=f"result{chunk}_{pair}") for pair in range(2)]
-            for tile0 in range(0, N // P, share):
-                y = bank(first_bank + tile0 // share, [P, HALF])
-                for i in range(share):
-                    n0 = (tile0 + i) * P
-                    for a in range(PASSES):
-                        for c0 in range(0, width, step):
-                            codes, scales = v_operand(a, j0 + c0, step)
-                            nc.tensor.matmul_mx(
-                                out=y[:, i * width + c0 : i * width + c0 + step],
-                                lhsT=w4_codes[:, a, 2 * n0 : 2 * (n0 + P)].bitcast(FP4X4),
-                                lhsT_scale=w4_scale_tile[:, a, n0 : n0 + P],
-                                rhs=codes.bitcast(FP8X4),
-                                rhs_scale=scales,
-                                start=(i == 0 and a == 0 and c0 == 0),
-                                stop=False,
-                            )
-                for b in range(PASSES):
-                    for i in range(share):
-                        n0 = (tile0 + i) * P
+            y_acc[chunk] = [bank(first_bank + i, [P, HALF]) for i in range(N // P // share)]
+            for tile in range(N // P):
+                y, i, n0 = y_acc[chunk][tile // share], tile % share, tile * P
+                for a in range(PASSES):
+                    for c0 in range(0, width, step):
+                        codes, scales = v_operand(a, j0 + c0, step)
                         nc.tensor.matmul_mx(
-                            out=y[:, i * width : (i + 1) * width],
-                            lhsT=val_mx[b][0][:, n0 : n0 + P].bitcast(FP8X4),
-                            lhsT_scale=val_mx[b][1][:, n0 : n0 + P],
-                            rhs=e_mx[b][0][:].bitcast(FP8X4),
-                            rhs_scale=e_mx[b][1][:],
-                            start=False,
-                            stop=(b == PASSES - 1 and i == share - 1),
+                            out=y[:, i * width + c0 : i * width + c0 + step],
+                            lhsT=w4_codes[:, a, 2 * n0 : 2 * (n0 + P)].bitcast(FP4X4),
+                            lhsT_scale=moved_scales[:, a, S + n0 : S + n0 + P],
+                            rhs=codes.bitcast(FP8X4),
+                            rhs_scale=scales,
+                            start=(i == 0 and a == 0 and c0 == 0),
+                            stop=False,
                         )
-                pair, within = divmod(tile0, 2)
-                nc.scalar.activation(
-                    out=results[pair][:, within * HALF : (within + 1) * HALF], in_=y[:], func=ACT.Silu
-                )
-                if within + share == 2:
-                    nc.sync.dma_start(
-                        out=out_rows[:, 2 * pair : 2 * pair + 2, j0 : j0 + width],
-                        in_=results[pair][:].rearrange("p (n j) -> p n j", n=2),
-                    )
 
-        units = [(chunk, b) for chunk in range(len(CHUNKS)) for b in range(PASSES)]
-        e_woven, e_mx = {}, {}
-        for i in range(len(units) + 1):
-            if i < len(units):
-                e_woven[units[i]] = score(*units[i])
-            if i == 0:
-                val_mx.append(quantize(nc, keep, val_woven[0], "val0", words_after(0, 0, 0, N, "val0_codes")))
-            if i == 1:
-                val_mx.append(quantize(nc, keep, val_woven[1], "val1", words_after(0, 1, 1, N, "val1_codes")))
-            if i > 0:
-                chunk, b = units[i - 1]
-                width = CHUNKS[chunk][1]
-                if i < len(units):
-                    codes = words_after(*units[i], 0, width, f"e{chunk}_{b}_codes")
-                else:
-                    codes = keep.tile([P, width], U32, name="last_codes", align_bytes=64)
-                e_mx[chunk, b] = quantize(nc, keep, e_woven[chunk, b], f"e{chunk}_{b}", codes)
-                if b == PASSES - 1:
-                    read_map(chunk, [e_mx[chunk, 0], e_mx[chunk, 1]])
+        def read_map(chunk, b):
+            width = CHUNKS[chunk][1]
+            share = HALF // width
+            for tile in range(N // P):
+                y, i, n0 = y_acc[chunk][tile // share], tile % share, tile * P
+                nc.tensor.matmul_mx(
+                    out=y[:, i * width : (i + 1) * width],
+                    lhsT=val_mx[b][0][:, n0 : n0 + P].bitcast(FP8X4),
+                    lhsT_scale=val_mx[b][1][:, n0 : n0 + P],
+                    rhs=e_mx[chunk, b][0][:].bitcast(FP8X4),
+                    rhs_scale=e_mx[chunk, b][1][:],
+                    start=False,
+                    stop=(b == PASSES - 1 and i == share - 1),
+                )
+
+        def finish(chunk):
+            j0, width = CHUNKS[chunk]
+            share = HALF // width
+            for i, y in enumerate(y_acc[chunk]):
+                result = keep.tile([P, HALF], F32, name=f"result{chunk}_{i}")
+                nc.scalar.activation(out=result[:], in_=y[:], func=ACT.Silu)
+                nc.sync.dma_start(
+                    out=out_rows[:, share * i : share * (i + 1), j0 : j0 + width],
+                    in_=result[:].rearrange("p (n j) -> p n j", n=share),
+                )
+
+        score(0, 0, 0)
+        score(0, 1, 4)
+        offset(0, 0)
+
+        weave_e(0, 0, nc.scalar.copy)
+        score(1, 0, 0)
+        score(1, 1, 2)
+        offset(0, 1)
+        weave_e(0, 1, nc.scalar.copy)
+        own_codes(0, 4)
+        quantize_val()
+        quantize_e(0, 0)
+        read_map(0, 0)
+        offset(1, 0)
+        weave_e(1, 0, nc.scalar.copy)
+        score(2, 0, 0)
+        quantize_e(0, 1)
+
+        read_map(0, 1)
+        offset(1, 1)
+        score(2, 1, 2)
+        finish(0)
+        weave_e(1, 1, nc.scalar.copy)
+        quantize_e(1, 0)
+        offset(2, 0)
+        own_codes(1, 4)
+        read_map(1, 0)
+        offset(2, 1)
+        own_codes(2, 6)
+        quantize_e(1, 1)
+        read_map(1, 1)
+        finish(1)
+        weave_e(2, 0, nc.vector.tensor_copy)
+        weave_e(2, 1, nc.vector.tensor_copy)
+        quantize_e(2, 0)
+        read_map(2, 0)
+        quantize_e(2, 1)
+        read_map(2, 1)
+        finish(2)

@@ -22,21 +22,8 @@ PASS = P * PACK
 PASSES = 2
 HALF = 512
 LIST_ROWS = 16
-WINDOW = 4 * T
-KIB = 1024
 CHUNKS = ((0, 512), (512, 256), (768, 256))
-
-def weave(copy, woven, planes):
-    copy(
-        out=woven.rearrange("p (c i) t -> p c t i", i=PACK),
-        in_=planes[:].rearrange("p t (c i) -> p c t i", i=PACK),
-    )
-
-def quantize(nc, pool, woven, name, codes):
-    width = woven.shape[1]
-    scales = pool.tile([P, width], U8, name=f"{name}_scales", align_bytes=64)
-    nc.vector.quantize_mx(out=codes[:].bitcast(FP8X4), scales=scales[:], in_=woven[:].rearrange("p c t -> p (c t)"))
-    return codes, scales
+KIB = 1024
 
 def tile_list_splice_map_reading_kernel(
     tc, tab_words, tab_scales, tab2_words, tab2_scales, offs, offs2, w4_words, w4_scales, wv, gm, gv, prior, out
@@ -44,8 +31,14 @@ def tile_list_splice_map_reading_kernel(
     nc = tc.nc
     with ExitStack() as ctx:
         keep = ctx.enter_context(tc.tile_pool(name="keep", bufs=1))
-        early = ctx.enter_context(tc.tile_pool(name="early", bufs=1))
+        shared = ctx.enter_context(tc.tile_pool(name="shared", bufs=1))
         psum = ctx.enter_context(tc.psum_pool(name="psum", bufs=1))
+
+        def kept(shape, dtype, name):
+            return keep.tile(shape, dtype, name=name, align_bytes=64)
+
+        def placed(shape, dtype, name, kib):
+            return shared.tile(shape, dtype, name=name, offset=kib * KIB, align_bytes=64)
 
         def bank(index, shape):
             return psum.tile(shape, F32, name=f"bank{index}", tag=f"bank{index}")
@@ -53,82 +46,114 @@ def tile_list_splice_map_reading_kernel(
         def scalar_cast(out, in_):
             nc.scalar.activation(out=out, in_=in_, func=ACT.Copy)
 
-        def load_words(words, a, name, pool, **place):
-            window = pool.tile([P, T], I32, name=name, align_bytes=64, **place)
+        def weave(copy, woven, planes):
+            copy(
+                out=woven.rearrange("p (c i) t -> p c t i", i=PACK),
+                in_=planes.rearrange("p t (c i) -> p c t i", i=PACK),
+            )
+
+        def scalar_weave(woven, planes):
+            weave(nc.scalar.copy, woven, planes)
+
+        def vector_weave(woven, planes):
+            weave(nc.vector.tensor_copy, woven, planes)
+
+        def gpsimd_weave(woven, planes):
+            nc.gpsimd.tensor_scalar(
+                out=woven, in0=planes.rearrange("p t c -> p c t"), scalar1=1.0, scalar2=0.0, op0=ALU.mult, op1=ALU.add
+            )
+
+        def quantize(woven, name, kib=None):
+            width = woven.shape[1]
+            codes = kept([P, width], U32, f"{name}_codes") if kib is None else placed([P, width], U32, f"{name}_codes", kib)
+            scales = kept([P, width], U8, f"{name}_scales")
+            nc.vector.quantize_mx(out=codes[:].bitcast(FP8X4), scales=scales[:], in_=woven[:].rearrange("p c t -> p (c t)"))
+            return codes, scales
+
+        def load_words(words, a, name, kib):
+            window = placed([P, T], I32, name, kib)
             nc.sync.dma_start(out=window[:], in_=words[a].rearrange("p t i -> p (t i)").bitcast(I32))
             return window
 
-        def load_wv(a, pieces):
-            width = N // pieces
+        def load_wv(a, kib, pieces):
             rows = wv[a * PASS : (a + 1) * PASS, :].rearrange("(p t) n -> p t n", t=PACK)
-            raw = []
+            halves = []
+            width = N // pieces
             for i in range(pieces):
-                piece = early.tile(
-                    [P, PACK, width], F32, name=f"wv_raw{a}_{i}", offset=a * WINDOW + i * WINDOW // pieces, align_bytes=64
-                )
-                nc.sync.dma_start(out=piece[:], in_=rows[:, :, i * width : (i + 1) * width])
-                raw.append(piece)
-            return raw
+                half = placed([P, PACK, width], F32, f"wv_raw{a}_{i}", kib + 8 // pieces * i)
+                nc.sync.dma_start(out=half[:], in_=rows[:, :, i * width : (i + 1) * width])
+                halves.append(half)
+            return halves
 
-        v2_scale_window = early.tile([P, T], U8, offset=4 * WINDOW, align_bytes=64)
-        v_scale_window = keep.tile([P, T], U8, align_bytes=64)
-        moved_scales = keep.tile([P, PASSES, S + N], U8, align_bytes=64)
-        nc.gpsimd.memset(v_scale_window[:].bitcast(I32), 0)
-        nc.vector.memset(v2_scale_window[:].bitcast(I32), 0)
+        prior_rows = {}
+
+        def load_prior(chunk, b, kib, t0=0, planes=PACK):
+            j0, width = CHUNKS[chunk]
+            rows = placed([P, planes, width], F32, f"prior{chunk}_{b}_{t0}", kib)
+            source = prior[b * PASS : (b + 1) * PASS, j0 : j0 + width].rearrange("(p t) j -> p t j", t=PACK)
+            nc.sync.dma_start(out=rows[:], in_=source[:, t0 : t0 + planes, :])
+            for t in range(planes):
+                prior_rows[chunk, b, t0 + t] = rows[:, t, :]
+
+        v2_scale_window = kept([P, T], U8, "v2_scale_window")
+        v_scale_window = placed([P, T], U8, "v_scale_window", 37)
+        moved_v2 = kept([P, PASSES, S + N], U8, "moved_v2")
+        moved_v = kept([P, PASSES, S], U8, "moved_v")
+        nc.gpsimd.memset(v2_scale_window[:].bitcast(I32), 0)
+        nc.vector.memset(v_scale_window[:, : T // 2].bitcast(I32), 0)
+        nc.gpsimd.memset(v_scale_window[:, T // 2 :].bitcast(I32), 0)
         warm = keep.tile([P, 2], F32)
         nc.gpsimd.memset(warm[:], 0.0)
-        nc.vector.memset(moved_scales[:].bitcast(I32), 0)
+        nc.vector.memset(moved_v2[:].bitcast(I32), 0)
+        nc.vector.memset(moved_v[:].bitcast(I32), 0)
 
-        lists = keep.tile([P, S // LIST_ROWS], U16)
-        nc.sync.dma_start(lists[:], offs)
         list2 = keep.tile([P, S // LIST_ROWS], U16)
         nc.sync.dma_start(list2[:], offs2)
+        lists = keep.tile([P, S // LIST_ROWS], U16)
+        nc.sync.dma_start(lists[:], offs)
         gm_cols = keep.tile([P, PASSES, PACK], F32)
         gv_cols = keep.tile([P, PASSES, PACK], F32)
         nc.sync.dma_start(out=gv_cols[:], in_=gv.rearrange("(b p t) -> p b t", p=P, t=PACK))
-        nc.sync.dma_start(out=gm_cols[:], in_=gm.rearrange("(b p t) -> p b t", p=P, t=PACK))
-        nc.sync.dma_start(
-            out=v_scale_window[0:P:4, :].bitcast(I32), in_=tab_scales.bitcast(I32).rearrange("a q t -> q a t")
-        )
-        for d in range(4):
-            nc.sync.dma_start(
-                out=v2_scale_window[32 * d : 32 * d + 8, :].bitcast(I32),
-                in_=tab2_scales.bitcast(I32)[:, 4 * d : 4 * d + 4, :],
-            )
-        nc.scalar.activation(out=warm[:, 1:2], in_=warm[:, 0:1], func=ACT.Silu)
-
-        wv_raw, v2_windows = [], []
-        wv_raw.append(load_wv(0, 2))
-        v2_windows.append(load_words(tab2_words, 0, "v2_window0", early, offset=2 * WINDOW))
-        staged_scales = keep.tile([P, S + N], U8, align_bytes=64)
+        staged_scales = kept([P, S + N], U8, "staged_scales")
         nc.sync.dma_start(
             out=staged_scales[0:P:4, S:].bitcast(I32), in_=w4_scales.bitcast(I32).rearrange("a q c -> q a c")
         )
-        v2_windows.append(load_words(tab2_words, 1, "v2_window1", early, offset=3 * WINDOW))
-        wv_raw.append(load_wv(1, 2))
+        nc.sync.dma_start(
+            out=v2_scale_window[0:P:4, :].bitcast(I32), in_=tab2_scales.bitcast(I32).rearrange("a q t -> q a t")
+        )
+        nc.scalar.activation(out=warm[:, 1:2], in_=warm[:, 0:1], func=ACT.Silu)
+        wv_raw = [load_wv(0, 0, 1)]
+        nc.sync.dma_start(
+            out=v_scale_window[0:P:4, :].bitcast(I32), in_=tab_scales.bitcast(I32).rearrange("a q t -> q a t")
+        )
+        nc.sync.dma_start(out=gm_cols[:], in_=gm.rearrange("(b p t) -> p b t", p=P, t=PACK))
+        v2_windows = [load_words(tab2_words, 0, "v2_window0", 16)]
+        wv_raw.append(load_wv(1, 8, 1))
 
-        v_scales_listed = keep.tile([P, S], U8, align_bytes=64)
-        nc.vector.tensor_copy(out=v_scales_listed[:], in_=v_scale_window[:].indirect(lists[:]))
+        def move_rows(moved, source):
+            for d in range(4):
+                nc.sync.dma_start(
+                    out=moved[32 * d : 32 * d + 4, :, :].bitcast(I32),
+                    in_=source[32 * d : 32 * d + 32 : 4, :].bitcast(I32),
+                )
 
-        nc.vector.tensor_copy(out=staged_scales[:, :S].bitcast(I32), in_=v_scales_listed[:].bitcast(I32))
-        for d in range(4):
-            nc.scalar.dma_start(
-                out=moved_scales[32 * d : 32 * d + 4, :, :].bitcast(I32),
-                in_=staged_scales[32 * d : 32 * d + 32 : 4, :].bitcast(I32),
-            )
-        v2_scales_listed = keep.tile([P, S], U8, align_bytes=64)
+        v2_scales_listed = placed([P, S], U8, "v2_scales_listed", 24)
         nc.vector.tensor_copy(out=v2_scales_listed[:], in_=v2_scale_window[:].indirect(list2[:]))
-        v2_scales = keep.tile([P, S], U8, align_bytes=64)
         nc.vector.tensor_copy(
-            out=v2_scales[:].rearrange("p (b t c) -> p b t c", b=PASSES, t=PACK),
+            out=staged_scales[:, :S].rearrange("p (b t c) -> p b t c", b=PASSES, t=PACK),
             in_=v2_scales_listed[:].rearrange("p (b c t) -> p b t c", b=PASSES, t=PACK),
         )
+        move_rows(moved_v2, staged_scales)
+        v2_windows.append(load_words(tab2_words, 1, "v2_window1", 24))
+        v_scales_listed = kept([P, S], U8, "v_scales_listed")
+        nc.vector.tensor_copy(out=v_scales_listed[:], in_=v_scale_window[:].indirect(lists[:]))
+        move_rows(moved_v, v_scales_listed)
 
         cols = HALF // LIST_ROWS
         v2_codes = {}
 
         def gather_v2(a, b):
-            codes = keep.tile([P, PACK, P], U32, name=f"v2_codes{a}_{b}", align_bytes=64)
+            codes = kept([P, PACK, P], U32, f"v2_codes{a}_{b}")
             nc.vector.tensor_copy(
                 out=codes[:].rearrange("p t c -> p c t"),
                 in_=v2_windows[a][:].bitcast(U32).indirect(list2[:, b * cols : (b + 1) * cols]),
@@ -140,7 +165,7 @@ def tile_list_splice_map_reading_kernel(
             nc.tensor.matmul_mx(
                 out=acc,
                 lhsT=v2_codes[a, b][:, t, :].bitcast(FP8X4),
-                lhsT_scale=v2_scales[4 * a : P, first : first + P],
+                lhsT_scale=moved_v2[:, a, first : first + P],
                 rhs=codes.bitcast(FP8X4),
                 rhs_scale=scales,
                 start=(a == 0),
@@ -148,132 +173,127 @@ def tile_list_splice_map_reading_kernel(
             )
 
         val_acc = {(b, t): bank(PACK * b + t, [P, N]) for b in range(PASSES) for t in range(PACK)}
-        val_planes = keep.tile([P, PASSES, PACK, N], BF16, align_bytes=64)
         for a in range(PASSES):
-            woven = keep.tile([P, N, PACK], BF16, name=f"wv_woven{a}", align_bytes=64)
-            width = N // len(wv_raw[a])
-            for i, piece in enumerate(wv_raw[a]):
-                weave(scalar_cast, woven[:, i * width : (i + 1) * width, :], piece)
-            gather_v2(a, 0)
-            if a == 1:
-                gather_v2(a, 1)
-            codes, scales = quantize(nc, keep, woven, f"wv{a}", keep.tile([P, N], U32, name=f"wv_codes{a}", align_bytes=64))
+            woven = kept([P, N, PACK], BF16, f"wv_woven{a}")
+            for i, half in enumerate(wv_raw[a]):
+                width = half.shape[2]
+                weave(scalar_cast, woven[:, i * width : (i + 1) * width, :], half[:])
             if a == 0:
-                gather_v2(a, 1)
+                gather_v2(a, 0)
+            codes, scales = quantize(woven, f"wv{a}")
+            if a == 1:
+                gather_v2(a, 0)
+            gather_v2(a, 1)
             for b in range(PASSES):
                 for t in range(PACK):
                     pass_v2(val_acc[b, t][:], a, b, t, codes[:], scales[:])
-
+        val_planes = placed([P, PASSES, PACK, N], BF16, "val_planes", 45)
         for b in range(PASSES):
             for t in range(PACK):
                 nc.scalar.activation(
                     out=val_planes[:, b, t, :], in_=val_acc[b, t][:], func=ACT.Copy, scale=gv_cols[:, b, t : t + 1]
                 )
 
-        v_windows = [load_words(tab_words, a, f"v_window{a}", early, offset=(4 - 4 * a) * WINDOW) for a in range(PASSES)]
-        prior_rows = {}
-
-        def load_prior(chunk, b, offset):
-            j0, width = CHUNKS[chunk]
-            rows = early.tile([P, PACK, width], F32, name=f"prior{chunk}_{b}", offset=offset, align_bytes=64)
-            nc.sync.dma_start(
-                out=rows[:],
-                in_=prior[b * PASS : (b + 1) * PASS, j0 : j0 + width].rearrange("(p t) j -> p t j", t=PACK),
-            )
-            prior_rows[chunk, b] = rows
-
-        load_prior(0, 0, 2 * WINDOW)
-        w4_codes = early.tile([P, PASSES, 2 * N], U8, offset=WINDOW, align_bytes=64)
+        v_windows = [load_words(tab_words, 0, "v_window0", 37), load_words(tab_words, 1, "v_window1", 0)]
+        load_prior(0, 0, 16)
+        load_prior(0, 1, 24)
+        w4_codes = placed([P, PASSES, 2 * N], U8, "w4_codes", 8)
         nc.sync.dma_start(out=w4_codes[:].bitcast(I32), in_=w4_words.bitcast(I32).rearrange("a p c -> p a c"))
-        load_prior(0, 1, 3 * WINDOW)
-        val_woven = keep.tile([P, PASSES * N, PACK], BF16, align_bytes=64)
-        nc.scalar.copy(
-            out=val_woven[:].rearrange("p (b c i) t -> p b c t i", b=PASSES, i=PACK),
-            in_=val_planes[:].rearrange("p b t (c i) -> p b c t i", i=PACK),
-        )
 
         v_codes = {}
         for h in range(S // HALF):
             for a in range(PASSES):
-                codes = keep.tile([P, HALF], U32, name=f"v_codes{a}_{h}", align_bytes=64)
+                codes = kept([P, HALF], U32, f"v_codes{a}_{h}")
                 nc.vector.tensor_copy(
                     out=codes[:], in_=v_windows[a][:].bitcast(U32).indirect(lists[:, h * cols : (h + 1) * cols])
                 )
                 v_codes[a, h] = codes
 
+        val_woven = placed([P, PASSES * N, PACK], BF16, "val_woven", 0)
+        scalar_weave(val_woven[:, N:, :], val_planes[:, 1])
+        gpsimd_weave(val_woven[:, :N, :], val_planes[:, 0])
         for chunk in (1, 2):
             for b in range(PASSES):
-                load_prior(chunk, b, (8 - 4 * chunk) * WINDOW + b * WINDOW // 2)
+                load_prior(chunk, b, 29 + 8 * chunk + 4 * b)
 
         def v_operand(a, j0, width):
             h, first = divmod(j0, HALF)
-            return v_codes[a, h][:, first : first + width], moved_scales[:, a, j0 : j0 + width]
+            return v_codes[a, h][:, first : first + width], moved_v[:, a, j0 : j0 + width]
 
         out_rows = out.rearrange("(n p) j -> p n j", p=P)
         e_acc, e_planes, e_woven, e_mx, val_mx, y_acc = {}, {}, {}, {}, {}, {}
 
-        def score(chunk, b, first_bank):
-            j0, width = CHUNKS[chunk]
+        def open_score(chunk, b, first_bank):
+            width = CHUNKS[chunk][1]
             share = HALF // width
             tiles = [bank(first_bank + i, [P, share, width]) for i in range(PACK // share)]
             e_acc[chunk, b] = [tiles[t // share][:, t % share, :] for t in range(PACK)]
-            if share == 1:
-                order = [(a, t) for a in range(PASSES) for t in range(PACK)]
-            else:
-                order = [(a, t) for t in range(PACK) for a in range(PASSES)]
+
+        def score_passes(chunk, b, order):
+            j0, width = CHUNKS[chunk]
             for a, t in order:
                 pass_v2(e_acc[chunk, b][t], a, b, t, *v_operand(a, j0, width))
 
-        def offset(chunk, b):
+        def score(chunk, b, first_bank):
+            open_score(chunk, b, first_bank)
+            score_passes(chunk, b, [(a, t) for t in range(PACK) for a in range(PASSES)])
+
+        def offset(chunk, b, kib):
             width = CHUNKS[chunk][1]
-            planes = keep.tile([P, PACK, width], BF16, name=f"e_planes{chunk}_{b}", align_bytes=64)
+            planes = placed([P, PACK, width], BF16, f"e_planes{chunk}_{b}", kib)
             for t in range(PACK):
                 nc.vector.scalar_tensor_tensor(
                     out=planes[:, t, :],
                     in0=e_acc[chunk, b][t],
                     scalar=gm_cols[:, b, t : t + 1],
-                    in1=prior_rows[chunk, b][:, t, :],
+                    in1=prior_rows[chunk, b, t],
                     op0=ALU.mult,
                     op1=ALU.add,
                 )
             e_planes[chunk, b] = planes
 
-        def weave_e(chunk, b, copy):
+        def weave_e(chunk, b, engine_weave, kib):
             width = CHUNKS[chunk][1]
-            woven = keep.tile([P, width, PACK], BF16, name=f"e_woven{chunk}_{b}", align_bytes=64)
-            weave(copy, woven[:], e_planes[chunk, b])
+            woven = placed([P, width, PACK], BF16, f"e_woven{chunk}_{b}", kib)
+            first = 0
+            for one_weave, columns in engine_weave:
+                one_weave(woven[:, first : first + columns, :], e_planes[chunk, b][:, :, first : first + columns])
+                first = first + columns
             e_woven[chunk, b] = woven
 
-        def quantize_e(chunk, b):
-            width = CHUNKS[chunk][1]
-            codes = keep.tile([P, width], U32, name=f"e_codes{chunk}_{b}", align_bytes=64)
-            e_mx[chunk, b] = quantize(nc, keep, e_woven[chunk, b], f"e{chunk}_{b}", codes)
+        def quantize_e(chunk, b, kib=None):
+            e_mx[chunk, b] = quantize(e_woven[chunk, b], f"e{chunk}_{b}", kib)
 
-        def quantize_val():
-            codes = keep.tile([P, PASSES * N], U32, name="val_codes", align_bytes=64)
-            codes, scales = quantize(nc, keep, val_woven, "val", codes)
+        def quantize_val(kib):
+            codes, scales = quantize(val_woven, "val", kib)
             for b in range(PASSES):
                 val_mx[b] = (codes[:, b * N : (b + 1) * N], scales[:, b * N : (b + 1) * N])
 
-        def own_codes(chunk, first_bank):
+        def open_y(chunk, first_bank):
+            share = HALF // CHUNKS[chunk][1]
+            y_acc[chunk] = [bank(first_bank + i, [P, HALF]) for i in range(N // P // share)]
+
+        def own_passes(chunk, order):
             j0, width = CHUNKS[chunk]
             share = HALF // width
             step = width if width == HALF else P
-            y_acc[chunk] = [bank(first_bank + i, [P, HALF]) for i in range(N // P // share)]
-            for tile in range(N // P):
+            for a, tile in order:
                 y, i, n0 = y_acc[chunk][tile // share], tile % share, tile * P
-                for a in range(PASSES):
-                    for c0 in range(0, width, step):
-                        codes, scales = v_operand(a, j0 + c0, step)
-                        nc.tensor.matmul_mx(
-                            out=y[:, i * width + c0 : i * width + c0 + step],
-                            lhsT=w4_codes[:, a, 2 * n0 : 2 * (n0 + P)].bitcast(FP4X4),
-                            lhsT_scale=moved_scales[:, a, S + n0 : S + n0 + P],
-                            rhs=codes.bitcast(FP8X4),
-                            rhs_scale=scales,
-                            start=(i == 0 and a == 0 and c0 == 0),
-                            stop=False,
-                        )
+                for c0 in range(0, width, step):
+                    codes, scales = v_operand(a, j0 + c0, step)
+                    nc.tensor.matmul_mx(
+                        out=y[:, i * width + c0 : i * width + c0 + step],
+                        lhsT=w4_codes[:, a, 2 * n0 : 2 * (n0 + P)].bitcast(FP4X4),
+                        lhsT_scale=moved_v2[:, a, S + n0 : S + n0 + P],
+                        rhs=codes.bitcast(FP8X4),
+                        rhs_scale=scales,
+                        start=(i == 0 and a == 0 and c0 == 0),
+                        stop=False,
+                    )
+
+        def own_codes(chunk, first_bank):
+            open_y(chunk, first_bank)
+            own_passes(chunk, [(a, tile) for tile in range(N // P) for a in range(PASSES)])
 
         def read_map(chunk, b):
             width = CHUNKS[chunk][1]
@@ -301,42 +321,43 @@ def tile_list_splice_map_reading_kernel(
                     in_=result[:].rearrange("p (n j) -> p n j", n=share),
                 )
 
-        score(0, 0, 0)
+        open_score(0, 0, 0)
+        score_passes(0, 0, [(a, t) for a in range(PASSES) for t in range(PACK)])
         score(0, 1, 4)
-        offset(0, 0)
-
-        weave_e(0, 0, nc.scalar.copy)
+        offset(0, 0, 54)
+        weave_e(0, 0, [(scalar_weave, 512)], 62)
         score(1, 0, 0)
         score(1, 1, 2)
-        offset(0, 1)
-        weave_e(0, 1, nc.scalar.copy)
+        offset(0, 1, 58)
+
+        weave_e(0, 1, [(scalar_weave, 512)], 66)
         own_codes(0, 4)
-        quantize_val()
-        quantize_e(0, 0)
+        quantize_val(24)
+        quantize_e(0, 0, 28)
         read_map(0, 0)
-        offset(1, 0)
-        weave_e(1, 0, nc.scalar.copy)
+        offset(1, 0, 62)
+        weave_e(1, 0, [(scalar_weave, 256)], 72)
         score(2, 0, 0)
-        quantize_e(0, 1)
+        quantize_e(0, 1, 37)
 
         read_map(0, 1)
-        offset(1, 1)
+        offset(1, 1, 66)
         score(2, 1, 2)
         finish(0)
-        weave_e(1, 1, nc.scalar.copy)
-        quantize_e(1, 0)
-        offset(2, 0)
+        quantize_e(1, 0, 41)
+        weave_e(1, 1, [(gpsimd_weave, 256)], 73)
+        offset(2, 0, 71)
+        weave_e(2, 0, [(scalar_weave, 256)], 76)
         own_codes(1, 4)
         read_map(1, 0)
-        offset(2, 1)
-        own_codes(2, 6)
-        quantize_e(1, 1)
+        quantize_e(1, 1, 45)
         read_map(1, 1)
+        offset(2, 1, 74)
+        own_codes(2, 6)
         finish(1)
-        weave_e(2, 0, nc.vector.tensor_copy)
-        weave_e(2, 1, nc.vector.tensor_copy)
-        quantize_e(2, 0)
+        quantize_e(2, 0, 49)
         read_map(2, 0)
+        weave_e(2, 1, [(vector_weave, 256)], 78)
         quantize_e(2, 1)
         read_map(2, 1)
         finish(2)

@@ -58,11 +58,6 @@ def tile_list_splice_map_reading_kernel(
         def vector_weave(woven, planes):
             weave(nc.vector.tensor_copy, woven, planes)
 
-        def gpsimd_weave(woven, planes):
-            nc.gpsimd.tensor_scalar(
-                out=woven, in0=planes.rearrange("p t c -> p c t"), scalar1=1.0, scalar2=0.0, op0=ALU.mult, op1=ALU.add
-            )
-
         def quantize(woven, name, kib=None):
             width = woven.shape[1]
             codes = kept([P, width], U32, f"{name}_codes") if kib is None else placed([P, width], U32, f"{name}_codes", kib)
@@ -128,7 +123,7 @@ def tile_list_splice_map_reading_kernel(
         )
         nc.sync.dma_start(out=gm_cols[:], in_=gm.rearrange("(b p t) -> p b t", p=P, t=PACK))
         v2_windows = [load_words(tab2_words, 0, "v2_window0", 16)]
-        wv_raw.append(load_wv(1, 8, 1))
+        wv_raw.append(load_wv(1, 8, 2))
 
         def move_rows(moved, source):
             for d in range(4):
@@ -180,7 +175,7 @@ def tile_list_splice_map_reading_kernel(
                 weave(scalar_cast, woven[:, i * width : (i + 1) * width, :], half[:])
             if a == 0:
                 gather_v2(a, 0)
-            codes, scales = quantize(woven, f"wv{a}")
+            codes, scales = quantize(woven, f"wv{a}", 80 + 2 * a)
             if a == 1:
                 gather_v2(a, 0)
             gather_v2(a, 1)
@@ -195,9 +190,9 @@ def tile_list_splice_map_reading_kernel(
                 )
 
         v_windows = [load_words(tab_words, 0, "v_window0", 37), load_words(tab_words, 1, "v_window1", 0)]
-        load_prior(0, 0, 16)
-        load_prior(0, 1, 24)
-        w4_codes = placed([P, PASSES, 2 * N], U8, "w4_codes", 8)
+        load_prior(0, 0, 15)
+        load_prior(0, 1, 25)
+        w4_codes = placed([P, PASSES, 2 * N], U8, "w4_codes", 23)
         nc.sync.dma_start(out=w4_codes[:].bitcast(I32), in_=w4_words.bitcast(I32).rearrange("a p c -> p a c"))
 
         v_codes = {}
@@ -209,12 +204,10 @@ def tile_list_splice_map_reading_kernel(
                 )
                 v_codes[a, h] = codes
 
-        val_woven = placed([P, PASSES * N, PACK], BF16, "val_woven", 0)
-        scalar_weave(val_woven[:, N:, :], val_planes[:, 1])
-        gpsimd_weave(val_woven[:, :N, :], val_planes[:, 0])
-        for chunk in (1, 2):
-            for b in range(PASSES):
-                load_prior(chunk, b, 29 + 8 * chunk + 4 * b)
+        for b in range(PASSES):
+            load_prior(1, b, 37 + 4 * b)
+        for b in range(PASSES):
+            load_prior(2, b, 4 * b)
 
         def v_operand(a, j0, width):
             h, first = divmod(j0, HALF)
@@ -264,10 +257,14 @@ def tile_list_splice_map_reading_kernel(
         def quantize_e(chunk, b, kib=None):
             e_mx[chunk, b] = quantize(e_woven[chunk, b], f"e{chunk}_{b}", kib)
 
-        def quantize_val(kib):
-            codes, scales = quantize(val_woven, "val", kib)
-            for b in range(PASSES):
-                val_mx[b] = (codes[:, b * N : (b + 1) * N], scales[:, b * N : (b + 1) * N])
+        val_woven = {}
+
+        def weave_val(b, engine_weave, kib):
+            val_woven[b] = placed([P, N, PACK], BF16, f"val_woven{b}", kib)
+            engine_weave(val_woven[b][:], val_planes[:, b])
+
+        def quantize_val(b, kib):
+            val_mx[b] = quantize(val_woven[b], f"val{b}", kib)
 
         def open_y(chunk, first_bank):
             share = HALF // CHUNKS[chunk][1]
@@ -310,10 +307,11 @@ def tile_list_splice_map_reading_kernel(
                     stop=(b == PASSES - 1 and i == share - 1),
                 )
 
-        def finish(chunk):
+        def finish(chunk, banks=None):
             j0, width = CHUNKS[chunk]
             share = HALF // width
-            for i, y in enumerate(y_acc[chunk]):
+            for i in banks or range(len(y_acc[chunk])):
+                y = y_acc[chunk][i]
                 result = keep.tile([P, HALF], F32, name=f"result{chunk}_{i}")
                 nc.scalar.activation(out=result[:], in_=y[:], func=ACT.Silu)
                 nc.sync.dma_start(
@@ -321,6 +319,8 @@ def tile_list_splice_map_reading_kernel(
                     in_=result[:].rearrange("p (n j) -> p n j", n=share),
                 )
 
+        weave_val(0, scalar_weave, 82)
+        weave_val(1, scalar_weave, 100)
         open_score(0, 0, 0)
         score_passes(0, 0, [(a, t) for a in range(PASSES) for t in range(PACK)])
         score(0, 1, 4)
@@ -329,35 +329,34 @@ def tile_list_splice_map_reading_kernel(
         score(1, 0, 0)
         score(1, 1, 2)
         offset(0, 1, 58)
-
-        weave_e(0, 1, [(scalar_weave, 512)], 66)
         own_codes(0, 4)
-        quantize_val(24)
-        quantize_e(0, 0, 28)
-        read_map(0, 0)
-        offset(1, 0, 62)
-        weave_e(1, 0, [(scalar_weave, 256)], 72)
+        quantize_val(0, 25)
+        quantize_val(1, 29)
+        offset(1, 0, 88)
         score(2, 0, 0)
-        quantize_e(0, 1, 37)
-
-        read_map(0, 1)
-        offset(1, 1, 66)
+        quantize_e(0, 0)
+        read_map(0, 0)
+        weave_e(0, 1, [(scalar_weave, 384), (vector_weave, 128)], 66)
+        offset(1, 1, 90)
         score(2, 1, 2)
+        weave_e(1, 0, [(scalar_weave, 256)], 72)
+        quantize_e(0, 1, None)
+        read_map(0, 1)
+        offset(2, 0, 92)
+        own_codes(1, 0)
+        offset(2, 1, 94)
+        own_codes(2, 2)
         finish(0)
-        quantize_e(1, 0, 41)
-        weave_e(1, 1, [(gpsimd_weave, 256)], 73)
-        offset(2, 0, 71)
+        quantize_e(1, 0)
+        weave_e(1, 1, [(vector_weave, 256)], 74)
         weave_e(2, 0, [(scalar_weave, 256)], 76)
-        own_codes(1, 4)
         read_map(1, 0)
-        quantize_e(1, 1, 45)
+        quantize_e(1, 1)
         read_map(1, 1)
-        offset(2, 1, 74)
-        own_codes(2, 6)
         finish(1)
-        quantize_e(2, 0, 49)
-        read_map(2, 0)
         weave_e(2, 1, [(vector_weave, 256)], 78)
+        quantize_e(2, 0)
+        read_map(2, 0)
         quantize_e(2, 1)
         read_map(2, 1)
         finish(2)

@@ -1,6 +1,7 @@
 from contextlib import ExitStack
 
 import concourse.mybir as mybir
+from concourse.masks import make_identity
 
 K, T, S, N = 1024, 2048, 1024, 512
 FLOPS = 2 * K * S * S + 2 * K * S * N + 2 * S * N * S + 2 * K * N * S
@@ -65,9 +66,12 @@ def tile_list_splice_map_reading_kernel(
             nc.vector.quantize_mx(out=codes[:].bitcast(FP8X4), scales=scales[:], in_=woven[:].rearrange("p c t -> p (c t)"))
             return codes, scales
 
+        def load_columns(window, words, a, columns):
+            nc.sync.dma_start(out=window[:, columns], in_=words[a].rearrange("p t i -> p (t i)").bitcast(I32)[:, columns])
+
         def load_words(words, a, name, kib):
             window = placed([P, T], I32, name, kib)
-            nc.sync.dma_start(out=window[:], in_=words[a].rearrange("p t i -> p (t i)").bitcast(I32))
+            load_columns(window, words, a, slice(0, T))
             return window
 
         def load_wv(a, kib, pieces):
@@ -99,16 +103,19 @@ def tile_list_splice_map_reading_kernel(
         nc.gpsimd.memset(v_scale_window[:, T // 2 :].bitcast(I32), 0)
         warm = keep.tile([P, 2], F32)
         nc.gpsimd.memset(warm[:], 0.0)
+        gain_rows = kept([P, PASS], F32, "gain_rows")
+        nc.vector.memset(gain_rows[:], 0.0)
+        identity = kept([P, P], F32, "identity")
+        make_identity(nc, identity[:])
         nc.vector.memset(moved_v2[:].bitcast(I32), 0)
         nc.vector.memset(moved_v[:].bitcast(I32), 0)
 
         list2 = keep.tile([P, S // LIST_ROWS], U16)
         nc.sync.dma_start(list2[:], offs2)
+        v2_windows = [placed([P, T], I32, "v2_window0", 16)]
+        load_columns(v2_windows[0], tab2_words, 0, slice(0, 1024))
         lists = keep.tile([P, S // LIST_ROWS], U16)
         nc.sync.dma_start(lists[:], offs)
-        gm_cols = keep.tile([P, PASSES, PACK], F32)
-        gv_cols = keep.tile([P, PASSES, PACK], F32)
-        nc.sync.dma_start(out=gv_cols[:], in_=gv.rearrange("(b p t) -> p b t", p=P, t=PACK))
         staged_scales = kept([P, S + N], U8, "staged_scales")
         nc.sync.dma_start(
             out=staged_scales[0:P:4, S:].bitcast(I32), in_=w4_scales.bitcast(I32).rearrange("a q c -> q a c")
@@ -121,9 +128,15 @@ def tile_list_splice_map_reading_kernel(
         nc.sync.dma_start(
             out=v_scale_window[0:P:4, :].bitcast(I32), in_=tab_scales.bitcast(I32).rearrange("a q t -> q a t")
         )
-        nc.sync.dma_start(out=gm_cols[:], in_=gm.rearrange("(b p t) -> p b t", p=P, t=PACK))
-        v2_windows = [load_words(tab2_words, 0, "v2_window0", 16)]
-        wv_raw.append(load_wv(1, 8, 2))
+        load_columns(v2_windows[0], tab2_words, 0, slice(1024, T))
+        wv_raw.append(load_wv(1, 8, 1))
+        for i, gain in enumerate((gv, gm)):
+            nc.sync.dma_start(out=gain_rows[PASSES * i : PASSES * (i + 1), :], in_=gain.rearrange("(b c) -> b c", b=PASSES))
+        turned = bank(7, [P, PACK, P])
+        for t in range(PACK):
+            nc.tensor.transpose(turned[:, t, :], gain_rows[:, t:PASS:PACK], identity[:])
+        gains = kept([P, PACK, 2 * PASSES], F32, "gains")
+        nc.scalar.copy(out=gains[:], in_=turned[:, :, : 2 * PASSES])
 
         def move_rows(moved, source):
             for d in range(4):
@@ -132,14 +145,14 @@ def tile_list_splice_map_reading_kernel(
                     in_=source[32 * d : 32 * d + 32 : 4, :].bitcast(I32),
                 )
 
-        v2_scales_listed = placed([P, S], U8, "v2_scales_listed", 24)
+        v2_scales_listed = placed([P, S], U8, "v2_scales_listed", 25)
         nc.vector.tensor_copy(out=v2_scales_listed[:], in_=v2_scale_window[:].indirect(list2[:]))
         nc.vector.tensor_copy(
             out=staged_scales[:, :S].rearrange("p (b t c) -> p b t c", b=PASSES, t=PACK),
             in_=v2_scales_listed[:].rearrange("p (b c t) -> p b t c", b=PASSES, t=PACK),
         )
         move_rows(moved_v2, staged_scales)
-        v2_windows.append(load_words(tab2_words, 1, "v2_window1", 24))
+        v2_windows.append(load_words(tab2_words, 1, "v2_window1", 25))
         v_scales_listed = kept([P, S], U8, "v_scales_listed")
         nc.vector.tensor_copy(out=v_scales_listed[:], in_=v_scale_window[:].indirect(lists[:]))
         move_rows(moved_v, v_scales_listed)
@@ -148,7 +161,8 @@ def tile_list_splice_map_reading_kernel(
         v2_codes = {}
 
         def gather_v2(a, b):
-            codes = kept([P, PACK, P], U32, f"v2_codes{a}_{b}")
+            name = f"v2_codes{a}_{b}"
+            codes = placed([P, PACK, P], U32, name, 108) if (a, b) == (0, 1) else kept([P, PACK, P], U32, name)
             nc.vector.tensor_copy(
                 out=codes[:].rearrange("p t c -> p c t"),
                 in_=v2_windows[a][:].bitcast(U32).indirect(list2[:, b * cols : (b + 1) * cols]),
@@ -169,7 +183,7 @@ def tile_list_splice_map_reading_kernel(
 
         val_acc = {(b, t): bank(PACK * b + t, [P, N]) for b in range(PASSES) for t in range(PACK)}
         for a in range(PASSES):
-            woven = kept([P, N, PACK], BF16, f"wv_woven{a}")
+            woven = placed([P, N, PACK], BF16, f"wv_woven{a}", 108 + 4 * a)
             for i, half in enumerate(wv_raw[a]):
                 width = half.shape[2]
                 weave(scalar_cast, woven[:, i * width : (i + 1) * width, :], half[:])
@@ -186,13 +200,13 @@ def tile_list_splice_map_reading_kernel(
         for b in range(PASSES):
             for t in range(PACK):
                 nc.scalar.activation(
-                    out=val_planes[:, b, t, :], in_=val_acc[b, t][:], func=ACT.Copy, scale=gv_cols[:, b, t : t + 1]
+                    out=val_planes[:, b, t, :], in_=val_acc[b, t][:], func=ACT.Copy, scale=gains[:, t, b : b + 1]
                 )
 
         v_windows = [load_words(tab_words, 0, "v_window0", 37), load_words(tab_words, 1, "v_window1", 0)]
-        load_prior(0, 0, 15)
-        load_prior(0, 1, 25)
-        w4_codes = placed([P, PASSES, 2 * N], U8, "w4_codes", 23)
+        load_prior(0, 0, 16)
+        load_prior(0, 1, 24)
+        w4_codes = placed([P, PASSES, 2 * N], U8, "w4_codes", 32)
         nc.sync.dma_start(out=w4_codes[:].bitcast(I32), in_=w4_words.bitcast(I32).rearrange("a p c -> p a c"))
 
         v_codes = {}
@@ -238,7 +252,7 @@ def tile_list_splice_map_reading_kernel(
                 nc.vector.scalar_tensor_tensor(
                     out=planes[:, t, :],
                     in0=e_acc[chunk, b][t],
-                    scalar=gm_cols[:, b, t : t + 1],
+                    scalar=gains[:, t, PASSES + b : PASSES + b + 1],
                     in1=prior_rows[chunk, b, t],
                     op0=ALU.mult,
                     op1=ALU.add,
@@ -292,10 +306,10 @@ def tile_list_splice_map_reading_kernel(
             open_y(chunk, first_bank)
             own_passes(chunk, [(a, tile) for tile in range(N // P) for a in range(PASSES)])
 
-        def read_map(chunk, b):
+        def read_map(chunk, b, tiles=range(N // P)):
             width = CHUNKS[chunk][1]
             share = HALF // width
-            for tile in range(N // P):
+            for tile in tiles:
                 y, i, n0 = y_acc[chunk][tile // share], tile % share, tile * P
                 nc.tensor.matmul_mx(
                     out=y[:, i * width : (i + 1) * width],
@@ -312,12 +326,15 @@ def tile_list_splice_map_reading_kernel(
             share = HALF // width
             for i in banks or range(len(y_acc[chunk])):
                 y = y_acc[chunk][i]
-                result = keep.tile([P, HALF], F32, name=f"result{chunk}_{i}")
-                nc.scalar.activation(out=result[:], in_=y[:], func=ACT.Silu)
-                nc.sync.dma_start(
-                    out=out_rows[:, share * i : share * (i + 1), j0 : j0 + width],
-                    in_=result[:].rearrange("p (n j) -> p n j", n=share),
-                )
+                last = chunk == len(CHUNKS) - 1 and i == len(y_acc[chunk]) - 1
+                tiles = 1 if last else share
+                for first in range(0, share, tiles):
+                    result = keep.tile([P, tiles, width], F32, name=f"result{chunk}_{i}_{first}")
+                    sums = y[:, first * width : (first + tiles) * width].rearrange("p (n j) -> p n j", n=tiles)
+                    nc.scalar.activation(out=result[:], in_=sums, func=ACT.Silu)
+                    tile = share * i + first
+                    queue = nc.scalar if last and first else nc.sync
+                    queue.dma_start(out=out_rows[:, tile : tile + tiles, j0 : j0 + width], in_=result[:])
 
         weave_val(0, scalar_weave, 82)
         weave_val(1, scalar_weave, 100)
@@ -330,13 +347,13 @@ def tile_list_splice_map_reading_kernel(
         score(1, 1, 2)
         offset(0, 1, 58)
         own_codes(0, 4)
-        quantize_val(0, 25)
-        quantize_val(1, 29)
+        quantize_val(0, 24)
+        quantize_val(1, 28)
         offset(1, 0, 88)
         score(2, 0, 0)
         quantize_e(0, 0)
         read_map(0, 0)
-        weave_e(0, 1, [(scalar_weave, 384), (vector_weave, 128)], 66)
+        weave_e(0, 1, [(scalar_weave, 512)], 66)
         offset(1, 1, 90)
         score(2, 1, 2)
         weave_e(1, 0, [(scalar_weave, 256)], 72)
@@ -348,15 +365,14 @@ def tile_list_splice_map_reading_kernel(
         own_codes(2, 2)
         finish(0)
         quantize_e(1, 0)
-        weave_e(1, 1, [(vector_weave, 256)], 74)
+        weave_e(1, 1, [(scalar_weave, 256)], 74)
         weave_e(2, 0, [(scalar_weave, 256)], 76)
-        read_map(1, 0)
         quantize_e(1, 1)
-        read_map(1, 1)
-        finish(1)
         weave_e(2, 1, [(vector_weave, 256)], 78)
         quantize_e(2, 0)
-        read_map(2, 0)
         quantize_e(2, 1)
-        read_map(2, 1)
-        finish(2)
+        for chunk in (1, 2):
+            for i in range(2):
+                for b in range(PASSES):
+                    read_map(chunk, b, (2 * i, 2 * i + 1))
+                finish(chunk, (i,))

@@ -39,7 +39,7 @@ def tile_list_splice_map_reading_kernel(
             return keep.tile(shape, dtype, name=name, align_bytes=64)
 
         def placed(shape, dtype, name, kib):
-            return shared.tile(shape, dtype, name=name, offset=kib * KIB, align_bytes=64)
+            return shared.tile(shape, dtype, name=name, offset=int(kib * KIB), align_bytes=64)
 
         def bank(index, shape):
             return psum.tile(shape, F32, name=f"bank{index}", tag=f"bank{index}")
@@ -95,7 +95,7 @@ def tile_list_splice_map_reading_kernel(
                 prior_rows[chunk, b, t0 + t] = rows[:, t, :]
 
         v2_scale_window = kept([P, T], U8, "v2_scale_window")
-        v_scale_window = placed([P, T], U8, "v_scale_window", 37)
+        v_scale_window = kept([P, T], U8, "v_scale_window")
         moved_v2 = kept([P, PASSES, S + N], U8, "moved_v2")
         moved_v = kept([P, PASSES, S], U8, "moved_v")
         nc.gpsimd.memset(v2_scale_window[:].bitcast(I32), 0)
@@ -110,10 +110,10 @@ def tile_list_splice_map_reading_kernel(
         nc.vector.memset(moved_v2[:].bitcast(I32), 0)
         nc.vector.memset(moved_v[:].bitcast(I32), 0)
 
+        v2_windows = [placed([P, T], I32, "v2_window0", 8)]
+        load_columns(v2_windows[0], tab2_words, 0, slice(0, 1024))
         list2 = keep.tile([P, S // LIST_ROWS], U16)
         nc.sync.dma_start(list2[:], offs2)
-        v2_windows = [placed([P, T], I32, "v2_window0", 16)]
-        load_columns(v2_windows[0], tab2_words, 0, slice(0, 1024))
         lists = keep.tile([P, S // LIST_ROWS], U16)
         nc.sync.dma_start(lists[:], offs)
         staged_scales = kept([P, S + N], U8, "staged_scales")
@@ -129,7 +129,7 @@ def tile_list_splice_map_reading_kernel(
             out=v_scale_window[0:P:4, :].bitcast(I32), in_=tab_scales.bitcast(I32).rearrange("a q t -> q a t")
         )
         load_columns(v2_windows[0], tab2_words, 0, slice(1024, T))
-        wv_raw.append(load_wv(1, 8, 1))
+        wv_raw.append(load_wv(1, 120, 1))
         for i, gain in enumerate((gv, gm)):
             nc.sync.dma_start(out=gain_rows[PASSES * i : PASSES * (i + 1), :], in_=gain.rearrange("(b c) -> b c", b=PASSES))
         turned = bank(7, [P, PACK, P])
@@ -145,14 +145,15 @@ def tile_list_splice_map_reading_kernel(
                     in_=source[32 * d : 32 * d + 32 : 4, :].bitcast(I32),
                 )
 
-        v2_scales_listed = placed([P, S], U8, "v2_scales_listed", 25)
+        v2_scales_listed = placed([P, S], U8, "v2_scales_listed", 25.5)
         nc.vector.tensor_copy(out=v2_scales_listed[:], in_=v2_scale_window[:].indirect(list2[:]))
         nc.vector.tensor_copy(
             out=staged_scales[:, :S].rearrange("p (b t c) -> p b t c", b=PASSES, t=PACK),
             in_=v2_scales_listed[:].rearrange("p (b c t) -> p b t c", b=PASSES, t=PACK),
         )
         move_rows(moved_v2, staged_scales)
-        v2_windows.append(load_words(tab2_words, 1, "v2_window1", 25))
+        v2_windows.append(load_words(tab2_words, 1, "v2_window1", 18))
+        v_windows = [load_words(tab_words, 0, "v_window0", 26)]
         v_scales_listed = kept([P, S], U8, "v_scales_listed")
         nc.vector.tensor_copy(out=v_scales_listed[:], in_=v_scale_window[:].indirect(lists[:]))
         move_rows(moved_v, v_scales_listed)
@@ -169,7 +170,7 @@ def tile_list_splice_map_reading_kernel(
             )
             v2_codes[a, b] = codes
 
-        def pass_v2(acc, a, b, t, codes, scales):
+        def pass_v2(acc, a, b, t, codes, scales, closes=True):
             first = b * PASS + t * P
             nc.tensor.matmul_mx(
                 out=acc,
@@ -178,7 +179,7 @@ def tile_list_splice_map_reading_kernel(
                 rhs=codes.bitcast(FP8X4),
                 rhs_scale=scales,
                 start=(a == 0),
-                stop=(a == PASSES - 1),
+                stop=(a == PASSES - 1 and closes),
             )
 
         val_acc = {(b, t): bank(PACK * b + t, [P, N]) for b in range(PASSES) for t in range(PACK)}
@@ -203,23 +204,29 @@ def tile_list_splice_map_reading_kernel(
                     out=val_planes[:, b, t, :], in_=val_acc[b, t][:], func=ACT.Copy, scale=gains[:, t, b : b + 1]
                 )
 
-        v_windows = [load_words(tab_words, 0, "v_window0", 37), load_words(tab_words, 1, "v_window1", 0)]
-        load_prior(0, 0, 16)
-        load_prior(0, 1, 24)
-        w4_codes = placed([P, PASSES, 2 * N], U8, "w4_codes", 32)
+        v_windows.append(load_words(tab_words, 1, "v_window1", 0))
+        load_prior(0, 0, 8, 0, 2)
+        load_prior(0, 0, 12, 2, 2)
+        load_prior(0, 1, 16, 0, 2)
+        w4_codes = placed([P, PASSES, 2 * N], U8, "w4_codes", 24)
         nc.sync.dma_start(out=w4_codes[:].bitcast(I32), in_=w4_words.bitcast(I32).rearrange("a p c -> p a c"))
+        load_prior(0, 1, 20, 2, 2)
 
         v_codes = {}
         for h in range(S // HALF):
             for a in range(PASSES):
                 codes = kept([P, HALF], U32, f"v_codes{a}_{h}")
-                nc.vector.tensor_copy(
-                    out=codes[:], in_=v_windows[a][:].bitcast(U32).indirect(lists[:, h * cols : (h + 1) * cols])
-                )
+                pieces = 2 if (a, h) == (1, 0) else 1
+                for i in range(pieces):
+                    first, step = (h * pieces + i) * cols // pieces, cols // pieces
+                    nc.vector.tensor_copy(
+                        out=codes[:, i * HALF // pieces : (i + 1) * HALF // pieces],
+                        in_=v_windows[a][:].bitcast(U32).indirect(lists[:, first : first + step]),
+                    )
                 v_codes[a, h] = codes
 
         for b in range(PASSES):
-            load_prior(1, b, 37 + 4 * b)
+            load_prior(1, b, 26 + 4 * b)
         for b in range(PASSES):
             load_prior(2, b, 4 * b)
 
@@ -339,16 +346,20 @@ def tile_list_splice_map_reading_kernel(
         weave_val(0, scalar_weave, 82)
         weave_val(1, scalar_weave, 100)
         open_score(0, 0, 0)
-        score_passes(0, 0, [(a, t) for a in range(PASSES) for t in range(PACK)])
+        score_passes(0, 0, [(0, t) for t in range(PACK)])
+        for first in (0, HALF // 2):
+            for t in range(PACK):
+                columns = e_acc[0, 0][t][:, first : first + HALF // 2]
+                pass_v2(columns, 1, 0, t, *v_operand(1, first, HALF // 2), closes=first > 0)
         score(0, 1, 4)
         offset(0, 0, 54)
         weave_e(0, 0, [(scalar_weave, 512)], 62)
         score(1, 0, 0)
         score(1, 1, 2)
         offset(0, 1, 58)
+        quantize_val(0, 16)
         own_codes(0, 4)
-        quantize_val(0, 24)
-        quantize_val(1, 28)
+        quantize_val(1, 20)
         offset(1, 0, 88)
         score(2, 0, 0)
         quantize_e(0, 0)

@@ -59,6 +59,11 @@ def tile_list_splice_map_reading_kernel(
         def vector_weave(woven, planes):
             weave(nc.vector.tensor_copy, woven, planes)
 
+        def gpsimd_weave(woven, planes):
+            nc.gpsimd.tensor_scalar(
+                out=woven, in0=planes.rearrange("p t c -> p c t"), scalar1=1.0, scalar2=0.0, op0=ALU.mult, op1=ALU.add
+            )
+
         def quantize(woven, name, kib=None):
             width = woven.shape[1]
             codes = kept([P, width], U32, f"{name}_codes") if kib is None else placed([P, width], U32, f"{name}_codes", kib)
@@ -343,8 +348,8 @@ def tile_list_splice_map_reading_kernel(
                     queue = nc.scalar if last and first else nc.sync
                     queue.dma_start(out=out_rows[:, tile : tile + tiles, j0 : j0 + width], in_=result[:])
 
-        weave_val(0, scalar_weave, 82)
-        weave_val(1, scalar_weave, 100)
+        weave_val(0, gpsimd_weave, 82)
+        weave_val(1, gpsimd_weave, 100)
         open_score(0, 0, 0)
         score_passes(0, 0, [(0, t) for t in range(PACK)])
         for first in (0, HALF // 2):

@@ -21,10 +21,13 @@ P = 128
 PACK = 4
 PASS = P * PACK
 PASSES = 2
+RUN = 8
+BLOCKS = P // RUN
 HALF = 512
+QUARTER = 256
 LIST_ROWS = 16
-CHUNKS = ((0, 512), (512, 256), (768, 256))
 KIB = 1024
+
 
 def tile_list_splice_map_reading_kernel(
     tc, tab_words, tab_scales, tab2_words, tab2_scales, offs, offs2, w4_words, w4_scales, wv, gm, gv, prior, out
@@ -35,29 +38,28 @@ def tile_list_splice_map_reading_kernel(
         shared = ctx.enter_context(tc.tile_pool(name="shared", bufs=1))
         psum = ctx.enter_context(tc.psum_pool(name="psum", bufs=1))
 
-        def kept(shape, dtype, name):
-            return keep.tile(shape, dtype, name=name, align_bytes=64)
-
-        def placed(shape, dtype, name, kib):
+        def sbuf(shape, dtype, name, kib=None):
+            if kib is None:
+                return keep.tile(shape, dtype, name=name, align_bytes=64)
             return shared.tile(shape, dtype, name=name, offset=int(kib * KIB), align_bytes=64)
 
         def bank(index, shape):
             return psum.tile(shape, F32, name=f"bank{index}", tag=f"bank{index}")
 
-        def scalar_cast(out, in_):
-            nc.scalar.activation(out=out, in_=in_, func=ACT.Copy)
-
-        def weave(copy, woven, planes):
+        def by_fours(copy, woven, planes):
             copy(
                 out=woven.rearrange("p (c i) t -> p c t i", i=PACK),
                 in_=planes.rearrange("p t (c i) -> p c t i", i=PACK),
             )
 
+        def scalar_cast(out, in_):
+            nc.scalar.activation(out=out, in_=in_, func=ACT.Copy)
+
         def scalar_weave(woven, planes):
-            weave(nc.scalar.copy, woven, planes)
+            by_fours(nc.scalar.copy, woven, planes)
 
         def vector_weave(woven, planes):
-            weave(nc.vector.tensor_copy, woven, planes)
+            by_fours(nc.vector.tensor_copy, woven, planes)
 
         def gpsimd_weave(woven, planes):
             nc.gpsimd.tensor_scalar(
@@ -66,62 +68,56 @@ def tile_list_splice_map_reading_kernel(
 
         def quantize(woven, name, kib=None):
             width = woven.shape[1]
-            codes = kept([P, width], U32, f"{name}_codes") if kib is None else placed([P, width], U32, f"{name}_codes", kib)
-            scales = kept([P, width], U8, f"{name}_scales")
+            codes = sbuf([P, width], U32, f"{name}_codes", kib)
+            scales = sbuf([P, width], U8, f"{name}_scales")
             nc.vector.quantize_mx(out=codes[:].bitcast(FP8X4), scales=scales[:], in_=woven[:].rearrange("p c t -> p (c t)"))
             return codes, scales
 
-        def load_columns(window, words, a, columns):
-            nc.sync.dma_start(out=window[:, columns], in_=words[a].rearrange("p t i -> p (t i)").bitcast(I32)[:, columns])
+        def load_columns(queue, window, words, a, columns):
+            queue.dma_start(out=window[:, columns], in_=words[a].rearrange("p t i -> p (t i)").bitcast(I32)[:, columns])
 
         def load_words(words, a, name, kib):
-            window = placed([P, T], I32, name, kib)
-            load_columns(window, words, a, slice(0, T))
+            window = sbuf([P, T], I32, name, kib)
+            load_columns(nc.sync, window, words, a, slice(0, T))
             return window
 
-        def load_wv(a, kib, pieces):
-            rows = wv[a * PASS : (a + 1) * PASS, :].rearrange("(p t) n -> p t n", t=PACK)
-            halves = []
-            width = N // pieces
-            for i in range(pieces):
-                half = placed([P, PACK, width], F32, f"wv_raw{a}_{i}", kib + 8 // pieces * i)
-                nc.sync.dma_start(out=half[:], in_=rows[:, :, i * width : (i + 1) * width])
-                halves.append(half)
-            return halves
+        def load_wv(a, kib):
+            raw = sbuf([P, PACK, N], F32, f"wv_raw{a}", kib)
+            nc.sync.dma_start(out=raw[:], in_=wv[a * PASS : (a + 1) * PASS, :].rearrange("(p t) n -> p t n", t=PACK))
+            return raw
 
         prior_rows = {}
 
-        def load_prior(chunk, b, kib, t0=0, planes=PACK):
-            j0, width = CHUNKS[chunk]
-            rows = placed([P, planes, width], F32, f"prior{chunk}_{b}_{t0}", kib)
-            source = prior[b * PASS : (b + 1) * PASS, j0 : j0 + width].rearrange("(p t) j -> p t j", t=PACK)
-            nc.sync.dma_start(out=rows[:], in_=source[:, t0 : t0 + planes, :])
-            for t in range(planes):
-                prior_rows[chunk, b, t0 + t] = rows[:, t, :]
+        def load_prior(h, b, kib):
+            source = prior[b * PASS : (b + 1) * PASS, h * HALF : (h + 1) * HALF].rearrange("(q t r) j -> t q r j", t=PACK, r=RUN)
+            for t in range(PACK):
+                rows = sbuf([P, HALF], F32, f"prior{h}_{b}_{t}", kib + 2 * t)
+                nc.sync.dma_start(out=rows[:], in_=source[t])
+                prior_rows[h, b, t] = rows
 
-        v2_scale_window = kept([P, T], U8, "v2_scale_window")
-        v_scale_window = kept([P, T], U8, "v_scale_window")
-        moved_v2 = kept([P, PASSES, S + N], U8, "moved_v2")
-        moved_v = kept([P, PASSES, S], U8, "moved_v")
+        v2_scale_window = sbuf([P, T], U8, "v2_scale_window")
+        v_scale_window = sbuf([P, T], U8, "v_scale_window")
+        moved_v2 = sbuf([P, PASSES, S + N], U8, "moved_v2")
+        moved_v = sbuf([P, PASSES, S], U8, "moved_v")
         nc.gpsimd.memset(v2_scale_window[:].bitcast(I32), 0)
         nc.vector.memset(v_scale_window[:, : T // 2].bitcast(I32), 0)
         nc.gpsimd.memset(v_scale_window[:, T // 2 :].bitcast(I32), 0)
         warm = keep.tile([P, 2], F32)
         nc.gpsimd.memset(warm[:], 0.0)
-        gain_rows = kept([P, PASS], F32, "gain_rows")
+        gain_rows = sbuf([P, PASS], F32, "gain_rows")
         nc.vector.memset(gain_rows[:], 0.0)
-        identity = kept([P, P], F32, "identity")
+        identity = sbuf([P, P], F32, "identity")
         make_identity(nc, identity[:])
         nc.vector.memset(moved_v2[:].bitcast(I32), 0)
         nc.vector.memset(moved_v[:].bitcast(I32), 0)
 
-        v2_windows = [placed([P, T], I32, "v2_window0", 8)]
-        load_columns(v2_windows[0], tab2_words, 0, slice(0, 1024))
+        v2_windows = [sbuf([P, T], I32, "v2_window0", 8)]
+        load_columns(nc.scalar, v2_windows[0], tab2_words, 0, slice(0, T // 2))
         list2 = keep.tile([P, S // LIST_ROWS], U16)
         nc.sync.dma_start(list2[:], offs2)
         lists = keep.tile([P, S // LIST_ROWS], U16)
         nc.sync.dma_start(lists[:], offs)
-        staged_scales = kept([P, S + N], U8, "staged_scales")
+        staged_scales = sbuf([P, S + N], U8, "staged_scales")
         nc.sync.dma_start(
             out=staged_scales[0:P:4, S:].bitcast(I32), in_=w4_scales.bitcast(I32).rearrange("a q c -> q a c")
         )
@@ -129,18 +125,27 @@ def tile_list_splice_map_reading_kernel(
             out=v2_scale_window[0:P:4, :].bitcast(I32), in_=tab2_scales.bitcast(I32).rearrange("a q t -> q a t")
         )
         nc.scalar.activation(out=warm[:, 1:2], in_=warm[:, 0:1], func=ACT.Silu)
-        wv_raw = [load_wv(0, 0, 1)]
+        wv_raw = [load_wv(0, 0)]
         nc.sync.dma_start(
             out=v_scale_window[0:P:4, :].bitcast(I32), in_=tab_scales.bitcast(I32).rearrange("a q t -> q a t")
         )
-        load_columns(v2_windows[0], tab2_words, 0, slice(1024, T))
-        wv_raw.append(load_wv(1, 120, 1))
         for i, gain in enumerate((gv, gm)):
             nc.sync.dma_start(out=gain_rows[PASSES * i : PASSES * (i + 1), :], in_=gain.rearrange("(b c) -> b c", b=PASSES))
+        load_columns(nc.sync, v2_windows[0], tab2_words, 0, slice(T // 2, T))
+        wv_raw.append(load_wv(1, 120))
+        gain_planes = sbuf([P, PACK, P], F32, "gain_planes")
+        nc.gpsimd.tensor_scalar(
+            out=gain_planes[:].rearrange("p t (q r) -> p t q r", r=RUN),
+            in0=gain_rows[:].rearrange("p (q t r) -> p t q r", t=PACK, r=RUN),
+            scalar1=1.0,
+            scalar2=0.0,
+            op0=ALU.mult,
+            op1=ALU.add,
+        )
         turned = bank(7, [P, PACK, P])
         for t in range(PACK):
-            nc.tensor.transpose(turned[:, t, :], gain_rows[:, t:PASS:PACK], identity[:])
-        gains = kept([P, PACK, 2 * PASSES], F32, "gains")
+            nc.tensor.transpose(turned[:, t, :], gain_planes[:, t, :], identity[:])
+        gains = sbuf([P, PACK, 2 * PASSES], F32, "gains")
         nc.scalar.copy(out=gains[:], in_=turned[:, :, : 2 * PASSES])
 
         def move_rows(moved, source):
@@ -150,27 +155,26 @@ def tile_list_splice_map_reading_kernel(
                     in_=source[32 * d : 32 * d + 32 : 4, :].bitcast(I32),
                 )
 
-        v2_scales_listed = placed([P, S], U8, "v2_scales_listed", 25.5)
+        v2_scales_listed = sbuf([P, S], U8, "v2_scales_listed", 25.5)
         nc.vector.tensor_copy(out=v2_scales_listed[:], in_=v2_scale_window[:].indirect(list2[:]))
         nc.vector.tensor_copy(
-            out=staged_scales[:, :S].rearrange("p (b t c) -> p b t c", b=PASSES, t=PACK),
-            in_=v2_scales_listed[:].rearrange("p (b c t) -> p b t c", b=PASSES, t=PACK),
+            out=staged_scales[:, :S].bitcast(I32).rearrange("p (b t q w) -> p b t q w", b=PASSES, t=PACK, q=BLOCKS),
+            in_=v2_scales_listed[:].bitcast(I32).rearrange("p (b q t w) -> p b t q w", b=PASSES, t=PACK, q=BLOCKS),
         )
         move_rows(moved_v2, staged_scales)
         v2_windows.append(load_words(tab2_words, 1, "v2_window1", 18))
         v_windows = [load_words(tab_words, 0, "v_window0", 26)]
-        v_scales_listed = kept([P, S], U8, "v_scales_listed")
+        v_scales_listed = sbuf([P, S], U8, "v_scales_listed")
         nc.vector.tensor_copy(out=v_scales_listed[:], in_=v_scale_window[:].indirect(lists[:]))
         move_rows(moved_v, v_scales_listed)
 
         cols = HALF // LIST_ROWS
         v2_codes = {}
 
-        def gather_v2(a, b):
-            name = f"v2_codes{a}_{b}"
-            codes = placed([P, PACK, P], U32, name, 108) if (a, b) == (0, 1) else kept([P, PACK, P], U32, name)
+        def gather_v2(a, b, kib=None):
+            codes = sbuf([P, PACK, P], U32, f"v2_codes{a}_{b}", kib)
             nc.vector.tensor_copy(
-                out=codes[:].rearrange("p t c -> p c t"),
+                out=codes[:].rearrange("p t (q r) -> p q t r", r=RUN),
                 in_=v2_windows[a][:].bitcast(U32).indirect(list2[:, b * cols : (b + 1) * cols]),
             )
             v2_codes[a, b] = codes
@@ -189,38 +193,35 @@ def tile_list_splice_map_reading_kernel(
 
         val_acc = {(b, t): bank(PACK * b + t, [P, N]) for b in range(PASSES) for t in range(PACK)}
         for a in range(PASSES):
-            woven = placed([P, N, PACK], BF16, f"wv_woven{a}", 108 + 4 * a)
-            for i, half in enumerate(wv_raw[a]):
-                width = half.shape[2]
-                weave(scalar_cast, woven[:, i * width : (i + 1) * width, :], half[:])
+            woven = sbuf([P, N, PACK], BF16, f"wv_woven{a}", 108 + 4 * a)
+            by_fours(scalar_cast, woven[:], wv_raw[a][:])
             if a == 0:
                 gather_v2(a, 0)
-            codes, scales = quantize(woven, f"wv{a}", 80 + 2 * a)
+            codes, scales = quantize(woven, f"wv{a}")
             if a == 1:
                 gather_v2(a, 0)
-            gather_v2(a, 1)
+            gather_v2(a, 1, 108 if a == 0 else None)
             for b in range(PASSES):
                 for t in range(PACK):
                     pass_v2(val_acc[b, t][:], a, b, t, codes[:], scales[:])
-        val_planes = placed([P, PASSES, PACK, N], BF16, "val_planes", 45)
+        val_woven = []
         for b in range(PASSES):
+            planes = sbuf([P, PACK, N], BF16, f"val_planes{b}")
             for t in range(PACK):
-                nc.scalar.activation(
-                    out=val_planes[:, b, t, :], in_=val_acc[b, t][:], func=ACT.Copy, scale=gains[:, t, b : b + 1]
-                )
+                nc.scalar.activation(out=planes[:, t, :], in_=val_acc[b, t][:], func=ACT.Copy, scale=gains[:, t, b : b + 1])
+            val_woven.append(sbuf([P, N, PACK], BF16, f"val_woven{b}"))
+            gpsimd_weave(val_woven[b][:], planes[:])
 
         v_windows.append(load_words(tab_words, 1, "v_window1", 0))
-        load_prior(0, 0, 8, 0, 2)
-        load_prior(0, 0, 12, 2, 2)
-        load_prior(0, 1, 16, 0, 2)
-        w4_codes = placed([P, PASSES, 2 * N], U8, "w4_codes", 24)
+        load_prior(0, 0, 8)
+        w4_codes = sbuf([P, PASSES, 2 * N], U8, "w4_codes", 120)
         nc.sync.dma_start(out=w4_codes[:].bitcast(I32), in_=w4_words.bitcast(I32).rearrange("a p c -> p a c"))
-        load_prior(0, 1, 20, 2, 2)
+        load_prior(0, 1, 18)
 
         v_codes = {}
         for h in range(S // HALF):
             for a in range(PASSES):
-                codes = kept([P, HALF], U32, f"v_codes{a}_{h}")
+                codes = sbuf([P, HALF], U32, f"v_codes{a}_{h}")
                 pieces = 2 if (a, h) == (1, 0) else 1
                 for i in range(pieces):
                     first, step = (h * pieces + i) * cols // pieces, cols // pieces
@@ -230,10 +231,8 @@ def tile_list_splice_map_reading_kernel(
                     )
                 v_codes[a, h] = codes
 
-        for b in range(PASSES):
-            load_prior(1, b, 26 + 4 * b)
-        for b in range(PASSES):
-            load_prior(2, b, 4 * b)
+        load_prior(1, 0, 26)
+        load_prior(1, 1, 0)
 
         def v_operand(a, j0, width):
             h, first = divmod(j0, HALF)
@@ -242,153 +241,129 @@ def tile_list_splice_map_reading_kernel(
         out_rows = out.rearrange("(n p) j -> p n j", p=P)
         e_acc, e_planes, e_woven, e_mx, val_mx, y_acc = {}, {}, {}, {}, {}, {}
 
-        def open_score(chunk, b, first_bank):
-            width = CHUNKS[chunk][1]
+        def open_score(unit, first_bank):
+            width = unit[1]
             share = HALF // width
             tiles = [bank(first_bank + i, [P, share, width]) for i in range(PACK // share)]
-            e_acc[chunk, b] = [tiles[t // share][:, t % share, :] for t in range(PACK)]
+            e_acc[unit] = [tiles[t // share][:, t % share, :] for t in range(PACK)]
 
-        def score_passes(chunk, b, order):
-            j0, width = CHUNKS[chunk]
-            for a, t in order:
-                pass_v2(e_acc[chunk, b][t], a, b, t, *v_operand(a, j0, width))
+        def score(unit, first_bank):
+            j0, width, b = unit
+            open_score(unit, first_bank)
+            for t in range(PACK):
+                for a in range(PASSES):
+                    pass_v2(e_acc[unit][t], a, b, t, *v_operand(a, j0, width))
 
-        def score(chunk, b, first_bank):
-            open_score(chunk, b, first_bank)
-            score_passes(chunk, b, [(a, t) for t in range(PACK) for a in range(PASSES)])
-
-        def offset(chunk, b, kib):
-            width = CHUNKS[chunk][1]
-            planes = placed([P, PACK, width], BF16, f"e_planes{chunk}_{b}", kib)
+        def offset(unit):
+            j0, width, b = unit
+            h, first = divmod(j0, HALF)
+            planes = sbuf([P, PACK, width], BF16, f"e_planes{j0}_{b}")
             for t in range(PACK):
                 nc.vector.scalar_tensor_tensor(
                     out=planes[:, t, :],
-                    in0=e_acc[chunk, b][t],
+                    in0=e_acc[unit][t],
                     scalar=gains[:, t, PASSES + b : PASSES + b + 1],
-                    in1=prior_rows[chunk, b, t],
+                    in1=prior_rows[h, b, t][:, first : first + width],
                     op0=ALU.mult,
                     op1=ALU.add,
                 )
-            e_planes[chunk, b] = planes
+            e_planes[unit] = planes
 
-        def weave_e(chunk, b, engine_weave, kib):
-            width = CHUNKS[chunk][1]
-            woven = placed([P, width, PACK], BF16, f"e_woven{chunk}_{b}", kib)
-            first = 0
-            for one_weave, columns in engine_weave:
-                one_weave(woven[:, first : first + columns, :], e_planes[chunk, b][:, :, first : first + columns])
-                first = first + columns
-            e_woven[chunk, b] = woven
+        def weave_e(unit, engine_weave):
+            j0, width, b = unit
+            e_woven[unit] = sbuf([P, width, PACK], BF16, f"e_woven{j0}_{b}")
+            engine_weave(e_woven[unit][:], e_planes[unit][:])
 
-        def quantize_e(chunk, b, kib=None):
-            e_mx[chunk, b] = quantize(e_woven[chunk, b], f"e{chunk}_{b}", kib)
+        def quantize_e(unit, kib=None):
+            e_mx[unit] = quantize(e_woven[unit], f"e{unit[0]}_{unit[2]}", kib)
 
-        val_woven = {}
-
-        def weave_val(b, engine_weave, kib):
-            val_woven[b] = placed([P, N, PACK], BF16, f"val_woven{b}", kib)
-            engine_weave(val_woven[b][:], val_planes[:, b])
-
-        def quantize_val(b, kib):
-            val_mx[b] = quantize(val_woven[b], f"val{b}", kib)
-
-        def open_y(chunk, first_bank):
-            share = HALF // CHUNKS[chunk][1]
-            y_acc[chunk] = [bank(first_bank + i, [P, HALF]) for i in range(N // P // share)]
-
-        def own_passes(chunk, order):
-            j0, width = CHUNKS[chunk]
+        def own_codes(j0, width, first_bank):
             share = HALF // width
+            y_acc[j0] = [bank(first_bank + i, [P, HALF]) for i in range(N // P // share)]
             step = width if width == HALF else P
-            for a, tile in order:
-                y, i, n0 = y_acc[chunk][tile // share], tile % share, tile * P
-                for c0 in range(0, width, step):
-                    codes, scales = v_operand(a, j0 + c0, step)
-                    nc.tensor.matmul_mx(
-                        out=y[:, i * width + c0 : i * width + c0 + step],
-                        lhsT=w4_codes[:, a, 2 * n0 : 2 * (n0 + P)].bitcast(FP4X4),
-                        lhsT_scale=moved_v2[:, a, S + n0 : S + n0 + P],
-                        rhs=codes.bitcast(FP8X4),
-                        rhs_scale=scales,
-                        start=(i == 0 and a == 0 and c0 == 0),
-                        stop=False,
-                    )
+            for tile in range(N // P):
+                y, i, n0 = y_acc[j0][tile // share], tile % share, tile * P
+                for a in range(PASSES):
+                    for c0 in range(0, width, step):
+                        codes, scales = v_operand(a, j0 + c0, step)
+                        nc.tensor.matmul_mx(
+                            out=y[:, i * width + c0 : i * width + c0 + step],
+                            lhsT=w4_codes[:, a, 2 * n0 : 2 * (n0 + P)].bitcast(FP4X4),
+                            lhsT_scale=moved_v2[:, a, S + n0 : S + n0 + P],
+                            rhs=codes.bitcast(FP8X4),
+                            rhs_scale=scales,
+                            start=(i == 0 and a == 0 and c0 == 0),
+                            stop=False,
+                        )
 
-        def own_codes(chunk, first_bank):
-            open_y(chunk, first_bank)
-            own_passes(chunk, [(a, tile) for tile in range(N // P) for a in range(PASSES)])
-
-        def read_map(chunk, b, tiles=range(N // P)):
-            width = CHUNKS[chunk][1]
+        def read_map(j0, width, unit, tiles=range(N // P)):
             share = HALF // width
+            first, b = j0 - unit[0], unit[2]
             for tile in tiles:
-                y, i, n0 = y_acc[chunk][tile // share], tile % share, tile * P
+                y, i, n0 = y_acc[j0][tile // share], tile % share, tile * P
                 nc.tensor.matmul_mx(
                     out=y[:, i * width : (i + 1) * width],
                     lhsT=val_mx[b][0][:, n0 : n0 + P].bitcast(FP8X4),
                     lhsT_scale=val_mx[b][1][:, n0 : n0 + P],
-                    rhs=e_mx[chunk, b][0][:].bitcast(FP8X4),
-                    rhs_scale=e_mx[chunk, b][1][:],
+                    rhs=e_mx[unit][0][:, first : first + width].bitcast(FP8X4),
+                    rhs_scale=e_mx[unit][1][:, first : first + width],
                     start=False,
                     stop=(b == PASSES - 1 and i == share - 1),
                 )
 
-        def finish(chunk, banks=None):
-            j0, width = CHUNKS[chunk]
+        def finish(j0, width, banks):
             share = HALF // width
-            for i in banks or range(len(y_acc[chunk])):
-                y = y_acc[chunk][i]
-                last = chunk == len(CHUNKS) - 1 and i == len(y_acc[chunk]) - 1
+            for i in banks:
+                y = y_acc[j0][i]
+                last = j0 + width == S and i == len(y_acc[j0]) - 1
                 tiles = 1 if last else share
                 for first in range(0, share, tiles):
-                    result = keep.tile([P, tiles, width], F32, name=f"result{chunk}_{i}_{first}")
+                    result = keep.tile([P, tiles, width], F32, name=f"result{j0}_{i}_{first}")
                     sums = y[:, first * width : (first + tiles) * width].rearrange("p (n j) -> p n j", n=tiles)
                     nc.scalar.activation(out=result[:], in_=sums, func=ACT.Silu)
                     tile = share * i + first
                     queue = nc.scalar if last and first else nc.sync
                     queue.dma_start(out=out_rows[:, tile : tile + tiles, j0 : j0 + width], in_=result[:])
 
-        weave_val(0, gpsimd_weave, 82)
-        weave_val(1, gpsimd_weave, 100)
-        open_score(0, 0, 0)
-        score_passes(0, 0, [(0, t) for t in range(PACK)])
-        for first in (0, HALF // 2):
+        left0, left1, right0 = (0, HALF, 0), (0, HALF, 1), (HALF, HALF, 0)
+        third1, fourth1 = (HALF, QUARTER, 1), (HALF + QUARTER, QUARTER, 1)
+
+        open_score(left0, 0)
+        for t in range(PACK):
+            pass_v2(e_acc[left0][t], 0, 0, t, *v_operand(0, 0, HALF))
+        for first in (0, QUARTER):
             for t in range(PACK):
-                columns = e_acc[0, 0][t][:, first : first + HALF // 2]
-                pass_v2(columns, 1, 0, t, *v_operand(1, first, HALF // 2), closes=first > 0)
-        score(0, 1, 4)
-        offset(0, 0, 54)
-        weave_e(0, 0, [(scalar_weave, 512)], 62)
-        score(1, 0, 0)
-        score(1, 1, 2)
-        offset(0, 1, 58)
-        quantize_val(0, 16)
-        own_codes(0, 4)
-        quantize_val(1, 20)
-        offset(1, 0, 88)
-        score(2, 0, 0)
-        quantize_e(0, 0)
-        read_map(0, 0)
-        weave_e(0, 1, [(scalar_weave, 512)], 66)
-        offset(1, 1, 90)
-        score(2, 1, 2)
-        weave_e(1, 0, [(scalar_weave, 256)], 72)
-        quantize_e(0, 1, None)
-        read_map(0, 1)
-        offset(2, 0, 92)
-        own_codes(1, 0)
-        offset(2, 1, 94)
-        own_codes(2, 2)
-        finish(0)
-        quantize_e(1, 0)
-        weave_e(1, 1, [(scalar_weave, 256)], 74)
-        weave_e(2, 0, [(scalar_weave, 256)], 76)
-        quantize_e(1, 1)
-        weave_e(2, 1, [(vector_weave, 256)], 78)
-        quantize_e(2, 0)
-        quantize_e(2, 1)
-        for chunk in (1, 2):
+                columns = e_acc[left0][t][:, first : first + QUARTER]
+                pass_v2(columns, 1, 0, t, *v_operand(1, first, QUARTER), closes=first > 0)
+        score(left1, 4)
+        offset(left0)
+        weave_e(left0, scalar_weave)
+        score(right0, 0)
+        offset(left1)
+        weave_e(left1, scalar_weave)
+        own_codes(0, HALF, 4)
+        val_mx[0] = quantize(val_woven[0], "val0", 20)
+        quantize_e(left0)
+        read_map(0, HALF, left0)
+        offset(right0)
+        weave_e(right0, scalar_weave)
+        score(third1, 0)
+        score(fourth1, 2)
+        val_mx[1] = quantize(val_woven[1], "val1", 28)
+        quantize_e(left1, 30)
+        read_map(0, HALF, left1)
+        finish(0, HALF, range(4))
+        offset(third1)
+        weave_e(third1, gpsimd_weave)
+        own_codes(HALF, QUARTER, 0)
+        offset(fourth1)
+        own_codes(HALF + QUARTER, QUARTER, 2)
+        quantize_e(right0, 2)
+        quantize_e(third1)
+        weave_e(fourth1, vector_weave)
+        quantize_e(fourth1)
+        for j0, unit in ((HALF, third1), (HALF + QUARTER, fourth1)):
             for i in range(2):
-                for b in range(PASSES):
-                    read_map(chunk, b, (2 * i, 2 * i + 1))
-                finish(chunk, (i,))
+                read_map(j0, QUARTER, right0, (2 * i, 2 * i + 1))
+                read_map(j0, QUARTER, unit, (2 * i, 2 * i + 1))
+                finish(j0, QUARTER, (i,))

@@ -21,8 +21,6 @@ P = 128
 PACK = 4
 PASS = P * PACK
 PASSES = 2
-RUN = 8
-BLOCKS = P // RUN
 HALF = 512
 QUARTER = 256
 LIST_ROWS = 16
@@ -88,12 +86,16 @@ def tile_list_splice_map_reading_kernel(
 
         prior_rows = {}
 
-        def load_prior(h, b, kib):
-            source = prior[b * PASS : (b + 1) * PASS, h * HALF : (h + 1) * HALF].rearrange("(q t r) j -> t q r j", t=PACK, r=RUN)
-            for t in range(PACK):
-                rows = sbuf([P, HALF], F32, f"prior{h}_{b}_{t}", kib + 2 * t)
-                nc.sync.dma_start(out=rows[:], in_=source[t])
-                prior_rows[h, b, t] = rows
+        def load_prior(unit, kib, t0=0, planes=PACK):
+            j0, width, b = unit
+            rows = sbuf([P, planes, width], F32, f"prior{j0}_{b}_{t0}", kib)
+            source = prior[b * PASS : (b + 1) * PASS, j0 : j0 + width].rearrange("(p t) j -> p t j", t=PACK)
+            nc.sync.dma_start(out=rows[:], in_=source[:, t0 : t0 + planes, :])
+            for t in range(planes):
+                prior_rows[unit, t0 + t] = rows[:, t, :]
+
+        left0, left1, right0 = (0, HALF, 0), (0, HALF, 1), (HALF, HALF, 0)
+        third1, fourth1 = (HALF, QUARTER, 1), (HALF + QUARTER, QUARTER, 1)
 
         v2_scale_window = sbuf([P, T], U8, "v2_scale_window")
         v_scale_window = sbuf([P, T], U8, "v_scale_window")
@@ -125,26 +127,17 @@ def tile_list_splice_map_reading_kernel(
             out=v2_scale_window[0:P:4, :].bitcast(I32), in_=tab2_scales.bitcast(I32).rearrange("a q t -> q a t")
         )
         nc.scalar.activation(out=warm[:, 1:2], in_=warm[:, 0:1], func=ACT.Silu)
-        wv_raw = [load_wv(0, 0)]
+        wv_raw = [load_wv(0, 40)]
         nc.sync.dma_start(
             out=v_scale_window[0:P:4, :].bitcast(I32), in_=tab_scales.bitcast(I32).rearrange("a q t -> q a t")
         )
         for i, gain in enumerate((gv, gm)):
             nc.sync.dma_start(out=gain_rows[PASSES * i : PASSES * (i + 1), :], in_=gain.rearrange("(b c) -> b c", b=PASSES))
         load_columns(nc.sync, v2_windows[0], tab2_words, 0, slice(T // 2, T))
-        wv_raw.append(load_wv(1, 120))
-        gain_planes = sbuf([P, PACK, P], F32, "gain_planes")
-        nc.gpsimd.tensor_scalar(
-            out=gain_planes[:].rearrange("p t (q r) -> p t q r", r=RUN),
-            in0=gain_rows[:].rearrange("p (q t r) -> p t q r", t=PACK, r=RUN),
-            scalar1=1.0,
-            scalar2=0.0,
-            op0=ALU.mult,
-            op1=ALU.add,
-        )
+        wv_raw.append(load_wv(1, 48))
         turned = bank(7, [P, PACK, P])
         for t in range(PACK):
-            nc.tensor.transpose(turned[:, t, :], gain_planes[:, t, :], identity[:])
+            nc.tensor.transpose(turned[:, t, :], gain_rows[:, t:PASS:PACK], identity[:])
         gains = sbuf([P, PACK, 2 * PASSES], F32, "gains")
         nc.scalar.copy(out=gains[:], in_=turned[:, :, : 2 * PASSES])
 
@@ -158,8 +151,8 @@ def tile_list_splice_map_reading_kernel(
         v2_scales_listed = sbuf([P, S], U8, "v2_scales_listed", 25.5)
         nc.vector.tensor_copy(out=v2_scales_listed[:], in_=v2_scale_window[:].indirect(list2[:]))
         nc.vector.tensor_copy(
-            out=staged_scales[:, :S].bitcast(I32).rearrange("p (b t q w) -> p b t q w", b=PASSES, t=PACK, q=BLOCKS),
-            in_=v2_scales_listed[:].bitcast(I32).rearrange("p (b q t w) -> p b t q w", b=PASSES, t=PACK, q=BLOCKS),
+            out=staged_scales[:, :S].rearrange("p (b t c) -> p b t c", b=PASSES, t=PACK),
+            in_=v2_scales_listed[:].rearrange("p (b c t) -> p b t c", b=PASSES, t=PACK),
         )
         move_rows(moved_v2, staged_scales)
         v2_windows.append(load_words(tab2_words, 1, "v2_window1", 18))
@@ -174,7 +167,7 @@ def tile_list_splice_map_reading_kernel(
         def gather_v2(a, b, kib=None):
             codes = sbuf([P, PACK, P], U32, f"v2_codes{a}_{b}", kib)
             nc.vector.tensor_copy(
-                out=codes[:].rearrange("p t (q r) -> p q t r", r=RUN),
+                out=codes[:].rearrange("p t c -> p c t"),
                 in_=v2_windows[a][:].bitcast(U32).indirect(list2[:, b * cols : (b + 1) * cols]),
             )
             v2_codes[a, b] = codes
@@ -193,14 +186,14 @@ def tile_list_splice_map_reading_kernel(
 
         val_acc = {(b, t): bank(PACK * b + t, [P, N]) for b in range(PASSES) for t in range(PACK)}
         for a in range(PASSES):
-            woven = sbuf([P, N, PACK], BF16, f"wv_woven{a}", 108 + 4 * a)
+            woven = sbuf([P, N, PACK], BF16, f"wv_woven{a}")
             by_fours(scalar_cast, woven[:], wv_raw[a][:])
             if a == 0:
                 gather_v2(a, 0)
             codes, scales = quantize(woven, f"wv{a}")
             if a == 1:
-                gather_v2(a, 0)
-            gather_v2(a, 1, 108 if a == 0 else None)
+                gather_v2(a, 0, 48)
+            gather_v2(a, 1, 46 if a == 0 else 50)
             for b in range(PASSES):
                 for t in range(PACK):
                     pass_v2(val_acc[b, t][:], a, b, t, codes[:], scales[:])
@@ -212,11 +205,13 @@ def tile_list_splice_map_reading_kernel(
             val_woven.append(sbuf([P, N, PACK], BF16, f"val_woven{b}"))
             gpsimd_weave(val_woven[b][:], planes[:])
 
-        v_windows.append(load_words(tab_words, 1, "v_window1", 0))
-        load_prior(0, 0, 8)
-        w4_codes = sbuf([P, PASSES, 2 * N], U8, "w4_codes", 120)
+        v_windows.append(load_words(tab_words, 1, "v_window1", 34))
+        load_prior(left0, 8, 0, 2)
+        load_prior(left0, 12, 2, 2)
+        w4_codes = sbuf([P, PASSES, 2 * N], U8, "w4_codes", 52)
         nc.sync.dma_start(out=w4_codes[:].bitcast(I32), in_=w4_words.bitcast(I32).rearrange("a p c -> p a c"))
-        load_prior(0, 1, 18)
+        load_prior(left1, 18, 0, 2)
+        load_prior(left1, 22, 2, 2)
 
         v_codes = {}
         for h in range(S // HALF):
@@ -231,8 +226,10 @@ def tile_list_splice_map_reading_kernel(
                     )
                 v_codes[a, h] = codes
 
-        load_prior(1, 0, 26)
-        load_prior(1, 1, 0)
+        load_prior(right0, 26, 0, 2)
+        load_prior(right0, 30, 2, 2)
+        load_prior(third1, 34)
+        load_prior(fourth1, 38)
 
         def v_operand(a, j0, width):
             h, first = divmod(j0, HALF)
@@ -256,14 +253,13 @@ def tile_list_splice_map_reading_kernel(
 
         def offset(unit):
             j0, width, b = unit
-            h, first = divmod(j0, HALF)
             planes = sbuf([P, PACK, width], BF16, f"e_planes{j0}_{b}")
             for t in range(PACK):
                 nc.vector.scalar_tensor_tensor(
                     out=planes[:, t, :],
                     in0=e_acc[unit][t],
                     scalar=gains[:, t, PASSES + b : PASSES + b + 1],
-                    in1=prior_rows[h, b, t][:, first : first + width],
+                    in1=prior_rows[unit, t],
                     op0=ALU.mult,
                     op1=ALU.add,
                 )
@@ -325,9 +321,6 @@ def tile_list_splice_map_reading_kernel(
                     queue = nc.scalar if last and first else nc.sync
                     queue.dma_start(out=out_rows[:, tile : tile + tiles, j0 : j0 + width], in_=result[:])
 
-        left0, left1, right0 = (0, HALF, 0), (0, HALF, 1), (HALF, HALF, 0)
-        third1, fourth1 = (HALF, QUARTER, 1), (HALF + QUARTER, QUARTER, 1)
-
         open_score(left0, 0)
         for t in range(PACK):
             pass_v2(e_acc[left0][t], 0, 0, t, *v_operand(0, 0, HALF))
@@ -342,15 +335,15 @@ def tile_list_splice_map_reading_kernel(
         offset(left1)
         weave_e(left1, scalar_weave)
         own_codes(0, HALF, 4)
-        val_mx[0] = quantize(val_woven[0], "val0", 20)
+        val_mx[0] = quantize(val_woven[0], "val0", 18)
         quantize_e(left0)
         read_map(0, HALF, left0)
         offset(right0)
         weave_e(right0, scalar_weave)
         score(third1, 0)
         score(fourth1, 2)
-        val_mx[1] = quantize(val_woven[1], "val1", 28)
-        quantize_e(left1, 30)
+        val_mx[1] = quantize(val_woven[1], "val1", 26)
+        quantize_e(left1, 28)
         read_map(0, HALF, left1)
         finish(0, HALF, range(4))
         offset(third1)
@@ -358,7 +351,7 @@ def tile_list_splice_map_reading_kernel(
         own_codes(HALF, QUARTER, 0)
         offset(fourth1)
         own_codes(HALF + QUARTER, QUARTER, 2)
-        quantize_e(right0, 2)
+        quantize_e(right0, 34)
         quantize_e(third1)
         weave_e(fourth1, vector_weave)
         quantize_e(fourth1)

@@ -71,12 +71,9 @@ def tile_list_splice_map_reading_kernel(
             nc.vector.quantize_mx(out=codes[:].bitcast(FP8X4), scales=scales[:], in_=woven[:].rearrange("p c t -> p (c t)"))
             return codes, scales
 
-        def load_columns(queue, window, words, a, columns):
-            queue.dma_start(out=window[:, columns], in_=words[a].rearrange("p t i -> p (t i)").bitcast(I32)[:, columns])
-
         def load_words(words, a, name, kib):
             window = sbuf([P, T], I32, name, kib)
-            load_columns(nc.sync, window, words, a, slice(0, T))
+            nc.sync.dma_start(out=window[:], in_=words[a].rearrange("p t i -> p (t i)").bitcast(I32))
             return window
 
         def load_wv(a, kib):
@@ -101,39 +98,37 @@ def tile_list_splice_map_reading_kernel(
         v_scale_window = sbuf([P, T], U8, "v_scale_window")
         moved_v2 = sbuf([P, PASSES, S + N], U8, "moved_v2")
         moved_v = sbuf([P, PASSES, S], U8, "moved_v")
-        nc.gpsimd.memset(v2_scale_window[:].bitcast(I32), 0)
-        nc.vector.memset(v_scale_window[:, : T // 2].bitcast(I32), 0)
-        nc.gpsimd.memset(v_scale_window[:, T // 2 :].bitcast(I32), 0)
-        warm = keep.tile([P, 2], F32)
-        nc.gpsimd.memset(warm[:], 0.0)
+        nc.gpsimd.memset(v_scale_window[:].bitcast(I32), 0)
         gain_rows = sbuf([P, PASS], F32, "gain_rows")
         nc.vector.memset(gain_rows[:], 0.0)
+        nc.vector.memset(v2_scale_window[32:64, :].bitcast(I32), 0)
+        nc.vector.memset(v2_scale_window[64:, :].bitcast(I32), 0)
+        warm = keep.tile([P, 2], F32)
+        nc.gpsimd.memset(warm[:], 0.0)
         identity = sbuf([P, P], F32, "identity")
         make_identity(nc, identity[:])
-        nc.vector.memset(moved_v2[:].bitcast(I32), 0)
-        nc.vector.memset(moved_v[:].bitcast(I32), 0)
+        nc.gpsimd.memset(moved_v2[:].bitcast(I32), 0)
+        nc.gpsimd.memset(moved_v[:].bitcast(I32), 0)
 
-        v2_windows = [sbuf([P, T], I32, "v2_window0", 8)]
-        load_columns(nc.scalar, v2_windows[0], tab2_words, 0, slice(0, T // 2))
         list2 = keep.tile([P, S // LIST_ROWS], U16)
         nc.sync.dma_start(list2[:], offs2)
+        nc.sync.dma_start(
+            out=v2_scale_window[:32, :].bitcast(I32), in_=tab2_scales.bitcast(I32).rearrange("a q t -> q a t")
+        )
         lists = keep.tile([P, S // LIST_ROWS], U16)
         nc.sync.dma_start(lists[:], offs)
         staged_scales = sbuf([P, S + N], U8, "staged_scales")
         nc.sync.dma_start(
-            out=staged_scales[0:P:4, S:].bitcast(I32), in_=w4_scales.bitcast(I32).rearrange("a q c -> q a c")
+            out=staged_scales[:32, S:].bitcast(I32), in_=w4_scales.bitcast(I32).rearrange("a q c -> q a c")
         )
-        nc.sync.dma_start(
-            out=v2_scale_window[0:P:4, :].bitcast(I32), in_=tab2_scales.bitcast(I32).rearrange("a q t -> q a t")
-        )
-        nc.scalar.activation(out=warm[:, 1:2], in_=warm[:, 0:1], func=ACT.Silu)
-        wv_raw = [load_wv(0, 40)]
         nc.sync.dma_start(
             out=v_scale_window[0:P:4, :].bitcast(I32), in_=tab_scales.bitcast(I32).rearrange("a q t -> q a t")
         )
+        nc.scalar.activation(out=warm[:, 1:2], in_=warm[:, 0:1], func=ACT.Silu)
+        wv_raw = [load_wv(0, 40)]
         for i, gain in enumerate((gv, gm)):
             nc.sync.dma_start(out=gain_rows[PASSES * i : PASSES * (i + 1), :], in_=gain.rearrange("(b c) -> b c", b=PASSES))
-        load_columns(nc.sync, v2_windows[0], tab2_words, 0, slice(T // 2, T))
+        v2_windows = [load_words(tab2_words, 0, "v2_window0", 8)]
         wv_raw.append(load_wv(1, 48))
         turned = bank(7, [P, PACK, P])
         for t in range(PACK):
@@ -141,11 +136,11 @@ def tile_list_splice_map_reading_kernel(
         gains = sbuf([P, PACK, 2 * PASSES], F32, "gains")
         nc.scalar.copy(out=gains[:], in_=turned[:, :, : 2 * PASSES])
 
-        def move_rows(moved, source):
+        def move_rows(moved, source, step):
             for d in range(4):
                 nc.sync.dma_start(
                     out=moved[32 * d : 32 * d + 4, :, :].bitcast(I32),
-                    in_=source[32 * d : 32 * d + 32 : 4, :].bitcast(I32),
+                    in_=source[8 * step * d : 8 * step * (d + 1) : step, :].bitcast(I32),
                 )
 
         v2_scales_listed = sbuf([P, S], U8, "v2_scales_listed", 25.5)
@@ -154,12 +149,12 @@ def tile_list_splice_map_reading_kernel(
             out=staged_scales[:, :S].rearrange("p (b t c) -> p b t c", b=PASSES, t=PACK),
             in_=v2_scales_listed[:].rearrange("p (b c t) -> p b t c", b=PASSES, t=PACK),
         )
-        move_rows(moved_v2, staged_scales)
+        move_rows(moved_v2, staged_scales, 1)
         v2_windows.append(load_words(tab2_words, 1, "v2_window1", 18))
         v_windows = [load_words(tab_words, 0, "v_window0", 26)]
         v_scales_listed = sbuf([P, S], U8, "v_scales_listed")
         nc.vector.tensor_copy(out=v_scales_listed[:], in_=v_scale_window[:].indirect(lists[:]))
-        move_rows(moved_v, v_scales_listed)
+        move_rows(moved_v, v_scales_listed, 4)
 
         cols = HALF // LIST_ROWS
         v2_codes = {}
@@ -186,8 +181,11 @@ def tile_list_splice_map_reading_kernel(
 
         val_acc = {(b, t): bank(PACK * b + t, [P, N]) for b in range(PASSES) for t in range(PACK)}
         for a in range(PASSES):
-            woven = sbuf([P, N, PACK], BF16, f"wv_woven{a}")
-            by_fours(scalar_cast, woven[:], wv_raw[a][:])
+            woven = sbuf([P, N, PACK], BF16, f"wv_woven{a}", 56)
+            share = N if a == 0 else N // 2
+            by_fours(scalar_cast, woven[:, :share, :], wv_raw[a][:, :, :share])
+            if share < N:
+                gpsimd_weave(woven[:, share:, :], wv_raw[a][:, :, share:])
             if a == 0:
                 gather_v2(a, 0)
             codes, scales = quantize(woven, f"wv{a}")

@@ -76,10 +76,9 @@ def tile_list_splice_map_reading_kernel(
             nc.sync.dma_start(out=window[:], in_=words[a].rearrange("p t i -> p (t i)").bitcast(I32))
             return window
 
-        def load_wv(a, kib):
-            raw = sbuf([P, PACK, N], F32, f"wv_raw{a}", kib)
-            nc.sync.dma_start(out=raw[:], in_=wv[a * PASS : (a + 1) * PASS, :].rearrange("(p t) n -> p t n", t=PACK))
-            return raw
+        def load_wv(queue, a, planes):
+            rows = wv[a * PASS : (a + 1) * PASS, :].rearrange("(p t) n -> p t n", t=PACK)
+            queue.dma_start(out=wv_raw[a][:, planes, :], in_=rows[:, planes, :])
 
         prior_rows = {}
 
@@ -110,6 +109,8 @@ def tile_list_splice_map_reading_kernel(
         nc.gpsimd.memset(moved_v2[:].bitcast(I32), 0)
         nc.gpsimd.memset(moved_v[:].bitcast(I32), 0)
 
+        wv_raw = [sbuf([P, PACK, N], F32, f"wv_raw{a}", 40 + 8 * a) for a in range(PASSES)]
+        load_wv(nc.scalar, 0, slice(0, 1))
         list2 = keep.tile([P, S // LIST_ROWS], U16)
         nc.sync.dma_start(list2[:], offs2)
         nc.sync.dma_start(
@@ -125,11 +126,11 @@ def tile_list_splice_map_reading_kernel(
             out=v_scale_window[0:P:4, :].bitcast(I32), in_=tab_scales.bitcast(I32).rearrange("a q t -> q a t")
         )
         nc.scalar.activation(out=warm[:, 1:2], in_=warm[:, 0:1], func=ACT.Silu)
-        wv_raw = [load_wv(0, 40)]
+        load_wv(nc.sync, 0, slice(1, PACK))
         for i, gain in enumerate((gv, gm)):
             nc.sync.dma_start(out=gain_rows[PASSES * i : PASSES * (i + 1), :], in_=gain.rearrange("(b c) -> b c", b=PASSES))
         v2_windows = [load_words(tab2_words, 0, "v2_window0", 8)]
-        wv_raw.append(load_wv(1, 48))
+        load_wv(nc.sync, 1, slice(0, PACK))
         turned = bank(7, [P, PACK, P])
         for t in range(PACK):
             nc.tensor.transpose(turned[:, t, :], gain_rows[:, t:PASS:PACK], identity[:])
@@ -233,7 +234,6 @@ def tile_list_splice_map_reading_kernel(
             h, first = divmod(j0, HALF)
             return v_codes[a, h][:, first : first + width], moved_v[:, a, j0 : j0 + width]
 
-        out_rows = out.rearrange("(n p) j -> p n j", p=P)
         e_acc, e_planes, e_woven, e_mx, val_mx, y_acc = {}, {}, {}, {}, {}, {}
 
         def open_score(unit, first_bank):
@@ -271,53 +271,45 @@ def tile_list_splice_map_reading_kernel(
         def quantize_e(unit, kib=None):
             e_mx[unit] = quantize(e_woven[unit], f"e{unit[0]}_{unit[2]}", kib)
 
-        def own_codes(j0, width, first_bank):
-            share = HALF // width
-            y_acc[j0] = [bank(first_bank + i, [P, HALF]) for i in range(N // P // share)]
-            step = width if width == HALF else P
-            for tile in range(N // P):
-                y, i, n0 = y_acc[j0][tile // share], tile % share, tile * P
-                for a in range(PASSES):
-                    for c0 in range(0, width, step):
-                        codes, scales = v_operand(a, j0 + c0, step)
-                        nc.tensor.matmul_mx(
-                            out=y[:, i * width + c0 : i * width + c0 + step],
-                            lhsT=w4_codes[:, a, 2 * n0 : 2 * (n0 + P)].bitcast(FP4X4),
-                            lhsT_scale=moved_v2[:, a, S + n0 : S + n0 + P],
-                            rhs=codes.bitcast(FP8X4),
-                            rhs_scale=scales,
-                            start=(i == 0 and a == 0 and c0 == 0),
-                            stop=False,
-                        )
-
-        def read_map(j0, width, unit, tiles=range(N // P)):
-            share = HALF // width
-            first, b = j0 - unit[0], unit[2]
+        def own_codes(h, first_bank, tiles=range(N // P)):
             for tile in tiles:
-                y, i, n0 = y_acc[j0][tile // share], tile % share, tile * P
-                nc.tensor.matmul_mx(
-                    out=y[:, i * width : (i + 1) * width],
-                    lhsT=val_mx[b][0][:, n0 : n0 + P].bitcast(FP8X4),
-                    lhsT_scale=val_mx[b][1][:, n0 : n0 + P],
-                    rhs=e_mx[unit][0][:, first : first + width].bitcast(FP8X4),
-                    rhs_scale=e_mx[unit][1][:, first : first + width],
-                    start=False,
-                    stop=(b == PASSES - 1 and i == share - 1),
-                )
+                y_acc[h, tile] = bank(first_bank + tile, [P, HALF])
+                n0 = tile * P
+                for a in range(PASSES):
+                    codes, scales = v_operand(a, h * HALF, HALF)
+                    nc.tensor.matmul_mx(
+                        out=y_acc[h, tile][:],
+                        lhsT=w4_codes[:, a, 2 * n0 : 2 * (n0 + P)].bitcast(FP4X4),
+                        lhsT_scale=moved_v2[:, a, S + n0 : S + n0 + P],
+                        rhs=codes.bitcast(FP8X4),
+                        rhs_scale=scales,
+                        start=(a == 0),
+                        stop=False,
+                    )
 
-        def finish(j0, width, banks):
-            share = HALF // width
-            for i in banks:
-                y = y_acc[j0][i]
-                last = j0 + width == S and i == len(y_acc[j0]) - 1
-                tiles = 1 if last else share
-                for first in range(0, share, tiles):
-                    result = keep.tile([P, tiles, width], F32, name=f"result{j0}_{i}_{first}")
-                    sums = y[:, first * width : (first + tiles) * width].rearrange("p (n j) -> p n j", n=tiles)
-                    nc.scalar.activation(out=result[:], in_=sums, func=ACT.Silu)
-                    tile = share * i + first
-                    queue = nc.scalar if last and first else nc.sync
-                    queue.dma_start(out=out_rows[:, tile : tile + tiles, j0 : j0 + width], in_=result[:])
+        def read_map(unit, tile, closes):
+            j0, width, b = unit
+            h, first = divmod(j0, HALF)
+            n0 = tile * P
+            nc.tensor.matmul_mx(
+                out=y_acc[h, tile][:, first : first + width],
+                lhsT=val_mx[b][0][:, n0 : n0 + P].bitcast(FP8X4),
+                lhsT_scale=val_mx[b][1][:, n0 : n0 + P],
+                rhs=e_mx[unit][0][:].bitcast(FP8X4),
+                rhs_scale=e_mx[unit][1][:],
+                start=False,
+                stop=closes,
+            )
+
+        def finish(h, tile):
+            last = h == 1 and tile == N // P - 1
+            width = QUARTER if last else HALF
+            for first in range(0, HALF, width):
+                result = keep.tile([P, width], F32, name=f"result{h}_{tile}_{first}")
+                nc.scalar.activation(out=result[:], in_=y_acc[h, tile][:, first : first + width], func=ACT.Silu)
+                queue = nc.scalar if last and first else nc.sync
+                j0 = h * HALF + first
+                queue.dma_start(out=out[tile * P : (tile + 1) * P, j0 : j0 + width], in_=result[:])
 
         open_score(left0, 0)
         for t in range(PACK):
@@ -332,29 +324,31 @@ def tile_list_splice_map_reading_kernel(
         score(right0, 0)
         offset(left1)
         weave_e(left1, scalar_weave)
-        own_codes(0, HALF, 4)
+        own_codes(0, 4)
         val_mx[0] = quantize(val_woven[0], "val0", 18)
         quantize_e(left0)
-        read_map(0, HALF, left0)
+        for tile in range(N // P):
+            read_map(left0, tile, False)
         offset(right0)
         weave_e(right0, scalar_weave)
         score(third1, 0)
         score(fourth1, 2)
         val_mx[1] = quantize(val_woven[1], "val1", 26)
         quantize_e(left1, 28)
-        read_map(0, HALF, left1)
-        finish(0, HALF, range(4))
+        for tile in range(N // P):
+            read_map(left1, tile, True)
+            finish(0, tile)
         offset(third1)
         weave_e(third1, gpsimd_weave)
-        own_codes(HALF, QUARTER, 0)
+        own_codes(1, 0, (0, 1))
         offset(fourth1)
-        own_codes(HALF + QUARTER, QUARTER, 2)
+        own_codes(1, 0, (2, 3))
         quantize_e(right0, 34)
         quantize_e(third1)
         weave_e(fourth1, vector_weave)
         quantize_e(fourth1)
-        for j0, unit in ((HALF, third1), (HALF + QUARTER, fourth1)):
-            for i in range(2):
-                read_map(j0, QUARTER, right0, (2 * i, 2 * i + 1))
-                read_map(j0, QUARTER, unit, (2 * i, 2 * i + 1))
-                finish(j0, QUARTER, (i,))
+        for tile in range(N // P):
+            read_map(right0, tile, False)
+            read_map(third1, tile, False)
+            read_map(fourth1, tile, True)
+            finish(1, tile)

@@ -228,12 +228,14 @@ def tile_list_splice_map_reading_kernel(
         load_prior(right0, 26, 0, 2)
         load_prior(right0, 30, 2, 2)
         load_prior(third1, 34)
-        load_prior(fourth1, 38)
+        load_prior(fourth1, 38, 0, 2)
+        load_prior(fourth1, 40, 2, 2)
 
         def v_operand(a, j0, width):
             h, first = divmod(j0, HALF)
             return v_codes[a, h][:, first : first + width], moved_v[:, a, j0 : j0 + width]
 
+        out_rows = out.rearrange("(n p) j -> p n j", p=P)
         e_acc, e_planes, e_woven, e_mx, val_mx, y_acc = {}, {}, {}, {}, {}, {}
 
         def open_score(unit, first_bank):
@@ -249,9 +251,9 @@ def tile_list_splice_map_reading_kernel(
                 for a in range(PASSES):
                     pass_v2(e_acc[unit][t], a, b, t, *v_operand(a, j0, width))
 
-        def offset(unit):
+        def offset(unit, kib=None):
             j0, width, b = unit
-            planes = sbuf([P, PACK, width], BF16, f"e_planes{j0}_{b}")
+            planes = sbuf([P, PACK, width], BF16, f"e_planes{j0}_{b}", kib)
             for t in range(PACK):
                 nc.vector.scalar_tensor_tensor(
                     out=planes[:, t, :],
@@ -263,53 +265,61 @@ def tile_list_splice_map_reading_kernel(
                 )
             e_planes[unit] = planes
 
-        def weave_e(unit, engine_weave):
+        def weave_e(unit, engine_weave, kib=None):
             j0, width, b = unit
-            e_woven[unit] = sbuf([P, width, PACK], BF16, f"e_woven{j0}_{b}")
+            e_woven[unit] = sbuf([P, width, PACK], BF16, f"e_woven{j0}_{b}", kib)
             engine_weave(e_woven[unit][:], e_planes[unit][:])
 
         def quantize_e(unit, kib=None):
             e_mx[unit] = quantize(e_woven[unit], f"e{unit[0]}_{unit[2]}", kib)
 
-        def own_codes(h, first_bank, tiles=range(N // P)):
-            for tile in tiles:
-                y_acc[h, tile] = bank(first_bank + tile, [P, HALF])
-                n0 = tile * P
+        def own_codes(j0, width, first_bank):
+            share = HALF // width
+            y_acc[j0] = [bank(first_bank + i, [P, HALF]) for i in range(N // P // share)]
+            step = width if width == HALF else P
+            for tile in range(N // P):
+                y, i, n0 = y_acc[j0][tile // share], tile % share, tile * P
                 for a in range(PASSES):
-                    codes, scales = v_operand(a, h * HALF, HALF)
-                    nc.tensor.matmul_mx(
-                        out=y_acc[h, tile][:],
-                        lhsT=w4_codes[:, a, 2 * n0 : 2 * (n0 + P)].bitcast(FP4X4),
-                        lhsT_scale=moved_v2[:, a, S + n0 : S + n0 + P],
-                        rhs=codes.bitcast(FP8X4),
-                        rhs_scale=scales,
-                        start=(a == 0),
-                        stop=False,
-                    )
+                    for c0 in range(0, width, step):
+                        codes, scales = v_operand(a, j0 + c0, step)
+                        nc.tensor.matmul_mx(
+                            out=y[:, i * width + c0 : i * width + c0 + step],
+                            lhsT=w4_codes[:, a, 2 * n0 : 2 * (n0 + P)].bitcast(FP4X4),
+                            lhsT_scale=moved_v2[:, a, S + n0 : S + n0 + P],
+                            rhs=codes.bitcast(FP8X4),
+                            rhs_scale=scales,
+                            start=(i == 0 and a == 0 and c0 == 0),
+                            stop=False,
+                        )
 
-        def read_map(unit, tile, closes):
-            j0, width, b = unit
-            h, first = divmod(j0, HALF)
-            n0 = tile * P
-            nc.tensor.matmul_mx(
-                out=y_acc[h, tile][:, first : first + width],
-                lhsT=val_mx[b][0][:, n0 : n0 + P].bitcast(FP8X4),
-                lhsT_scale=val_mx[b][1][:, n0 : n0 + P],
-                rhs=e_mx[unit][0][:].bitcast(FP8X4),
-                rhs_scale=e_mx[unit][1][:],
-                start=False,
-                stop=closes,
-            )
+        def read_map(j0, width, unit, tiles=range(N // P)):
+            share = HALF // width
+            first, b = j0 - unit[0], unit[2]
+            for tile in tiles:
+                y, i, n0 = y_acc[j0][tile // share], tile % share, tile * P
+                nc.tensor.matmul_mx(
+                    out=y[:, i * width : (i + 1) * width],
+                    lhsT=val_mx[b][0][:, n0 : n0 + P].bitcast(FP8X4),
+                    lhsT_scale=val_mx[b][1][:, n0 : n0 + P],
+                    rhs=e_mx[unit][0][:, first : first + width].bitcast(FP8X4),
+                    rhs_scale=e_mx[unit][1][:, first : first + width],
+                    start=False,
+                    stop=(b == PASSES - 1 and i == share - 1),
+                )
 
-        def finish(h, tile):
-            last = h == 1 and tile == N // P - 1
-            width = QUARTER if last else HALF
-            for first in range(0, HALF, width):
-                result = keep.tile([P, width], F32, name=f"result{h}_{tile}_{first}")
-                nc.scalar.activation(out=result[:], in_=y_acc[h, tile][:, first : first + width], func=ACT.Silu)
-                queue = nc.scalar if last and first else nc.sync
-                j0 = h * HALF + first
-                queue.dma_start(out=out[tile * P : (tile + 1) * P, j0 : j0 + width], in_=result[:])
+        def finish(j0, width, banks):
+            share = HALF // width
+            for i in banks:
+                y = y_acc[j0][i]
+                last = j0 + width == S and i == len(y_acc[j0]) - 1
+                tiles = 1 if last else share
+                for first in range(0, share, tiles):
+                    result = keep.tile([P, tiles, width], F32, name=f"result{j0}_{i}_{first}")
+                    sums = y[:, first * width : (first + tiles) * width].rearrange("p (n j) -> p n j", n=tiles)
+                    nc.scalar.activation(out=result[:], in_=sums, func=ACT.Silu)
+                    tile = share * i + first
+                    queue = nc.scalar if last and first else nc.sync
+                    queue.dma_start(out=out_rows[:, tile : tile + tiles, j0 : j0 + width], in_=result[:])
 
         open_score(left0, 0)
         for t in range(PACK):
@@ -324,31 +334,29 @@ def tile_list_splice_map_reading_kernel(
         score(right0, 0)
         offset(left1)
         weave_e(left1, scalar_weave)
-        own_codes(0, 4)
+        own_codes(0, HALF, 4)
         val_mx[0] = quantize(val_woven[0], "val0", 18)
         quantize_e(left0)
-        for tile in range(N // P):
-            read_map(left0, tile, False)
+        read_map(0, HALF, left0)
         offset(right0)
-        weave_e(right0, scalar_weave)
+        weave_e(right0, scalar_weave, 60)
         score(third1, 0)
         score(fourth1, 2)
         val_mx[1] = quantize(val_woven[1], "val1", 26)
         quantize_e(left1, 28)
-        for tile in range(N // P):
-            read_map(left1, tile, True)
-            finish(0, tile)
+        read_map(0, HALF, left1)
+        finish(0, HALF, range(4))
         offset(third1)
-        weave_e(third1, gpsimd_weave)
-        own_codes(1, 0, (0, 1))
-        offset(fourth1)
-        own_codes(1, 0, (2, 3))
+        own_codes(HALF, QUARTER, 0)
         quantize_e(right0, 34)
-        quantize_e(third1)
+        weave_e(third1, gpsimd_weave, 60)
+        offset(fourth1, 30)
+        own_codes(HALF + QUARTER, QUARTER, 2)
         weave_e(fourth1, vector_weave)
+        quantize_e(third1, 38)
         quantize_e(fourth1)
-        for tile in range(N // P):
-            read_map(right0, tile, False)
-            read_map(third1, tile, False)
-            read_map(fourth1, tile, True)
-            finish(1, tile)
+        for j0, unit in ((HALF, third1), (HALF + QUARTER, fourth1)):
+            for i in range(2):
+                read_map(j0, QUARTER, right0, (2 * i, 2 * i + 1))
+                read_map(j0, QUARTER, unit, (2 * i, 2 * i + 1))
+                finish(j0, QUARTER, (i,))

@@ -24,6 +24,7 @@ PASSES = 2
 HALF = 512
 QUARTER = 256
 LIST_ROWS = 16
+SCALAR_CAST = 336
 KIB = 1024
 
 
@@ -183,7 +184,7 @@ def tile_list_splice_map_reading_kernel(
         val_acc = {(b, t): bank(PACK * b + t, [P, N]) for b in range(PASSES) for t in range(PACK)}
         for a in range(PASSES):
             woven = sbuf([P, N, PACK], BF16, f"wv_woven{a}", 56)
-            share = N if a == 0 else N // 2
+            share = N if a == 0 else SCALAR_CAST
             by_fours(scalar_cast, woven[:, :share, :], wv_raw[a][:, :, :share])
             if share < N:
                 gpsimd_weave(woven[:, share:, :], wv_raw[a][:, :, share:])
@@ -202,7 +203,7 @@ def tile_list_splice_map_reading_kernel(
             for t in range(PACK):
                 nc.scalar.activation(out=planes[:, t, :], in_=val_acc[b, t][:], func=ACT.Copy, scale=gains[:, t, b : b + 1])
             val_woven.append(sbuf([P, N, PACK], BF16, f"val_woven{b}"))
-            gpsimd_weave(val_woven[b][:], planes[:])
+            (scalar_weave if b else gpsimd_weave)(val_woven[b][:], planes[:])
 
         v_windows.append(load_words(tab_words, 1, "v_window1", 34))
         load_prior(left0, 8, 0, 2)
@@ -228,8 +229,7 @@ def tile_list_splice_map_reading_kernel(
         load_prior(right0, 26, 0, 2)
         load_prior(right0, 30, 2, 2)
         load_prior(third1, 34)
-        load_prior(fourth1, 38, 0, 2)
-        load_prior(fourth1, 40, 2, 2)
+        load_prior(fourth1, 38)
 
         def v_operand(a, j0, width):
             h, first = divmod(j0, HALF)
@@ -339,7 +339,7 @@ def tile_list_splice_map_reading_kernel(
         quantize_e(left0)
         read_map(0, HALF, left0)
         offset(right0)
-        weave_e(right0, scalar_weave, 60)
+        weave_e(right0, scalar_weave)
         score(third1, 0)
         score(fourth1, 2)
         val_mx[1] = quantize(val_woven[1], "val1", 26)
@@ -348,12 +348,12 @@ def tile_list_splice_map_reading_kernel(
         finish(0, HALF, range(4))
         offset(third1)
         own_codes(HALF, QUARTER, 0)
-        quantize_e(right0, 34)
-        weave_e(third1, gpsimd_weave, 60)
-        offset(fourth1, 30)
+        offset(fourth1)
         own_codes(HALF + QUARTER, QUARTER, 2)
+        weave_e(third1, vector_weave, 38)
+        quantize_e(right0, 40)
+        quantize_e(third1)
         weave_e(fourth1, vector_weave)
-        quantize_e(third1, 38)
         quantize_e(fourth1)
         for j0, unit in ((HALF, third1), (HALF + QUARTER, fourth1)):
             for i in range(2):

@@ -23,6 +23,7 @@ PASS = P * PACK
 PASSES = 2
 HALF = 512
 QUARTER = 256
+TILES = N // P
 LIST_ROWS = 16
 SCALAR_CAST = 336
 KIB = 1024
@@ -45,31 +46,23 @@ def tile_list_splice_map_reading_kernel(
         def bank(index, shape):
             return psum.tile(shape, F32, name=f"bank{index}", tag=f"bank{index}")
 
-        def by_fours(copy, woven, planes):
-            copy(
-                out=woven.rearrange("p (c i) t -> p c t i", i=PACK),
-                in_=planes.rearrange("p t (c i) -> p c t i", i=PACK),
-            )
+        def woven_walk(woven, run):
+            return woven.rearrange("p (c i) t -> p c t i", i=run)
 
-        def scalar_cast(out, in_):
-            nc.scalar.activation(out=out, in_=in_, func=ACT.Copy)
-
-        def scalar_weave(woven, planes):
-            by_fours(nc.scalar.copy, woven, planes)
-
-        def vector_weave(woven, planes):
-            by_fours(nc.vector.tensor_copy, woven, planes)
+        def plane_walk(planes, run):
+            return planes.rearrange("p t (c i) -> p c t i", i=run)
 
         def gpsimd_weave(woven, planes):
             nc.gpsimd.tensor_scalar(
                 out=woven, in0=planes.rearrange("p t c -> p c t"), scalar1=1.0, scalar2=0.0, op0=ALU.mult, op1=ALU.add
             )
 
-        def quantize(woven, name, kib=None):
-            width = woven.shape[1]
+        def quantize(woven, width, name, kib=None, scales=None):
             codes = sbuf([P, width], U32, f"{name}_codes", kib)
-            scales = sbuf([P, width], U8, f"{name}_scales")
-            nc.vector.quantize_mx(out=codes[:].bitcast(FP8X4), scales=scales[:], in_=woven[:].rearrange("p c t -> p (c t)"))
+            if scales is None:
+                tile = sbuf([P, width], U8, f"{name}_scales")
+                scales = tile[:]
+            nc.vector.quantize_mx(out=codes[:].bitcast(FP8X4), scales=scales, in_=woven)
             return codes, scales
 
         def load_words(words, a, name, kib):
@@ -81,36 +74,36 @@ def tile_list_splice_map_reading_kernel(
             rows = wv[a * PASS : (a + 1) * PASS, :].rearrange("(p t) n -> p t n", t=PACK)
             queue.dma_start(out=wv_raw[a][:, planes, :], in_=rows[:, planes, :])
 
-        prior_rows = {}
+        def load_prior(h, b, kib):
+            rows = sbuf([P, PACK, HALF], F32, f"prior{h}_{b}", kib)
+            source = prior[b * PASS : (b + 1) * PASS, h * HALF : (h + 1) * HALF].rearrange("(p t) j -> p t j", t=PACK)
+            nc.sync.dma_start(out=rows[:], in_=source)
+            return rows
 
-        def load_prior(unit, kib, t0=0, planes=PACK):
-            j0, width, b = unit
-            rows = sbuf([P, planes, width], F32, f"prior{j0}_{b}_{t0}", kib)
-            source = prior[b * PASS : (b + 1) * PASS, j0 : j0 + width].rearrange("(p t) j -> p t j", t=PACK)
-            nc.sync.dma_start(out=rows[:], in_=source[:, t0 : t0 + planes, :])
-            for t in range(planes):
-                prior_rows[unit, t0 + t] = rows[:, t, :]
+        def move_rows(queue, moved, source, step):
+            for d in range(4):
+                queue.dma_start(
+                    out=moved[32 * d : 32 * d + 4, :, :].bitcast(I32),
+                    in_=source[8 * step * d : 8 * step * (d + 1) : step, :].bitcast(I32),
+                )
 
-        left0, left1, right0 = (0, HALF, 0), (0, HALF, 1), (HALF, HALF, 0)
-        third1, fourth1 = (HALF, QUARTER, 1), (HALF + QUARTER, QUARTER, 1)
-
-        v2_scale_window = sbuf([P, T], U8, "v2_scale_window")
-        v_scale_window = sbuf([P, T], U8, "v_scale_window")
-        moved_v2 = sbuf([P, PASSES, S + N], U8, "moved_v2")
+        v2_scale_window = sbuf([P, T], U8, "v2_scale_window", 15)
+        v_scale_window = sbuf([P, T], U8, "v_scale_window", 34)
+        moved_v2 = sbuf([P, PASSES, S], U8, "moved_v2")
         moved_v = sbuf([P, PASSES, S], U8, "moved_v")
-        nc.gpsimd.memset(v_scale_window[:].bitcast(I32), 0)
         gain_rows = sbuf([P, PASS], F32, "gain_rows")
+        identity = sbuf([P, P], F32, "identity")
+        nc.gpsimd.memset(v_scale_window[:].bitcast(I32), 0)
         nc.vector.memset(gain_rows[:], 0.0)
         nc.vector.memset(v2_scale_window[32:64, :].bitcast(I32), 0)
         nc.vector.memset(v2_scale_window[64:, :].bitcast(I32), 0)
         warm = keep.tile([P, 2], F32)
         nc.gpsimd.memset(warm[:], 0.0)
-        identity = sbuf([P, P], F32, "identity")
         make_identity(nc, identity[:])
         nc.gpsimd.memset(moved_v2[:].bitcast(I32), 0)
         nc.gpsimd.memset(moved_v[:].bitcast(I32), 0)
 
-        wv_raw = [sbuf([P, PACK, N], F32, f"wv_raw{a}", 40 + 8 * a) for a in range(PASSES)]
+        wv_raw = [sbuf([P, PACK, N], F32, f"wv_raw{a}", kib) for a, kib in enumerate((40, 48))]
         load_wv(nc.scalar, 0, slice(0, 1))
         list2 = keep.tile([P, S // LIST_ROWS], U16)
         nc.sync.dma_start(list2[:], offs2)
@@ -119,18 +112,14 @@ def tile_list_splice_map_reading_kernel(
         )
         lists = keep.tile([P, S // LIST_ROWS], U16)
         nc.sync.dma_start(lists[:], offs)
-        staged_scales = sbuf([P, S + N], U8, "staged_scales")
-        nc.sync.dma_start(
-            out=staged_scales[:32, S:].bitcast(I32), in_=w4_scales.bitcast(I32).rearrange("a q c -> q a c")
-        )
         nc.sync.dma_start(
             out=v_scale_window[0:P:4, :].bitcast(I32), in_=tab_scales.bitcast(I32).rearrange("a q t -> q a t")
         )
-        nc.scalar.activation(out=warm[:, 1:2], in_=warm[:, 0:1], func=ACT.Silu)
         load_wv(nc.sync, 0, slice(1, PACK))
+        nc.scalar.activation(out=warm[:, 1:2], in_=warm[:, 0:1], func=ACT.Silu)
         for i, gain in enumerate((gv, gm)):
             nc.sync.dma_start(out=gain_rows[PASSES * i : PASSES * (i + 1), :], in_=gain.rearrange("(b c) -> b c", b=PASSES))
-        v2_windows = [load_words(tab2_words, 0, "v2_window0", 8)]
+        v2_windows = [load_words(tab2_words, 0, "v2_window0", 0)]
         load_wv(nc.sync, 1, slice(0, PACK))
         turned = bank(7, [P, PACK, P])
         for t in range(PACK):
@@ -138,25 +127,18 @@ def tile_list_splice_map_reading_kernel(
         gains = sbuf([P, PACK, 2 * PASSES], F32, "gains")
         nc.scalar.copy(out=gains[:], in_=turned[:, :, : 2 * PASSES])
 
-        def move_rows(moved, source, step):
-            for d in range(4):
-                nc.sync.dma_start(
-                    out=moved[32 * d : 32 * d + 4, :, :].bitcast(I32),
-                    in_=source[8 * step * d : 8 * step * (d + 1) : step, :].bitcast(I32),
-                )
-
-        v2_scales_listed = sbuf([P, S], U8, "v2_scales_listed", 25.5)
-        nc.vector.tensor_copy(out=v2_scales_listed[:], in_=v2_scale_window[:].indirect(list2[:]))
+        v2_scales_listed = sbuf([P, S], U8, "v2_scales_listed")
         nc.vector.tensor_copy(
-            out=staged_scales[:, :S].rearrange("p (b t c) -> p b t c", b=PASSES, t=PACK),
-            in_=v2_scales_listed[:].rearrange("p (b c t) -> p b t c", b=PASSES, t=PACK),
+            out=v2_scales_listed[:].rearrange("p (b t c) -> p b c t", b=PASSES, t=PACK),
+            in_=v2_scale_window[:].indirect(list2[:]),
         )
-        move_rows(moved_v2, staged_scales, 1)
-        v2_windows.append(load_words(tab2_words, 1, "v2_window1", 18))
-        v_windows = [load_words(tab_words, 0, "v_window0", 26)]
+        move_rows(nc.sync, moved_v2, v2_scales_listed, 1)
+        v2_windows.append(load_words(tab2_words, 1, "v2_window1", 8))
+        v_windows = [load_words(tab_words, 0, "v_window0", 16)]
         v_scales_listed = sbuf([P, S], U8, "v_scales_listed")
         nc.vector.tensor_copy(out=v_scales_listed[:], in_=v_scale_window[:].indirect(lists[:]))
-        move_rows(moved_v, v_scales_listed, 4)
+        move_rows(nc.sync, moved_v, v_scales_listed, 4)
+        v_windows.append(load_words(tab_words, 1, "v_window1", 27))
 
         cols = HALF // LIST_ROWS
         v2_codes = {}
@@ -169,7 +151,7 @@ def tile_list_splice_map_reading_kernel(
             )
             v2_codes[a, b] = codes
 
-        def pass_v2(acc, a, b, t, codes, scales, closes=True):
+        def pass_v2(acc, a, b, t, codes, scales):
             first = b * PASS + t * P
             nc.tensor.matmul_mx(
                 out=acc,
@@ -178,65 +160,67 @@ def tile_list_splice_map_reading_kernel(
                 rhs=codes.bitcast(FP8X4),
                 rhs_scale=scales,
                 start=(a == 0),
-                stop=(a == PASSES - 1 and closes),
+                stop=(a == PASSES - 1),
             )
 
+        w4_planes = sbuf([P, PASSES, N], U8, "w4_planes")
         val_acc = {(b, t): bank(PACK * b + t, [P, N]) for b in range(PASSES) for t in range(PACK)}
         for a in range(PASSES):
-            woven = sbuf([P, N, PACK], BF16, f"wv_woven{a}", 56)
+            woven = sbuf([P, N, PACK], BF16, f"wv_woven{a}")
             share = N if a == 0 else SCALAR_CAST
-            by_fours(scalar_cast, woven[:, :share, :], wv_raw[a][:, :, :share])
+            nc.scalar.activation(
+                out=woven_walk(woven[:, :share, :], PACK), in_=plane_walk(wv_raw[a][:, :, :share], PACK), func=ACT.Copy
+            )
             if share < N:
                 gpsimd_weave(woven[:, share:, :], wv_raw[a][:, :, share:])
             if a == 0:
                 gather_v2(a, 0)
-            codes, scales = quantize(woven, f"wv{a}")
+            codes, scales = quantize(woven[:].rearrange("p c t -> p (c t)"), N, f"wv{a}", None, w4_planes[:, a, :])
             if a == 1:
                 gather_v2(a, 0, 48)
             gather_v2(a, 1, 46 if a == 0 else 50)
             for b in range(PASSES):
                 for t in range(PACK):
-                    pass_v2(val_acc[b, t][:], a, b, t, codes[:], scales[:])
-        val_woven = []
+                    pass_v2(val_acc[b, t][:], a, b, t, codes[:], scales)
+        val_planes = []
         for b in range(PASSES):
-            planes = sbuf([P, PACK, N], BF16, f"val_planes{b}")
+            val_planes.append(sbuf([P, PACK, N], BF16, f"val_planes{b}"))
             for t in range(PACK):
-                nc.scalar.activation(out=planes[:, t, :], in_=val_acc[b, t][:], func=ACT.Copy, scale=gains[:, t, b : b + 1])
-            val_woven.append(sbuf([P, N, PACK], BF16, f"val_woven{b}"))
-            (scalar_weave if b else gpsimd_weave)(val_woven[b][:], planes[:])
+                nc.scalar.activation(
+                    out=val_planes[b][:, t, :], in_=val_acc[b, t][:], func=ACT.Copy, scale=gains[:, t, b : b + 1]
+                )
 
-        v_windows.append(load_words(tab_words, 1, "v_window1", 34))
-        load_prior(left0, 8, 0, 2)
-        load_prior(left0, 12, 2, 2)
-        w4_codes = sbuf([P, PASSES, 2 * N], U8, "w4_codes", 52)
+        prior_rows = {(0, 0): load_prior(0, 0, 0), (0, 1): load_prior(0, 1, 8)}
+        w4_codes = sbuf([P, PASSES, 2 * N], U8, "w4_codes", 16)
         nc.sync.dma_start(out=w4_codes[:].bitcast(I32), in_=w4_words.bitcast(I32).rearrange("a p c -> p a c"))
-        load_prior(left1, 18, 0, 2)
-        load_prior(left1, 22, 2, 2)
+        w4_rows = w4_scales.bitcast(I32).rearrange("a q c -> q a c")
+        for d in range(4):
+            nc.sync.dma_start(out=w4_planes[32 * d : 32 * d + 4, :, :].bitcast(I32), in_=w4_rows[4 * d : 4 * d + 4])
+
+        val_woven = [sbuf([P, N, PACK], BF16, f"val_woven{b}", kib) for b, kib in enumerate((None, 27))]
+        gpsimd_weave(val_woven[0][:], val_planes[0][:])
 
         v_codes = {}
-        for h in range(S // HALF):
-            for a in range(PASSES):
+        for a in range(PASSES):
+            for h in range(S // HALF):
                 codes = sbuf([P, HALF], U32, f"v_codes{a}_{h}")
-                pieces = 2 if (a, h) == (1, 0) else 1
-                for i in range(pieces):
-                    first, step = (h * pieces + i) * cols // pieces, cols // pieces
-                    nc.vector.tensor_copy(
-                        out=codes[:, i * HALF // pieces : (i + 1) * HALF // pieces],
-                        in_=v_windows[a][:].bitcast(U32).indirect(lists[:, first : first + step]),
-                    )
+                nc.vector.tensor_copy(
+                    out=codes[:], in_=v_windows[a][:].bitcast(U32).indirect(lists[:, h * cols : (h + 1) * cols])
+                )
                 v_codes[a, h] = codes
+        for b in range(PASSES):
+            prior_rows[1, b] = load_prior(1, b, 19 + 14 * b)
 
-        load_prior(right0, 26, 0, 2)
-        load_prior(right0, 30, 2, 2)
-        load_prior(third1, 34)
-        load_prior(fourth1, 38)
+        nc.vector.tensor_copy(out=woven_walk(val_woven[1][:], PACK), in_=plane_walk(val_planes[1][:], PACK))
+        val_mx = [
+            quantize(val_woven[b][:].rearrange("p c t -> p (c t)"), N, f"val{b}", kib) for b, kib in enumerate((31, None))
+        ]
 
         def v_operand(a, j0, width):
             h, first = divmod(j0, HALF)
             return v_codes[a, h][:, first : first + width], moved_v[:, a, j0 : j0 + width]
 
-        out_rows = out.rearrange("(n p) j -> p n j", p=P)
-        e_acc, e_planes, e_woven, e_mx, val_mx, y_acc = {}, {}, {}, {}, {}, {}
+        e_acc, e_scaled, e_mx, y_acc = {}, {}, {}, {}
 
         def open_score(unit, first_bank):
             width = unit[1]
@@ -244,119 +228,127 @@ def tile_list_splice_map_reading_kernel(
             tiles = [bank(first_bank + i, [P, share, width]) for i in range(PACK // share)]
             e_acc[unit] = [tiles[t // share][:, t % share, :] for t in range(PACK)]
 
-        def score(unit, first_bank):
+        def score_pass(unit, a, t):
             j0, width, b = unit
-            open_score(unit, first_bank)
+            pass_v2(e_acc[unit][t], a, b, t, *v_operand(a, j0, width))
+
+        def scale_out(unit):
+            j0, width, b = unit
+            e_scaled[unit] = sbuf([P, PACK, width], F32, f"e_scaled{j0}_{b}")
             for t in range(PACK):
-                for a in range(PASSES):
-                    pass_v2(e_acc[unit][t], a, b, t, *v_operand(a, j0, width))
+                gain = gains[:, t, PASSES + b : PASSES + b + 1]
+                nc.scalar.activation(out=e_scaled[unit][:, t, :], in_=e_acc[unit][t], func=ACT.Copy, scale=gain)
 
-        def offset(unit, kib=None):
+        def add_prior(unit, woven):
             j0, width, b = unit
-            planes = sbuf([P, PACK, width], BF16, f"e_planes{j0}_{b}", kib)
-            for t in range(PACK):
-                nc.vector.scalar_tensor_tensor(
-                    out=planes[:, t, :],
-                    in0=e_acc[unit][t],
-                    scalar=gains[:, t, PASSES + b : PASSES + b + 1],
-                    in1=prior_rows[unit, t],
-                    op0=ALU.mult,
-                    op1=ALU.add,
-                )
-            e_planes[unit] = planes
-
-        def weave_e(unit, engine_weave, kib=None):
-            j0, width, b = unit
-            e_woven[unit] = sbuf([P, width, PACK], BF16, f"e_woven{j0}_{b}", kib)
-            engine_weave(e_woven[unit][:], e_planes[unit][:])
-
-        def quantize_e(unit, kib=None):
-            e_mx[unit] = quantize(e_woven[unit], f"e{unit[0]}_{unit[2]}", kib)
+            h, first = divmod(j0, HALF)
+            nc.vector.tensor_tensor(
+                out=woven_walk(woven, 2),
+                in0=plane_walk(e_scaled[unit][:], 2),
+                in1=plane_walk(prior_rows[h, b][:, :, first : first + width], 2),
+                op=ALU.add,
+            )
 
         def own_codes(j0, width, first_bank):
             share = HALF // width
-            y_acc[j0] = [bank(first_bank + i, [P, HALF]) for i in range(N // P // share)]
-            step = width if width == HALF else P
-            for tile in range(N // P):
-                y, i, n0 = y_acc[j0][tile // share], tile % share, tile * P
+            y_acc[j0] = [bank(first_bank + i, [P, share, width]) for i in range(TILES // share)]
+            for tile in range(TILES):
+                n0 = tile * P
                 for a in range(PASSES):
-                    for c0 in range(0, width, step):
-                        codes, scales = v_operand(a, j0 + c0, step)
-                        nc.tensor.matmul_mx(
-                            out=y[:, i * width + c0 : i * width + c0 + step],
-                            lhsT=w4_codes[:, a, 2 * n0 : 2 * (n0 + P)].bitcast(FP4X4),
-                            lhsT_scale=moved_v2[:, a, S + n0 : S + n0 + P],
-                            rhs=codes.bitcast(FP8X4),
-                            rhs_scale=scales,
-                            start=(i == 0 and a == 0 and c0 == 0),
-                            stop=False,
-                        )
+                    codes, scales = v_operand(a, j0, width)
+                    nc.tensor.matmul_mx(
+                        out=y_acc[j0][tile // share][:, tile % share, :],
+                        lhsT=w4_codes[:, a, 2 * n0 : 2 * (n0 + P)].bitcast(FP4X4),
+                        lhsT_scale=w4_planes[:, a, n0 : n0 + P],
+                        rhs=codes.bitcast(FP8X4),
+                        rhs_scale=scales,
+                        start=(tile % share == 0 and a == 0),
+                        stop=False,
+                    )
 
-        def read_map(j0, width, unit, tiles=range(N // P)):
+        def read_map(j0, width, b, tile):
             share = HALF // width
-            first, b = j0 - unit[0], unit[2]
-            for tile in tiles:
-                y, i, n0 = y_acc[j0][tile // share], tile % share, tile * P
-                nc.tensor.matmul_mx(
-                    out=y[:, i * width : (i + 1) * width],
-                    lhsT=val_mx[b][0][:, n0 : n0 + P].bitcast(FP8X4),
-                    lhsT_scale=val_mx[b][1][:, n0 : n0 + P],
-                    rhs=e_mx[unit][0][:, first : first + width].bitcast(FP8X4),
-                    rhs_scale=e_mx[unit][1][:, first : first + width],
-                    start=False,
-                    stop=(b == PASSES - 1 and i == share - 1),
-                )
+            n0 = tile * P
+            codes, scales = e_mx[j0, b]
+            nc.tensor.matmul_mx(
+                out=y_acc[j0][tile // share][:, tile % share, :],
+                lhsT=val_mx[b][0][:, n0 : n0 + P].bitcast(FP8X4),
+                lhsT_scale=val_mx[b][1][:, n0 : n0 + P],
+                rhs=codes.bitcast(FP8X4),
+                rhs_scale=scales,
+                start=False,
+                stop=(b == PASSES - 1 and tile % share == share - 1),
+            )
 
-        def finish(j0, width, banks):
+        out_rows = out.rearrange("(n p) j -> p n j", p=P)
+
+        def finish(j0, width, first_tile, tiles, queue):
             share = HALF // width
-            for i in banks:
-                y = y_acc[j0][i]
-                last = j0 + width == S and i == len(y_acc[j0]) - 1
-                tiles = 1 if last else share
-                for first in range(0, share, tiles):
-                    result = keep.tile([P, tiles, width], F32, name=f"result{j0}_{i}_{first}")
-                    sums = y[:, first * width : (first + tiles) * width].rearrange("p (n j) -> p n j", n=tiles)
-                    nc.scalar.activation(out=result[:], in_=sums, func=ACT.Silu)
-                    tile = share * i + first
-                    queue = nc.scalar if last and first else nc.sync
-                    queue.dma_start(out=out_rows[:, tile : tile + tiles, j0 : j0 + width], in_=result[:])
+            sums = y_acc[j0][first_tile // share][:, first_tile % share : first_tile % share + tiles, :]
+            result = keep.tile([P, tiles, width], F32, name=f"result{j0}_{first_tile}")
+            nc.scalar.activation(out=result[:], in_=sums, func=ACT.Silu)
+            queue.dma_start(out=out_rows[:, first_tile : first_tile + tiles, j0 : j0 + width], in_=result[:])
 
-        open_score(left0, 0)
-        for t in range(PACK):
-            pass_v2(e_acc[left0][t], 0, 0, t, *v_operand(0, 0, HALF))
-        for first in (0, QUARTER):
-            for t in range(PACK):
-                columns = e_acc[left0][t][:, first : first + QUARTER]
-                pass_v2(columns, 1, 0, t, *v_operand(1, first, QUARTER), closes=first > 0)
-        score(left1, 4)
-        offset(left0)
-        weave_e(left0, scalar_weave)
-        score(right0, 0)
-        offset(left1)
-        weave_e(left1, scalar_weave)
-        own_codes(0, HALF, 4)
-        val_mx[0] = quantize(val_woven[0], "val0", 18)
-        quantize_e(left0)
-        read_map(0, HALF, left0)
-        offset(right0)
-        weave_e(right0, scalar_weave)
-        score(third1, 0)
-        score(fourth1, 2)
-        val_mx[1] = quantize(val_woven[1], "val1", 26)
-        quantize_e(left1, 28)
-        read_map(0, HALF, left1)
-        finish(0, HALF, range(4))
-        offset(third1)
-        own_codes(HALF, QUARTER, 0)
-        offset(fourth1)
-        own_codes(HALF + QUARTER, QUARTER, 2)
-        weave_e(third1, vector_weave, 38)
-        quantize_e(right0, 40)
-        quantize_e(third1)
-        weave_e(fourth1, vector_weave)
-        quantize_e(fourth1)
-        for j0, unit in ((HALF, third1), (HALF + QUARTER, fourth1)):
-            for i in range(2):
-                read_map(j0, QUARTER, right0, (2 * i, 2 * i + 1))
-                read_map(j0, QUARTER, unit, (2 * i, 2 * i + 1))
-                finish(j0, QUARTER, (i,))
+        left = [(0, HALF, b) for b in range(PASSES)]
+        quarters = (HALF, HALF + QUARTER)
+        for b in range(PASSES):
+            open_score(left[b], PACK * b)
+        for a in range(PASSES):
+            for b in range(PASSES):
+                for t in range(PACK):
+                    score_pass(left[b], a, t)
+        for b in range(PASSES):
+            scale_out(left[b])
+        for i, j0 in enumerate(quarters):
+            for b in range(PASSES):
+                unit = (j0, QUARTER, b)
+                open_score(unit, 4 * i + 2 * b)
+                for t in range(PACK):
+                    for a in range(PASSES):
+                        score_pass(unit, a, t)
+                scale_out(unit)
+
+        left_woven = [sbuf([P, HALF, PACK], BF16, f"e_woven0_{b}") for b in range(PASSES)]
+        quarter_woven = {j0: sbuf([P, PASSES, QUARTER, PACK], BF16, f"e_woven{j0}") for j0 in quarters}
+
+        def quantize_left(b):
+            codes, scales = quantize(left_woven[b][:].rearrange("p c t -> p (c t)"), HALF, f"e0_{b}")
+            e_mx[0, b] = codes[:], scales
+
+        def quantize_quarter(j0):
+            codes, scales = quantize(quarter_woven[j0][:].rearrange("p b c t -> p (b c t)"), HALF, f"e{j0}")
+            for b in range(PASSES):
+                e_mx[j0, b] = codes[:, b * QUARTER : (b + 1) * QUARTER], scales[:, b * QUARTER : (b + 1) * QUARTER]
+
+        def add_quarter(j0, b):
+            add_prior((j0, QUARTER, b), quarter_woven[j0][:, b, :, :])
+
+        third, fourth = quarters
+        add_prior(left[0], left_woven[0][:])
+        add_prior(left[1], left_woven[1][:])
+        quantize_left(0)
+        quantize_left(1)
+        add_quarter(third, 0)
+        add_quarter(third, 1)
+        add_quarter(fourth, 0)
+        quantize_quarter(third)
+        add_quarter(fourth, 1)
+        quantize_quarter(fourth)
+
+        own_codes(0, HALF, 0)
+        for b in range(PASSES):
+            for tile in range(TILES):
+                read_map(0, HALF, b, tile)
+        for tile in range(TILES):
+            finish(0, HALF, tile, 1, nc.sync)
+        for i, j0 in enumerate(quarters):
+            own_codes(j0, QUARTER, 4 + 2 * i)
+            for first_tile in (0, 2):
+                for b in range(PASSES):
+                    for tile in (first_tile, first_tile + 1):
+                        read_map(j0, QUARTER, b, tile)
+                if j0 == fourth and first_tile:
+                    finish(j0, QUARTER, first_tile, 1, nc.sync)
+                    finish(j0, QUARTER, first_tile + 1, 1, nc.scalar)
+                else:
+                    finish(j0, QUARTER, first_tile, 2, nc.sync)

@@ -26,6 +26,7 @@ QUARTER = 256
 TILES = N // P
 LIST_ROWS = 16
 SCALAR_CAST = 336
+EARLY = 2
 KIB = 1024
 
 
@@ -70,25 +71,25 @@ def tile_list_splice_map_reading_kernel(
             nc.sync.dma_start(out=window[:], in_=words[a].rearrange("p t i -> p (t i)").bitcast(I32))
             return window
 
-        def load_wv(queue, a, planes):
+        def load_wv(queue, a):
             rows = wv[a * PASS : (a + 1) * PASS, :].rearrange("(p t) n -> p t n", t=PACK)
-            queue.dma_start(out=wv_raw[a][:, planes, :], in_=rows[:, planes, :])
+            queue.dma_start(out=wv_raw[a][:], in_=rows)
 
-        def load_prior(h, b, kib):
-            rows = sbuf([P, PACK, HALF], F32, f"prior{h}_{b}", kib)
+        def load_prior(h, b, kib, t0=0, planes=PACK):
+            rows = sbuf([P, planes, HALF], F32, f"prior{h}_{b}_{t0}", kib)
             source = prior[b * PASS : (b + 1) * PASS, h * HALF : (h + 1) * HALF].rearrange("(p t) j -> p t j", t=PACK)
-            nc.sync.dma_start(out=rows[:], in_=source)
+            nc.sync.dma_start(out=rows[:], in_=source[:, t0 : t0 + planes, :])
             return rows
 
         def move_rows(queue, moved, source, step):
-            for d in range(4):
+            for d in (0, 2, 1, 3):
                 queue.dma_start(
                     out=moved[32 * d : 32 * d + 4, :, :].bitcast(I32),
                     in_=source[8 * step * d : 8 * step * (d + 1) : step, :].bitcast(I32),
                 )
 
         v2_scale_window = sbuf([P, T], U8, "v2_scale_window", 15)
-        v_scale_window = sbuf([P, T], U8, "v_scale_window", 34)
+        v_scale_window = sbuf([P, T], U8, "v_scale_window", 35)
         moved_v2 = sbuf([P, PASSES, S], U8, "moved_v2")
         moved_v = sbuf([P, PASSES, S], U8, "moved_v")
         gain_rows = sbuf([P, PASS], F32, "gain_rows")
@@ -104,23 +105,22 @@ def tile_list_splice_map_reading_kernel(
         nc.gpsimd.memset(moved_v[:].bitcast(I32), 0)
 
         wv_raw = [sbuf([P, PACK, N], F32, f"wv_raw{a}", kib) for a, kib in enumerate((40, 48))]
-        load_wv(nc.scalar, 0, slice(0, 1))
         list2 = keep.tile([P, S // LIST_ROWS], U16)
         nc.sync.dma_start(list2[:], offs2)
-        nc.sync.dma_start(
+        nc.scalar.dma_start(
             out=v2_scale_window[:32, :].bitcast(I32), in_=tab2_scales.bitcast(I32).rearrange("a q t -> q a t")
         )
+        load_wv(nc.scalar, 0)
         lists = keep.tile([P, S // LIST_ROWS], U16)
         nc.sync.dma_start(lists[:], offs)
         nc.sync.dma_start(
             out=v_scale_window[0:P:4, :].bitcast(I32), in_=tab_scales.bitcast(I32).rearrange("a q t -> q a t")
         )
-        load_wv(nc.sync, 0, slice(1, PACK))
         nc.scalar.activation(out=warm[:, 1:2], in_=warm[:, 0:1], func=ACT.Silu)
         for i, gain in enumerate((gv, gm)):
             nc.sync.dma_start(out=gain_rows[PASSES * i : PASSES * (i + 1), :], in_=gain.rearrange("(b c) -> b c", b=PASSES))
         v2_windows = [load_words(tab2_words, 0, "v2_window0", 0)]
-        load_wv(nc.sync, 1, slice(0, PACK))
+        load_wv(nc.sync, 1)
         turned = bank(7, [P, PACK, P])
         for t in range(PACK):
             nc.tensor.transpose(turned[:, t, :], gain_rows[:, t:PASS:PACK], identity[:])
@@ -138,7 +138,7 @@ def tile_list_splice_map_reading_kernel(
         v_scales_listed = sbuf([P, S], U8, "v_scales_listed")
         nc.vector.tensor_copy(out=v_scales_listed[:], in_=v_scale_window[:].indirect(lists[:]))
         move_rows(nc.sync, moved_v, v_scales_listed, 4)
-        v_windows.append(load_words(tab_words, 1, "v_window1", 27))
+        v_windows.append(load_words(tab_words, 1, "v_window1", 28))
 
         cols = HALF // LIST_ROWS
         v2_codes = {}
@@ -151,7 +151,7 @@ def tile_list_splice_map_reading_kernel(
             )
             v2_codes[a, b] = codes
 
-        def pass_v2(acc, a, b, t, codes, scales):
+        def pass_v2(acc, a, b, t, codes, scales, opening=0, closes=True):
             first = b * PASS + t * P
             nc.tensor.matmul_mx(
                 out=acc,
@@ -159,8 +159,8 @@ def tile_list_splice_map_reading_kernel(
                 lhsT_scale=moved_v2[:, a, first : first + P],
                 rhs=codes.bitcast(FP8X4),
                 rhs_scale=scales,
-                start=(a == 0),
-                stop=(a == PASSES - 1),
+                start=(a == opening),
+                stop=(a != opening and closes),
             )
 
         w4_planes = sbuf([P, PASSES, N], U8, "w4_planes")
@@ -190,37 +190,42 @@ def tile_list_splice_map_reading_kernel(
                     out=val_planes[b][:, t, :], in_=val_acc[b, t][:], func=ACT.Copy, scale=gains[:, t, b : b + 1]
                 )
 
-        prior_rows = {(0, 0): load_prior(0, 0, 0), (0, 1): load_prior(0, 1, 8)}
-        w4_codes = sbuf([P, PASSES, 2 * N], U8, "w4_codes", 16)
+        prior_pairs = [load_prior(0, 1, 2 * t0, t0, 2) for t0 in (0, 2)]
+        prior_rows = {(0, 0): load_prior(0, 0, 8)}
+        w4_codes = sbuf([P, PASSES, 2 * N], U8, "w4_codes", 52)
         nc.sync.dma_start(out=w4_codes[:].bitcast(I32), in_=w4_words.bitcast(I32).rearrange("a p c -> p a c"))
         w4_rows = w4_scales.bitcast(I32).rearrange("a q c -> q a c")
         for d in range(4):
             nc.sync.dma_start(out=w4_planes[32 * d : 32 * d + 4, :, :].bitcast(I32), in_=w4_rows[4 * d : 4 * d + 4])
 
-        val_woven = [sbuf([P, N, PACK], BF16, f"val_woven{b}", kib) for b, kib in enumerate((None, 27))]
-        gpsimd_weave(val_woven[0][:], val_planes[0][:])
+        val_woven = [sbuf([P, N, PACK], BF16, f"val_woven{b}", None) for b in range(PASSES)]
+        for b in range(PASSES):
+            gpsimd_weave(val_woven[b][:], val_planes[b][:])
 
         v_codes = {}
         for a in range(PASSES):
             for h in range(S // HALF):
                 codes = sbuf([P, HALF], U32, f"v_codes{a}_{h}")
-                nc.vector.tensor_copy(
-                    out=codes[:], in_=v_windows[a][:].bitcast(U32).indirect(lists[:, h * cols : (h + 1) * cols])
-                )
+                step = QUARTER if (a, h) == (1, 0) else HALF
+                for first in range(0, HALF, step):
+                    entry = (h * HALF + first) // LIST_ROWS
+                    offsets = lists[:, entry : entry + step // LIST_ROWS]
+                    nc.vector.tensor_copy(
+                        out=codes[:, first : first + step], in_=v_windows[a][:].bitcast(U32).indirect(offsets)
+                    )
                 v_codes[a, h] = codes
-        for b in range(PASSES):
-            prior_rows[1, b] = load_prior(1, b, 19 + 14 * b)
+        prior_rows[1, 0] = load_prior(1, 0, 16)
+        prior_rows[1, 1] = load_prior(1, 1, 34)
+        val_mx = {}
 
-        nc.vector.tensor_copy(out=woven_walk(val_woven[1][:], PACK), in_=plane_walk(val_planes[1][:], PACK))
-        val_mx = [
-            quantize(val_woven[b][:].rearrange("p c t -> p (c t)"), N, f"val{b}", kib) for b, kib in enumerate((31, None))
-        ]
+        def quantize_val(b, kib):
+            val_mx[b] = quantize(val_woven[b][:].rearrange("p c t -> p (c t)"), N, f"val{b}", kib)
 
         def v_operand(a, j0, width):
             h, first = divmod(j0, HALF)
             return v_codes[a, h][:, first : first + width], moved_v[:, a, j0 : j0 + width]
 
-        e_acc, e_scaled, e_mx, y_acc = {}, {}, {}, {}
+        e_acc, e_scaled, e_mx, y_acc, shares = {}, {}, {}, {}, {}
 
         def open_score(unit, first_bank):
             width = unit[1]
@@ -228,9 +233,9 @@ def tile_list_splice_map_reading_kernel(
             tiles = [bank(first_bank + i, [P, share, width]) for i in range(PACK // share)]
             e_acc[unit] = [tiles[t // share][:, t % share, :] for t in range(PACK)]
 
-        def score_pass(unit, a, t):
+        def score_pass(unit, a, t, opening):
             j0, width, b = unit
-            pass_v2(e_acc[unit][t], a, b, t, *v_operand(a, j0, width))
+            pass_v2(e_acc[unit][t], a, b, t, *v_operand(a, j0, width), opening)
 
         def scale_out(unit):
             j0, width, b = unit
@@ -239,19 +244,20 @@ def tile_list_splice_map_reading_kernel(
                 gain = gains[:, t, PASSES + b : PASSES + b + 1]
                 nc.scalar.activation(out=e_scaled[unit][:, t, :], in_=e_acc[unit][t], func=ACT.Copy, scale=gain)
 
-        def add_prior(unit, woven):
-            j0, width, b = unit
+        def add_prior(unit, woven, skip=0):
+            j0, width, b = unit[0] + skip, woven.shape[1], unit[2]
             h, first = divmod(j0, HALF)
             nc.vector.tensor_tensor(
                 out=woven_walk(woven, 2),
-                in0=plane_walk(e_scaled[unit][:], 2),
+                in0=plane_walk(e_scaled[unit][:, :, skip : skip + width], 2),
                 in1=plane_walk(prior_rows[h, b][:, :, first : first + width], 2),
                 op=ALU.add,
             )
 
-        def own_codes(j0, width, first_bank):
-            share = HALF // width
-            y_acc[j0] = [bank(first_bank + i, [P, share, width]) for i in range(TILES // share)]
+        def own_codes(j0, width, banks):
+            share = TILES // len(banks)
+            shares[j0] = share
+            y_acc[j0] = [bank(i, [P, share, width]) for i in banks]
             for tile in range(TILES):
                 n0 = tile * P
                 for a in range(PASSES):
@@ -267,7 +273,7 @@ def tile_list_splice_map_reading_kernel(
                     )
 
         def read_map(j0, width, b, tile):
-            share = HALF // width
+            share = shares[j0]
             n0 = tile * P
             codes, scales = e_mx[j0, b]
             nc.tensor.matmul_mx(
@@ -283,7 +289,7 @@ def tile_list_splice_map_reading_kernel(
         out_rows = out.rearrange("(n p) j -> p n j", p=P)
 
         def finish(j0, width, first_tile, tiles, queue):
-            share = HALF // width
+            share = shares[j0]
             sums = y_acc[j0][first_tile // share][:, first_tile % share : first_tile % share + tiles, :]
             result = keep.tile([P, tiles, width], F32, name=f"result{j0}_{first_tile}")
             nc.scalar.activation(out=result[:], in_=sums, func=ACT.Silu)
@@ -293,62 +299,91 @@ def tile_list_splice_map_reading_kernel(
         quarters = (HALF, HALF + QUARTER)
         for b in range(PASSES):
             open_score(left[b], PACK * b)
-        for a in range(PASSES):
-            for b in range(PASSES):
-                for t in range(PACK):
-                    score_pass(left[b], a, t)
+        for t in range(PACK):
+            score_pass(left[0], 0, t, 0)
+        for t in range(EARLY):
+            score_pass(left[1], 0, t, 0)
+        for first in (0, QUARTER):
+            for t in range(PACK):
+                columns = e_acc[left[0]][t][:, first : first + QUARTER]
+                pass_v2(columns, 1, 0, t, *v_operand(1, first, QUARTER), 0, first > 0)
+        for t in range(EARLY):
+            score_pass(left[1], 1, t, 0)
+        for t in range(EARLY, PACK):
+            for a in (1, 0):
+                score_pass(left[1], a, t, 1)
+        scale_out(left[0])
+        planes = sbuf([P, PACK, HALF], BF16, "e_planes")
+        for t in range(PACK):
+            nc.vector.scalar_tensor_tensor(
+                out=planes[:, t, :],
+                in0=e_acc[left[1]][t],
+                scalar=gains[:, t, PASSES + 1 : PASSES + 2],
+                in1=prior_pairs[t // 2][:, t % 2, :],
+                op0=ALU.mult,
+                op1=ALU.add,
+            )
+        left_woven = [sbuf([P, HALF, PACK], BF16, f"e_woven0_{b}", kib) for b, kib in enumerate((0, None))]
+        right = [(HALF, HALF, b) for b in range(PASSES)]
         for b in range(PASSES):
-            scale_out(left[b])
-        for i, j0 in enumerate(quarters):
-            for b in range(PASSES):
-                unit = (j0, QUARTER, b)
-                open_score(unit, 4 * i + 2 * b)
-                for t in range(PACK):
-                    for a in range(PASSES):
-                        score_pass(unit, a, t)
-                scale_out(unit)
+            open_score(right[b], PACK * b)
+            for t in range(PACK):
+                for a in range(PASSES):
+                    score_pass(right[b], a, t, 0)
+            scale_out(right[b])
+            if b == 0:
+                nc.scalar.copy(out=woven_walk(left_woven[1][:], PACK), in_=plane_walk(planes[:], PACK))
+        right_woven = [sbuf([P, HALF, PACK], BF16, f"e_woven1_{b}") for b in range(PASSES)]
 
-        left_woven = [sbuf([P, HALF, PACK], BF16, f"e_woven0_{b}") for b in range(PASSES)]
-        quarter_woven = {j0: sbuf([P, PASSES, QUARTER, PACK], BF16, f"e_woven{j0}") for j0 in quarters}
+        third = (HALF, QUARTER)
+        eighths = ((HALF + QUARTER, P), (HALF + QUARTER + P, P))
 
-        def quantize_left(b):
-            codes, scales = quantize(left_woven[b][:].rearrange("p c t -> p (c t)"), HALF, f"e0_{b}")
-            e_mx[0, b] = codes[:], scales
+        def quantize_e(woven, b, pieces):
+            width = woven.shape[1]
+            codes, scales = quantize(woven.rearrange("p c t -> p (c t)"), width, f"e{pieces[0][0]}_{b}")
+            for j0, piece in pieces:
+                first = j0 - pieces[0][0]
+                e_mx[j0, b] = codes[:, first : first + piece], scales[:, first : first + piece]
 
-        def quantize_quarter(j0):
-            codes, scales = quantize(quarter_woven[j0][:].rearrange("p b c t -> p (b c t)"), HALF, f"e{j0}")
-            for b in range(PASSES):
-                e_mx[j0, b] = codes[:, b * QUARTER : (b + 1) * QUARTER], scales[:, b * QUARTER : (b + 1) * QUARTER]
+        def last_unit(piece):
+            first = piece[0] - HALF
+            return right_woven[1][:, first : first + piece[1], :]
 
-        def add_quarter(j0, b):
-            add_prior((j0, QUARTER, b), quarter_woven[j0][:, b, :, :])
+        def add_last(piece):
+            add_prior(right[1], last_unit(piece), piece[0] - HALF)
 
-        third, fourth = quarters
         add_prior(left[0], left_woven[0][:])
-        add_prior(left[1], left_woven[1][:])
-        quantize_left(0)
-        quantize_left(1)
-        add_quarter(third, 0)
-        add_quarter(third, 1)
-        add_quarter(fourth, 0)
-        quantize_quarter(third)
-        add_quarter(fourth, 1)
-        quantize_quarter(fourth)
+        quantize_val(0, 4)
+        quantize_val(1, 6)
+        quantize_e(left_woven[0][:], 0, [(0, HALF)])
+        quantize_e(left_woven[1][:], 1, [(0, HALF)])
+        add_prior(right[0], right_woven[0][:])
+        add_last(third)
+        quantize_e(right_woven[0][:], 0, [third, *eighths])
+        add_last(eighths[0])
+        quantize_e(last_unit(third), 1, [third])
+        add_last(eighths[1])
+        for piece in eighths:
+            quantize_e(last_unit(piece), 1, [piece])
 
-        own_codes(0, HALF, 0)
+        own_codes(0, HALF, (0, 1, 2, 3))
         for b in range(PASSES):
             for tile in range(TILES):
                 read_map(0, HALF, b, tile)
         for tile in range(TILES):
             finish(0, HALF, tile, 1, nc.sync)
-        for i, j0 in enumerate(quarters):
-            own_codes(j0, QUARTER, 4 + 2 * i)
-            for first_tile in (0, 2):
-                for b in range(PASSES):
-                    for tile in (first_tile, first_tile + 1):
-                        read_map(j0, QUARTER, b, tile)
-                if j0 == fourth and first_tile:
-                    finish(j0, QUARTER, first_tile, 1, nc.sync)
-                    finish(j0, QUARTER, first_tile + 1, 1, nc.scalar)
-                else:
-                    finish(j0, QUARTER, first_tile, 2, nc.sync)
+        own_codes(*third, (6, 7))
+        own_codes(*eighths[0], (0,))
+        for first_tile in (0, 2):
+            for b in range(PASSES):
+                for tile in (first_tile, first_tile + 1):
+                    read_map(*third, b, tile)
+            finish(*third, first_tile, 2, nc.sync)
+        own_codes(*eighths[1], (1, 2))
+        for piece in eighths:
+            for b in range(PASSES):
+                for tile in range(TILES):
+                    read_map(*piece, b, tile)
+        finish(*eighths[0], 0, TILES, nc.sync)
+        finish(*eighths[1], 0, 2, nc.sync)
+        finish(*eighths[1], 2, 2, nc.scalar)

@@ -75,9 +75,9 @@ def tile_list_splice_map_reading_kernel(
             rows = wv[a * PASS : (a + 1) * PASS, :].rearrange("(p t) n -> p t n", t=PACK)
             queue.dma_start(out=wv_raw[a][:], in_=rows)
 
-        def load_prior(h, b, kib, t0=0, planes=PACK):
-            rows = sbuf([P, planes, HALF], F32, f"prior{h}_{b}_{t0}", kib)
-            source = prior[b * PASS : (b + 1) * PASS, h * HALF : (h + 1) * HALF].rearrange("(p t) j -> p t j", t=PACK)
+        def load_prior(j0, width, b, kib, t0=0, planes=PACK):
+            rows = sbuf([P, planes, width], F32, f"prior{j0}_{b}_{t0}", kib)
+            source = prior[b * PASS : (b + 1) * PASS, j0 : j0 + width].rearrange("(p t) j -> p t j", t=PACK)
             nc.sync.dma_start(out=rows[:], in_=source[:, t0 : t0 + planes, :])
             return rows
 
@@ -190,8 +190,8 @@ def tile_list_splice_map_reading_kernel(
                     out=val_planes[b][:, t, :], in_=val_acc[b, t][:], func=ACT.Copy, scale=gains[:, t, b : b + 1]
                 )
 
-        prior_pairs = [load_prior(0, 1, 2 * t0, t0, 2) for t0 in (0, 2)]
-        prior_rows = {(0, 0): load_prior(0, 0, 8)}
+        prior_pairs = [load_prior(0, HALF, 1, 2 * t0, t0, 2) for t0 in (0, 2)]
+        prior_rows = {(0, 0): load_prior(0, HALF, 0, 8)}
         w4_codes = sbuf([P, PASSES, 2 * N], U8, "w4_codes", 52)
         nc.sync.dma_start(out=w4_codes[:].bitcast(I32), in_=w4_words.bitcast(I32).rearrange("a p c -> p a c"))
         w4_rows = w4_scales.bitcast(I32).rearrange("a q c -> q a c")
@@ -214,8 +214,9 @@ def tile_list_splice_map_reading_kernel(
                         out=codes[:, first : first + step], in_=v_windows[a][:].bitcast(U32).indirect(offsets)
                     )
                 v_codes[a, h] = codes
-        prior_rows[1, 0] = load_prior(1, 0, 16)
-        prior_rows[1, 1] = load_prior(1, 1, 34)
+        prior_rows[HALF, 0] = load_prior(HALF, HALF, 0, 16)
+        prior_rows[HALF, 1] = load_prior(HALF, QUARTER, 1, 28)
+        prior_rows[HALF + QUARTER, 1] = load_prior(HALF + QUARTER, QUARTER, 1, 32)
         val_mx = {}
 
         def quantize_val(b, kib):
@@ -246,19 +247,18 @@ def tile_list_splice_map_reading_kernel(
 
         def add_prior(unit, woven, skip=0):
             j0, width, b = unit[0] + skip, woven.shape[1], unit[2]
-            h, first = divmod(j0, HALF)
             nc.vector.tensor_tensor(
                 out=woven_walk(woven, 2),
                 in0=plane_walk(e_scaled[unit][:, :, skip : skip + width], 2),
-                in1=plane_walk(prior_rows[h, b][:, :, first : first + width], 2),
+                in1=plane_walk(prior_rows[j0, b][:], 2),
                 op=ALU.add,
             )
 
-        def own_codes(j0, width, banks):
-            share = TILES // len(banks)
+        def own_codes(j0, width, index, tiles):
+            share = len(tiles)
             shares[j0] = share
-            y_acc[j0] = [bank(i, [P, share, width]) for i in banks]
-            for tile in range(TILES):
+            y_acc.setdefault(j0, []).append(bank(index, [P, share, width]))
+            for tile in tiles:
                 n0 = tile * P
                 for a in range(PASSES):
                     codes, scales = v_operand(a, j0, width)
@@ -335,8 +335,7 @@ def tile_list_splice_map_reading_kernel(
                 nc.scalar.copy(out=woven_walk(left_woven[1][:], PACK), in_=plane_walk(planes[:], PACK))
         right_woven = [sbuf([P, HALF, PACK], BF16, f"e_woven1_{b}") for b in range(PASSES)]
 
-        third = (HALF, QUARTER)
-        eighths = ((HALF + QUARTER, P), (HALF + QUARTER + P, P))
+        quarters = ((HALF, QUARTER), (HALF + QUARTER, QUARTER))
 
         def quantize_e(woven, b, pieces):
             width = woven.shape[1]
@@ -349,41 +348,42 @@ def tile_list_splice_map_reading_kernel(
             first = piece[0] - HALF
             return right_woven[1][:, first : first + piece[1], :]
 
-        def add_last(piece):
-            add_prior(right[1], last_unit(piece), piece[0] - HALF)
-
         add_prior(left[0], left_woven[0][:])
         quantize_val(0, 4)
         quantize_val(1, 6)
         quantize_e(left_woven[0][:], 0, [(0, HALF)])
         quantize_e(left_woven[1][:], 1, [(0, HALF)])
         add_prior(right[0], right_woven[0][:])
-        add_last(third)
-        quantize_e(right_woven[0][:], 0, [third, *eighths])
-        add_last(eighths[0])
-        quantize_e(last_unit(third), 1, [third])
-        add_last(eighths[1])
-        for piece in eighths:
-            quantize_e(last_unit(piece), 1, [piece])
+        add_prior(right[1], last_unit(quarters[0]), 0)
+        quantize_e(right_woven[0][:], 0, quarters)
+        quantize_e(last_unit(quarters[0]), 1, [quarters[0]])
+        add_prior(right[1], last_unit(quarters[1]), QUARTER)
+        quantize_e(last_unit(quarters[1]), 1, [quarters[1]])
 
-        own_codes(0, HALF, (0, 1, 2, 3))
+        for tile in range(TILES):
+            own_codes(0, HALF, tile, (tile,))
         for b in range(PASSES):
             for tile in range(TILES):
                 read_map(0, HALF, b, tile)
         for tile in range(TILES):
             finish(0, HALF, tile, 1, nc.sync)
-        own_codes(*third, (6, 7))
-        own_codes(*eighths[0], (0,))
-        for first_tile in (0, 2):
+        third, fourth = quarters
+        pairs = ((0, 1), (2, 3))
+        for i, pair in enumerate(pairs):
+            own_codes(*third, 4 + i, pair)
+        own_codes(*fourth, 6, pairs[0])
+        for pair in pairs:
             for b in range(PASSES):
-                for tile in (first_tile, first_tile + 1):
+                for tile in pair:
                     read_map(*third, b, tile)
-            finish(*third, first_tile, 2, nc.sync)
-        own_codes(*eighths[1], (1, 2))
-        for piece in eighths:
-            for b in range(PASSES):
-                for tile in range(TILES):
-                    read_map(*piece, b, tile)
-        finish(*eighths[0], 0, TILES, nc.sync)
-        finish(*eighths[1], 0, 2, nc.sync)
-        finish(*eighths[1], 2, 2, nc.scalar)
+            finish(*third, pair[0], 2, nc.sync)
+        for tile in pairs[0]:
+            read_map(*fourth, 0, tile)
+        own_codes(*fourth, 1, pairs[1])
+        for tile in pairs[1]:
+            read_map(*fourth, 0, tile)
+        for tile in range(TILES):
+            read_map(*fourth, 1, tile)
+        finish(*fourth, 0, 2, nc.sync)
+        finish(*fourth, 2, 1, nc.sync)
+        finish(*fourth, 3, 1, nc.scalar)

@@ -41,8 +41,8 @@ def tile_list_splice_map_reading_kernel(
 
         def sbuf(shape, dtype, name, kib=None):
             if kib is None:
-                return keep.tile(shape, dtype, name=name, align_bytes=64)
-            return shared.tile(shape, dtype, name=name, offset=int(kib * KIB), align_bytes=64)
+                return keep.tile(shape, dtype, name=name, align_bytes=256)
+            return shared.tile(shape, dtype, name=name, offset=int(kib * KIB), align_bytes=256)
 
         def bank(index, shape):
             return psum.tile(shape, F32, name=f"bank{index}", tag=f"bank{index}")

@@ -355,9 +355,10 @@ def tile_list_splice_map_reading_kernel(
         quantize_e(left_woven[1][:], 1, [(0, HALF)])
         add_prior(right[0], right_woven[0][:])
         add_prior(right[1], last_unit(quarters[0]), 0)
-        quantize_e(right_woven[0][:], 0, quarters)
+        quantize_e(right_woven[0][:, :QUARTER, :], 0, [quarters[0]])
         quantize_e(last_unit(quarters[0]), 1, [quarters[0]])
         add_prior(right[1], last_unit(quarters[1]), QUARTER)
+        quantize_e(right_woven[0][:, QUARTER:, :], 0, [quarters[1]])
         quantize_e(last_unit(quarters[1]), 1, [quarters[1]])
 
         for tile in range(TILES):
@@ -371,19 +372,17 @@ def tile_list_splice_map_reading_kernel(
         pairs = ((0, 1), (2, 3))
         for i, pair in enumerate(pairs):
             own_codes(*third, 4 + i, pair)
-        own_codes(*fourth, 6, pairs[0])
+        last_banks = (6, 7, 1, 2)
+        for tile in pairs[0]:
+            own_codes(*fourth, last_banks[tile], (tile,))
         for pair in pairs:
             for b in range(PASSES):
                 for tile in pair:
                     read_map(*third, b, tile)
             finish(*third, pair[0], 2, nc.sync)
-        for tile in pairs[0]:
-            read_map(*fourth, 0, tile)
-        own_codes(*fourth, 1, pairs[1])
         for tile in pairs[1]:
-            read_map(*fourth, 0, tile)
+            own_codes(*fourth, last_banks[tile], (tile,))
         for tile in range(TILES):
-            read_map(*fourth, 1, tile)
-        finish(*fourth, 0, 2, nc.sync)
-        finish(*fourth, 2, 1, nc.sync)
-        finish(*fourth, 3, 1, nc.scalar)
+            for b in range(PASSES):
+                read_map(*fourth, b, tile)
+            finish(*fourth, tile, 1, nc.scalar if tile == TILES - 1 else nc.sync)

@@ -96,8 +96,8 @@ def tile_list_splice_map_reading_kernel(
         identity = sbuf([P, P], F32, "identity")
         nc.gpsimd.memset(v_scale_window[:].bitcast(I32), 0)
         nc.vector.memset(gain_rows[:], 0.0)
-        nc.vector.memset(v2_scale_window[32:64, :].bitcast(I32), 0)
-        nc.vector.memset(v2_scale_window[64:, :].bitcast(I32), 0)
+        nc.gpsimd.memset(v2_scale_window[32:64, :].bitcast(I32), 0)
+        nc.gpsimd.memset(v2_scale_window[64:, :].bitcast(I32), 0)
         warm = keep.tile([P, 2], F32)
         nc.gpsimd.memset(warm[:], 0.0)
         make_identity(nc, identity[:])

@@ -95,11 +95,11 @@ def tile_list_splice_map_reading_kernel(
         gain_rows = sbuf([P, PASS], F32, "gain_rows")
         identity = sbuf([P, P], F32, "identity")
         nc.gpsimd.memset(v_scale_window[:].bitcast(I32), 0)
-        nc.vector.memset(gain_rows[:], 0.0)
         nc.gpsimd.memset(v2_scale_window[32:64, :].bitcast(I32), 0)
         nc.gpsimd.memset(v2_scale_window[64:, :].bitcast(I32), 0)
         warm = keep.tile([P, 2], F32)
         nc.gpsimd.memset(warm[:], 0.0)
+        nc.gpsimd.memset(gain_rows[:], 0.0)
         make_identity(nc, identity[:])
         nc.gpsimd.memset(moved_v2[:].bitcast(I32), 0)
         nc.gpsimd.memset(moved_v[:].bitcast(I32), 0)
@@ -117,9 +117,9 @@ def tile_list_splice_map_reading_kernel(
             out=v_scale_window[0:P:4, :].bitcast(I32), in_=tab_scales.bitcast(I32).rearrange("a q t -> q a t")
         )
         nc.scalar.activation(out=warm[:, 1:2], in_=warm[:, 0:1], func=ACT.Silu)
+        v2_windows = [load_words(tab2_words, 0, "v2_window0", 0)]
         for i, gain in enumerate((gv, gm)):
             nc.sync.dma_start(out=gain_rows[PASSES * i : PASSES * (i + 1), :], in_=gain.rearrange("(b c) -> b c", b=PASSES))
-        v2_windows = [load_words(tab2_words, 0, "v2_window0", 0)]
         load_wv(nc.sync, 1)
         turned = bank(7, [P, PACK, P])
         for t in range(PACK):

@@ -28,6 +28,7 @@ LIST_ROWS = 16
 SCALAR_CAST = 336
 EARLY = 2
 KIB = 1024
+STATIONARY_ROW = 4
 
 
 def tile_list_splice_map_reading_kernel(
@@ -81,10 +82,10 @@ def tile_list_splice_map_reading_kernel(
             nc.sync.dma_start(out=rows[:], in_=source[:, t0 : t0 + planes, :])
             return rows
 
-        def move_rows(queue, moved, source, step):
+        def move_rows(queue, moved, source, step, row):
             for d in (0, 2, 1, 3):
                 queue.dma_start(
-                    out=moved[32 * d : 32 * d + 4, :, :].bitcast(I32),
+                    out=moved[32 * d + row : 32 * d + row + 4, :, :].bitcast(I32),
                     in_=source[8 * step * d : 8 * step * (d + 1) : step, :].bitcast(I32),
                 )
 
@@ -132,12 +133,12 @@ def tile_list_splice_map_reading_kernel(
             out=v2_scales_listed[:].rearrange("p (b t c) -> p b c t", b=PASSES, t=PACK),
             in_=v2_scale_window[:].indirect(list2[:]),
         )
-        move_rows(nc.sync, moved_v2, v2_scales_listed, 1)
+        move_rows(nc.sync, moved_v2, v2_scales_listed, 1, STATIONARY_ROW)
         v2_windows.append(load_words(tab2_words, 1, "v2_window1", 8))
         v_windows = [load_words(tab_words, 0, "v_window0", 16)]
         v_scales_listed = sbuf([P, S], U8, "v_scales_listed")
         nc.vector.tensor_copy(out=v_scales_listed[:], in_=v_scale_window[:].indirect(lists[:]))
-        move_rows(nc.sync, moved_v, v_scales_listed, 4)
+        move_rows(nc.sync, moved_v, v_scales_listed, 4, 0)
         v_windows.append(load_words(tab_words, 1, "v_window1", 28))
 
         cols = HALF // LIST_ROWS
@@ -156,7 +157,7 @@ def tile_list_splice_map_reading_kernel(
             nc.tensor.matmul_mx(
                 out=acc,
                 lhsT=v2_codes[a, b][:, t, :].bitcast(FP8X4),
-                lhsT_scale=moved_v2[:, a, first : first + P],
+                lhsT_scale=moved_v2[STATIONARY_ROW:, a, first : first + P],
                 rhs=codes.bitcast(FP8X4),
                 rhs_scale=scales,
                 start=(a == opening),
@@ -220,7 +221,9 @@ def tile_list_splice_map_reading_kernel(
         val_mx = {}
 
         def quantize_val(b, kib):
-            val_mx[b] = quantize(val_woven[b][:].rearrange("p c t -> p (c t)"), N, f"val{b}", kib)
+            plane = sbuf([P, N], U8, f"val{b}_plane")
+            woven = val_woven[b][:].rearrange("p c t -> p (c t)")
+            val_mx[b] = quantize(woven, N, f"val{b}", kib, plane[STATIONARY_ROW:, :])
 
         def v_operand(a, j0, width):
             h, first = divmod(j0, HALF)
@@ -307,8 +310,8 @@ def tile_list_splice_map_reading_kernel(
             for t in range(PACK):
                 columns = e_acc[left[0]][t][:, first : first + QUARTER]
                 pass_v2(columns, 1, 0, t, *v_operand(1, first, QUARTER), 0, first > 0)
-        for t in range(EARLY):
-            score_pass(left[1], 1, t, 0)
+                if first > 0 and t % 2 == 1:
+                    score_pass(left[1], 1, t // 2, 0)
         for t in range(EARLY, PACK):
             for a in (1, 0):
                 score_pass(left[1], a, t, 1)
@@ -372,7 +375,7 @@ def tile_list_splice_map_reading_kernel(
         pairs = ((0, 1), (2, 3))
         for i, pair in enumerate(pairs):
             own_codes(*third, 4 + i, pair)
-        last_banks = (6, 7, 1, 2)
+        last_banks = (6, 7, 1, 5)
         for tile in pairs[0]:
             own_codes(*fourth, last_banks[tile], (tile,))
         for pair in pairs:
@@ -380,9 +383,10 @@ def tile_list_splice_map_reading_kernel(
                 for tile in pair:
                     read_map(*third, b, tile)
             finish(*third, pair[0], 2, nc.sync)
-        for tile in pairs[1]:
-            own_codes(*fourth, last_banks[tile], (tile,))
+        own_codes(*fourth, last_banks[2], (2,))
         for tile in range(TILES):
+            if tile == TILES - 1:
+                own_codes(*fourth, last_banks[tile], (tile,))
             for b in range(PASSES):
                 read_map(*fourth, b, tile)
             finish(*fourth, tile, 1, nc.scalar if tile == TILES - 1 else nc.sync)

from contextlib import ExitStack

import concourse.mybir as mybir
from concourse.masks import make_identity

K, T, S, N = 1024, 2048, 1024, 512
FLOPS = 2 * K * S * S + 2 * K * S * N + 2 * S * N * S + 2 * K * N * S

F32 = mybir.dt.float32
BF16 = mybir.dt.bfloat16
I32 = mybir.dt.int32
U32 = mybir.dt.uint32
U16 = mybir.dt.uint16
U8 = mybir.dt.uint8
FP8X4 = mybir.dt.float8_e4m3fn_x4
FP4X4 = mybir.dt.float4_e2m1fn_x4
ACT = mybir.ActivationFunctionType
ALU = mybir.AluOpType

P = 128
PACK = 4
PASS = P * PACK
PASSES = 2
HALF = 512
QUARTER = 256
TILES = N // P
LIST_ROWS = 16
SCALAR_CAST = 336
EARLY = 2
KIB = 1024
STATIONARY_ROW = 4


def tile_list_splice_map_reading_kernel(
    tc, tab_words, tab_scales, tab2_words, tab2_scales, offs, offs2, w4_words, w4_scales, wv, gm, gv, prior, out
):
    nc = tc.nc
    with ExitStack() as ctx:
        keep = ctx.enter_context(tc.tile_pool(name="keep", bufs=1))
        shared = ctx.enter_context(tc.tile_pool(name="shared", bufs=1))
        psum = ctx.enter_context(tc.psum_pool(name="psum", bufs=1))

        def sbuf(shape, dtype, name, kib=None):
            if kib is None:
                return keep.tile(shape, dtype, name=name, align_bytes=256)
            return shared.tile(shape, dtype, name=name, offset=int(kib * KIB), align_bytes=256)

        def bank(index, shape):
            return psum.tile(shape, F32, name=f"bank{index}", tag=f"bank{index}")

        def woven_walk(woven, run):
            return woven.rearrange("p (c i) t -> p c t i", i=run)

        def plane_walk(planes, run):
            return planes.rearrange("p t (c i) -> p c t i", i=run)

        def gpsimd_weave(woven, planes):
            nc.gpsimd.tensor_scalar(
                out=woven, in0=planes.rearrange("p t c -> p c t"), scalar1=1.0, scalar2=0.0, op0=ALU.mult, op1=ALU.add
            )

        def quantize(woven, width, name, kib=None, scales=None):
            codes = sbuf([P, width], U32, f"{name}_codes", kib)
            if scales is None:
                tile = sbuf([P, width], U8, f"{name}_scales")
                scales = tile[:]
            nc.vector.quantize_mx(out=codes[:].bitcast(FP8X4), scales=scales, in_=woven)
            return codes, scales

        def load_words(words, a, name, kib):
            window = sbuf([P, T], I32, name, kib)
            nc.sync.dma_start(out=window[:], in_=words[a].rearrange("p t i -> p (t i)").bitcast(I32))
            return window

        def load_wv(queue, a):
            rows = wv[a * PASS : (a + 1) * PASS, :].rearrange("(p t) n -> p t n", t=PACK)
            queue.dma_start(out=wv_raw[a][:], in_=rows)

        def load_prior(j0, width, b, kib, t0=0, planes=PACK):
            rows = sbuf([P, planes, width], F32, f"prior{j0}_{b}_{t0}", kib)
            source = prior[b * PASS : (b + 1) * PASS, j0 : j0 + width].rearrange("(p t) j -> p t j", t=PACK)
            nc.sync.dma_start(out=rows[:], in_=source[:, t0 : t0 + planes, :])
            return rows

        def move_rows(queue, moved, source, step, row):
            for d in (0, 2, 1, 3):
                queue.dma_start(
                    out=moved[32 * d + row : 32 * d + row + 4, :, :].bitcast(I32),
                    in_=source[8 * step * d : 8 * step * (d + 1) : step, :].bitcast(I32),
                )

        v2_scale_window = sbuf([P, T], U8, "v2_scale_window", 15)
        v_scale_window = sbuf([P, T], U8, "v_scale_window", 35)
        moved_v2 = sbuf([P, PASSES, S], U8, "moved_v2")
        moved_v = sbuf([P, PASSES, S], U8, "moved_v")
        gain_rows = sbuf([P, PASS], F32, "gain_rows")
        identity = sbuf([P, P], F32, "identity")
        nc.gpsimd.memset(v_scale_window[:].bitcast(I32), 0)
        nc.gpsimd.memset(v2_scale_window[32:64, :].bitcast(I32), 0)
        nc.gpsimd.memset(v2_scale_window[64:, :].bitcast(I32), 0)
        warm = keep.tile([P, 2], F32)
        nc.gpsimd.memset(warm[:], 0.0)
        nc.gpsimd.memset(gain_rows[:], 0.0)
        make_identity(nc, identity[:])
        nc.gpsimd.memset(moved_v2[:].bitcast(I32), 0)
        nc.gpsimd.memset(moved_v[:].bitcast(I32), 0)

        wv_raw = [sbuf([P, PACK, N], F32, f"wv_raw{a}", kib) for a, kib in enumerate((40, 48))]
        list2 = keep.tile([P, S // LIST_ROWS], U16)
        nc.sync.dma_start(list2[:], offs2)
        nc.scalar.dma_start(
            out=v2_scale_window[:32, :].bitcast(I32), in_=tab2_scales.bitcast(I32).rearrange("a q t -> q a t")
        )
        load_wv(nc.scalar, 0)
        lists = keep.tile([P, S // LIST_ROWS], U16)
        nc.sync.dma_start(lists[:], offs)
        nc.sync.dma_start(
            out=v_scale_window[0:P:4, :].bitcast(I32), in_=tab_scales.bitcast(I32).rearrange("a q t -> q a t")
        )
        nc.scalar.activation(out=warm[:, 1:2], in_=warm[:, 0:1], func=ACT.Silu)
        v2_windows = [load_words(tab2_words, 0, "v2_window0", 0)]
        for i, gain in enumerate((gv, gm)):
            nc.sync.dma_start(out=gain_rows[PASSES * i : PASSES * (i + 1), :], in_=gain.rearrange("(b c) -> b c", b=PASSES))
        load_wv(nc.sync, 1)
        turned = bank(7, [P, PACK, P])
        for t in range(PACK):
            nc.tensor.transpose(turned[:, t, :], gain_rows[:, t:PASS:PACK], identity[:])
        gains = sbuf([P, PACK, 2 * PASSES], F32, "gains")
        nc.scalar.copy(out=gains[:], in_=turned[:, :, : 2 * PASSES])

        v2_scales_listed = sbuf([P, S], U8, "v2_scales_listed")
        nc.vector.tensor_copy(
            out=v2_scales_listed[:].rearrange("p (b t c) -> p b c t", b=PASSES, t=PACK),
            in_=v2_scale_window[:].indirect(list2[:]),
        )
        move_rows(nc.sync, moved_v2, v2_scales_listed, 1, STATIONARY_ROW)
        v2_windows.append(load_words(tab2_words, 1, "v2_window1", 8))
        v_windows = [load_words(tab_words, 0, "v_window0", 16)]
        v_scales_listed = sbuf([P, S], U8, "v_scales_listed")
        nc.vector.tensor_copy(out=v_scales_listed[:], in_=v_scale_window[:].indirect(lists[:]))
        move_rows(nc.sync, moved_v, v_scales_listed, 4, 0)
        v_windows.append(load_words(tab_words, 1, "v_window1", 28))

        cols = HALF // LIST_ROWS
        v2_codes = {}

        def gather_v2(a, b, kib=None):
            codes = sbuf([P, PACK, P], U32, f"v2_codes{a}_{b}", kib)
            nc.vector.tensor_copy(
                out=codes[:].rearrange("p t c -> p c t"),
                in_=v2_windows[a][:].bitcast(U32).indirect(list2[:, b * cols : (b + 1) * cols]),
            )
            v2_codes[a, b] = codes

        def pass_v2(acc, a, b, t, codes, scales, opening=0, closes=True):
            first = b * PASS + t * P
            nc.tensor.matmul_mx(
                out=acc,
                lhsT=v2_codes[a, b][:, t, :].bitcast(FP8X4),
                lhsT_scale=moved_v2[STATIONARY_ROW:, a, first : first + P],
                rhs=codes.bitcast(FP8X4),
                rhs_scale=scales,
                start=(a == opening),
                stop=(a != opening and closes),
            )

        w4_planes = sbuf([P, PASSES, N], U8, "w4_planes")
        val_acc = {(b, t): bank(PACK * b + t, [P, N]) for b in range(PASSES) for t in range(PACK)}
        for a in range(PASSES):
            woven = sbuf([P, N, PACK], BF16, f"wv_woven{a}")
            share = N if a == 0 else SCALAR_CAST
            nc.scalar.activation(
                out=woven_walk(woven[:, :share, :], PACK), in_=plane_walk(wv_raw[a][:, :, :share], PACK), func=ACT.Copy
            )
            if share < N:
                gpsimd_weave(woven[:, share:, :], wv_raw[a][:, :, share:])
            if a == 0:
                gather_v2(a, 0)
            codes, scales = quantize(woven[:].rearrange("p c t -> p (c t)"), N, f"wv{a}", None, w4_planes[:, a, :])
            if a == 1:
                gather_v2(a, 0, 48)
            gather_v2(a, 1, 46 if a == 0 else 50)
            for b in range(PASSES):
                for t in range(PACK):
                    pass_v2(val_acc[b, t][:], a, b, t, codes[:], scales)
        val_planes = []
        for b in range(PASSES):
            val_planes.append(sbuf([P, PACK, N], BF16, f"val_planes{b}"))
            for t in range(PACK):
                nc.scalar.activation(
                    out=val_planes[b][:, t, :], in_=val_acc[b, t][:], func=ACT.Copy, scale=gains[:, t, b : b + 1]
                )

        prior_pairs = [load_prior(0, HALF, 1, 2 * t0, t0, 2) for t0 in (0, 2)]
        prior_rows = {(0, 0): load_prior(0, HALF, 0, 8)}
        w4_codes = sbuf([P, PASSES, 2 * N], U8, "w4_codes", 52)
        nc.sync.dma_start(out=w4_codes[:].bitcast(I32), in_=w4_words.bitcast(I32).rearrange("a p c -> p a c"))
        w4_rows = w4_scales.bitcast(I32).rearrange("a q c -> q a c")
        for d in range(4):
            nc.sync.dma_start(out=w4_planes[32 * d : 32 * d + 4, :, :].bitcast(I32), in_=w4_rows[4 * d : 4 * d + 4])

        val_woven = [sbuf([P, N, PACK], BF16, f"val_woven{b}", None) for b in range(PASSES)]
        for b in range(PASSES):
            gpsimd_weave(val_woven[b][:], val_planes[b][:])

        v_codes = {}
        for a in range(PASSES):
            for h in range(S // HALF):
                codes = sbuf([P, HALF], U32, f"v_codes{a}_{h}")
                step = QUARTER if (a, h) == (1, 0) else HALF
                for first in range(0, HALF, step):
                    entry = (h * HALF + first) // LIST_ROWS
                    offsets = lists[:, entry : entry + step // LIST_ROWS]
                    nc.vector.tensor_copy(
                        out=codes[:, first : first + step], in_=v_windows[a][:].bitcast(U32).indirect(offsets)
                    )
                v_codes[a, h] = codes
        prior_rows[HALF, 0] = load_prior(HALF, HALF, 0, 16)
        prior_rows[HALF, 1] = load_prior(HALF, QUARTER, 1, 28)
        prior_rows[HALF + QUARTER, 1] = load_prior(HALF + QUARTER, QUARTER, 1, 32)
        val_mx = {}

        def quantize_val(b, kib):
            plane = sbuf([P, N], U8, f"val{b}_plane")
            woven = val_woven[b][:].rearrange("p c t -> p (c t)")
            val_mx[b] = quantize(woven, N, f"val{b}", kib, plane[STATIONARY_ROW:, :])

        def v_operand(a, j0, width):
            h, first = divmod(j0, HALF)
            return v_codes[a, h][:, first : first + width], moved_v[:, a, j0 : j0 + width]

        e_acc, e_scaled, e_mx, y_acc, shares = {}, {}, {}, {}, {}

        def open_score(unit, first_bank):
            width = unit[1]
            share = HALF // width
            tiles = [bank(first_bank + i, [P, share, width]) for i in range(PACK // share)]
            e_acc[unit] = [tiles[t // share][:, t % share, :] for t in range(PACK)]

        def score_pass(unit, a, t, opening):
            j0, width, b = unit
            pass_v2(e_acc[unit][t], a, b, t, *v_operand(a, j0, width), opening)

        def scale_out(unit):
            j0, width, b = unit
            e_scaled[unit] = sbuf([P, PACK, width], F32, f"e_scaled{j0}_{b}")
            for t in range(PACK):
                gain = gains[:, t, PASSES + b : PASSES + b + 1]
                nc.scalar.activation(out=e_scaled[unit][:, t, :], in_=e_acc[unit][t], func=ACT.Copy, scale=gain)

        def add_prior(unit, woven, skip=0):
            j0, width, b = unit[0] + skip, woven.shape[1], unit[2]
            nc.vector.tensor_tensor(
                out=woven_walk(woven, 2),
                in0=plane_walk(e_scaled[unit][:, :, skip : skip + width], 2),
                in1=plane_walk(prior_rows[j0, b][:], 2),
                op=ALU.add,
            )

        def own_codes(j0, width, index, tiles):
            share = len(tiles)
            shares[j0] = share
            y_acc.setdefault(j0, []).append(bank(index, [P, share, width]))
            for tile in tiles:
                n0 = tile * P
                for a in range(PASSES):
                    codes, scales = v_operand(a, j0, width)
                    nc.tensor.matmul_mx(
                        out=y_acc[j0][tile // share][:, tile % share, :],
                        lhsT=w4_codes[:, a, 2 * n0 : 2 * (n0 + P)].bitcast(FP4X4),
                        lhsT_scale=w4_planes[:, a, n0 : n0 + P],
                        rhs=codes.bitcast(FP8X4),
                        rhs_scale=scales,
                        start=(tile % share == 0 and a == 0),
                        stop=False,
                    )

        def read_map(j0, width, b, tile):
            share = shares[j0]
            n0 = tile * P
            codes, scales = e_mx[j0, b]
            nc.tensor.matmul_mx(
                out=y_acc[j0][tile // share][:, tile % share, :],
                lhsT=val_mx[b][0][:, n0 : n0 + P].bitcast(FP8X4),
                lhsT_scale=val_mx[b][1][:, n0 : n0 + P],
                rhs=codes.bitcast(FP8X4),
                rhs_scale=scales,
                start=False,
                stop=(b == PASSES - 1 and tile % share == share - 1),
            )

        out_rows = out.rearrange("(n p) j -> p n j", p=P)

        def finish(j0, width, first_tile, tiles, queue):
            share = shares[j0]
            sums = y_acc[j0][first_tile // share][:, first_tile % share : first_tile % share + tiles, :]
            result = keep.tile([P, tiles, width], F32, name=f"result{j0}_{first_tile}")
            nc.scalar.activation(out=result[:], in_=sums, func=ACT.Silu)
            queue.dma_start(out=out_rows[:, first_tile : first_tile + tiles, j0 : j0 + width], in_=result[:])

        left = [(0, HALF, b) for b in range(PASSES)]
        quarters = (HALF, HALF + QUARTER)
        for b in range(PASSES):
            open_score(left[b], PACK * b)
        for t in range(PACK):
            score_pass(left[0], 0, t, 0)
        for t in range(EARLY):
            score_pass(left[1], 0, t, 0)
        for first in (0, QUARTER):
            for t in range(PACK):
                columns = e_acc[left[0]][t][:, first : first + QUARTER]
                pass_v2(columns, 1, 0, t, *v_operand(1, first, QUARTER), 0, first > 0)
                if first > 0 and t % 2 == 1:
                    score_pass(left[1], 1, t // 2, 0)
        for t in range(EARLY, PACK):
            for a in (1, 0):
                score_pass(left[1], a, t, 1)
        scale_out(left[0])
        planes = sbuf([P, PACK, HALF], BF16, "e_planes")
        for t in range(PACK):
            nc.vector.scalar_tensor_tensor(
                out=planes[:, t, :],
                in0=e_acc[left[1]][t],
                scalar=gains[:, t, PASSES + 1 : PASSES + 2],
                in1=prior_pairs[t // 2][:, t % 2, :],
                op0=ALU.mult,
                op1=ALU.add,
            )
        left_woven = [sbuf([P, HALF, PACK], BF16, f"e_woven0_{b}", kib) for b, kib in enumerate((0, None))]
        right = [(HALF, HALF, b) for b in range(PASSES)]
        for b in range(PASSES):
            open_score(right[b], PACK * b)
            for t in range(PACK):
                for a in range(PASSES):
                    score_pass(right[b], a, t, 0)
            scale_out(right[b])
            if b == 0:
                nc.scalar.copy(out=woven_walk(left_woven[1][:], PACK), in_=plane_walk(planes[:], PACK))
        right_woven = [sbuf([P, HALF, PACK], BF16, f"e_woven1_{b}") for b in range(PASSES)]

        quarters = ((HALF, QUARTER), (HALF + QUARTER, QUARTER))

        def quantize_e(woven, b, pieces):
            width = woven.shape[1]
            codes, scales = quantize(woven.rearrange("p c t -> p (c t)"), width, f"e{pieces[0][0]}_{b}")
            for j0, piece in pieces:
                first = j0 - pieces[0][0]
                e_mx[j0, b] = codes[:, first : first + piece], scales[:, first : first + piece]

        def last_unit(piece):
            first = piece[0] - HALF
            return right_woven[1][:, first : first + piece[1], :]

        add_prior(left[0], left_woven[0][:])
        quantize_val(0, 4)
        quantize_val(1, 6)
        quantize_e(left_woven[0][:], 0, [(0, HALF)])
        quantize_e(left_woven[1][:], 1, [(0, HALF)])
        add_prior(right[0], right_woven[0][:])
        add_prior(right[1], last_unit(quarters[0]), 0)
        quantize_e(right_woven[0][:, :QUARTER, :], 0, [quarters[0]])
        quantize_e(last_unit(quarters[0]), 1, [quarters[0]])
        add_prior(right[1], last_unit(quarters[1]), QUARTER)
        quantize_e(right_woven[0][:, QUARTER:, :], 0, [quarters[1]])
        quantize_e(last_unit(quarters[1]), 1, [quarters[1]])

        for tile in range(TILES):
            own_codes(0, HALF, tile, (tile,))
        for b in range(PASSES):
            for tile in range(TILES):
                read_map(0, HALF, b, tile)
        for tile in range(TILES):
            finish(0, HALF, tile, 1, nc.sync)
        third, fourth = quarters
        pairs = ((0, 1), (2, 3))
        for i, pair in enumerate(pairs):
            own_codes(*third, 4 + i, pair)
        last_banks = (6, 7, 1, 5)
        for tile in pairs[0]:
            own_codes(*fourth, last_banks[tile], (tile,))
        for pair in pairs:
            for b in range(PASSES):
                for tile in pair:
                    read_map(*third, b, tile)
            finish(*third, pair[0], 2, nc.sync)
        own_codes(*fourth, last_banks[2], (2,))
        for tile in range(TILES):
            if tile == TILES - 1:
                own_codes(*fourth, last_banks[tile], (tile,))
            for b in range(PASSES):
                read_map(*fourth, b, tile)
            finish(*fourth, tile, 1, nc.scalar if tile == TILES - 1 else nc.sync)
